import numpy as np, ml_dtypes
CORES = [6,15,38,47]
N = 4
BF = ml_dtypes.bfloat16
def gentries(a):
    return np.ascontiguousarray(a.reshape(8, 16, -1).transpose(0, 2, 1)).reshape(8, -1)
def gtable(e):
    e = np.asarray(e); return np.ascontiguousarray(e.reshape(8, -1, 16).transpose(0, 2, 1)).reshape(128, -1).astype(np.int32)
V, K, C, M, T, H, LX = 4096, 4096, 16, 2, 6, 2, 255
TH = np.array([65])
LA = K // C
def parts(rng):
    w = np.floor(256 * rng.random((N, 8, 16, V)) * rng.random((N, 8, 16, V)))
    l = 1 + np.floor(LX * rng.random((N, 8, V)) * rng.random((N, 8, V))).astype(np.int64)
    d = np.argsort(rng.random((N, 8, M, V)), axis=-1)
    o = np.floor(LX * rng.random((N, 8, M, V)) * rng.random((N, 8, M, V))).astype(np.int64)
    b = rng.integers(0, V, (N, 8, LA, C)); c = np.floor(LX * rng.random((N, 8, LA, C)) * rng.random((N, 8, LA, C))).astype(np.int64)
    return w, l, d, o, b, c
def pack(w, l, d, o, b, c):
    return {"wp": np.ascontiguousarray(w.reshape(N, 128, V)).astype(np.float32).astype(BF), "rl": np.ascontiguousarray(l).astype(np.int32),
            "dm": np.ascontiguousarray(d.reshape(N, 8, M * V)).astype(np.int32), "om": np.ascontiguousarray(o.reshape(N, 8, M * V)).astype(np.int32),
            "cb": np.stack([gtable(a.reshape(8, -1)) for a in b]), "co": np.stack([gtable(a.reshape(8, -1)) for a in c])}
def setup_inputs(rng):
    return pack(*parts(rng))
def setup_inputs_spread(rng):
    bits = LX.bit_length()
    w = np.floor(np.exp2(8 * rng.random((N, 8, 1, V))) * rng.random((N, 8, 16, V)) * (rng.random((N, 8, 1, V)) > 0.0625))
    l = np.floor(np.exp2(bits * rng.random((N, 8, V)))).astype(np.int64)
    d = np.floor(V * rng.random((N, 8, M, V)) ** 3).astype(np.int64)
    o = np.floor(np.exp2(bits * rng.random((N, 8, M, V)))).astype(np.int64) - 1
    b = V - 1 - np.floor(V * rng.random((N, 8, LA, C)) ** 3).astype(np.int64)
    c = np.floor(np.exp2(bits * rng.random((N, 8, LA, C)))).astype(np.int64) - 1
    return pack(w, np.clip(l, 1, LX), np.clip(d, 0, V - 1), np.clip(o, 0, LX - 1), np.clip(b, 0, V - 1), np.clip(c, 0, LX - 1))
def setup_inputs_ends(rng):
    def ends(lo, hi, *shape): return np.where(rng.random(shape) < 0.5, lo, hi)
    s0 = V // 4; n0 = V * 3 // 8; mid = slice(s0, s0 + n0)
    share = np.broadcast_to(np.where(rng.random((N, 1, 1, V)) < 0.5, 0.9, 0.1), (N, 8, 16, V)).copy(); share[:, :, [3, 8, 15]] = 0.005
    w = np.where(rng.random((N, 8, 16, V)) < share, 255, 0); w[..., 0] = 0; w[..., V - 1] = 0
    full = [V - 1 if q % 2 == 1 or q == N - 1 else 0 for q in range(N)]
    for q in range(N): w[q, :, :, full[q]] = 255
    l = ends(1, LX, N, 8, V); l[..., mid] = ends(1, LX, N, 1, n0)
    d = ends(0, V - 1, N, 8, M, V); d[..., mid] = s0 + rng.integers(0, n0 - H, (N, 1, M, n0))
    o = ends(0, LX - 1, N, 8, M, V); o[..., mid] = ends(0, LX - 1, N, 1, M, n0)
    b = ends(0, V - 1, N, 8, LA, C); c = ends(0, LX - 1, N, 8, LA, C)
    quiet = rng.permutation(np.arange(3, LA - 2))[:LA * 3 // 8]; nq = len(quiet)
    b[:, :, quiet] = s0 + rng.integers(0, n0 - H, (N, 1, nq, C)); c[:, :, quiet] = ends(0, LX - 1, N, 1, nq, C)
    for i in (0, 1, 2, LA - 2, LA - 1):
        for q in range(N): b[q, :, i] = np.where((np.arange(C) + i + (LA - 1) + (C - 1)) % 2 == 0, full[q], V - 1 - full[q])
    return pack(w, l, d, o, b, c)
def setup_inputs_brink(rng):
    w, l, d, o, b, c = parts(rng); n8 = V // 8
    levels = np.array(sorted(set([0, 1, 127, 128] + [int(v) for h in TH for v in (h - 1, h, 128 - h, 129 - h)])))
    lev = np.repeat(rng.choice(levels, (N, n8)), 8, axis=1)[:, None, None, :]
    late = np.zeros((N, 8, 16)); late[0::4, :, 8:] = 1; late[1::4, :, :8] = 1; late[2::4, 4:] = 1
    pos = np.argsort(np.argsort((rng.random((N, 8, 16)) + late).reshape(N, 128), axis=1), axis=1).reshape(N, 8, 16, 1)
    lo = rng.integers(0, 255, (N, 8, 16, 1)); hi = lo + 1 + np.floor((255 - lo) * rng.random((N, 8, 16, 1))).astype(np.int64)
    rich = np.repeat(rng.random((N, n8)) < 0.3, 8, axis=1)[:, None, None, :]
    w = np.where(rich, w, np.where(pos < lev, hi, lo))
    d = 8 * np.repeat(np.argsort(rng.random((N, 1, M, n8)), axis=-1), 8, axis=-1) + rng.integers(0, 8 - H, (N, 8, M, V))
    b = 8 * rng.integers(0, n8, (N, 1, LA, C)) + rng.integers(0, 8 - H, (N, 8, LA, C))
    for g in range(8):
        s = g // 2
        if g % 2 == 0: lv, ov, cv = [max(s, 1), s + 1, s + 2], [0, 0, 1, s], [s, s, s + 1]
        else: lv, ov, cv = [LX - 1, LX], [0, 1, 2, LX - 1], [LX - 3, LX - 2, LX - 1]
        l[:, g] = rng.choice(np.array(lv), (N, V)); o[:, g] = rng.choice(np.array(ov), (N, M, V)); c[:, g] = rng.choice(np.array(cv), (N, LA, C))
    return pack(w, l, d, o, b, c)
def setup_inputs_corners(rng):
    w, l, d, o, b, c = parts(rng); v = np.arange(V)
    for q in range(N):
        for g in range(8):
            kd = (g + q) % 4; kl = (g // 2 + q) % 4; ko = (g + 2 * q) % 3; z = rng.random((M, V)) < 0.25
            if kd == 0: d[q, g, 0] = v; d[q, g, 1:] = v[::-1]
            elif kd == 1: d[q, g] = np.where(z, V - 1 - rng.integers(0, 3, (M, V)), d[q, g])
            elif kd == 2: d[q, g] = np.where(z, (V - 1) * rng.integers(0, 2, (M, V)), d[q, g])
            else: d[q, g] = (v[None, :] + 1 + np.arange(M)[:, None]) % V
            if kl == 0: l[q, g] = 1
            elif kl == 1: l[q, g] = LX
            elif kl == 2: l[q, g] = rng.choice(np.array([1, 2, LX - 1, LX]), V)
            else: l[q, g, V - 3:] = 1; l[q, g, :2] = (1, LX)
            if ko == 0: o[q, g] = 0
            elif ko == 1: o[q, g] = LX - 1
            else: o[q, g] = rng.choice(np.array([0, 1, LX - 2, LX - 1]), (M, V))
    c = np.where(rng.random(c.shape) < 0.5, rng.choice(np.array([0, 1, LX - 2, LX - 1]), c.shape), c)
    b = np.where(rng.random(b.shape) < 0.25, rng.choice(np.array([0, V - 2, V - 1]), b.shape), b)
    b[:, :, 0, 0] = 0; b[:, :, LA - 1, C - 1] = V - 1
    s = 256 // C; p = np.arange(128).reshape(8, 16, 1)
    w[2] = s * (C - 1 - (v - p) % C) + rng.integers(0, s, (8, 16, V))
    for g in range(8):
        bl = np.concatenate([[0], 1 + rng.permutation(LA - 2), [LA - 1]]) % (V // C)
        b[2, g] = C * bl[:, None] + np.arange(C)
    for g in (1, 4, 7):
        w[:, g, rng.integers(0, 16)] = np.where(rng.random((N, V)) * 2 * C < 1, rng.integers(1, 4, (N, V)), 0)
    w[1] = rng.integers(0, 4, (8, 16, 1))
    return pack(w, l, d, o, b, c)
def setup_inputs_crowd(rng):
    w, l, d, o, b, c = parts(rng)
    x = np.argsort(rng.random((N, 8, V)), axis=-1)[..., :3]; wide_x = np.ascontiguousarray(np.broadcast_to(x[:, :, None, :], (N, 8, M, 3)))
    prof = np.zeros((N, 8, 16, 3)); prof[..., 0] = 255; prof[..., 2] = 255
    for q in range(N): prof[q, rng.integers(0, 8), rng.integers(0, 16), 2] = 0
    np.put_along_axis(w, np.ascontiguousarray(np.broadcast_to(x[:, :, None, :], (N, 8, 16, 3))), prof, 3)
    np.put_along_axis(l, x, LX, 2); np.put_along_axis(o, wide_x, rng.integers(0, 4, (N, 8, M, 3)), 3)
    to = np.argsort(rng.random((N, 1, M, 3)), axis=-1); nx = np.broadcast_to(np.roll(x, -1, axis=0)[:, :, None, :], (N, 8, M, 3))
    np.put_along_axis(d, wide_x, np.take_along_axis(nx, np.ascontiguousarray(np.broadcast_to(to, (N, 8, M, 3))), 3), 3)
    one = rng.integers(0, 3, (N, 1, LA, C)); k = np.arange(C)
    one[:, :, LA - 1] = np.where(k % 2 == 1, 0, 1); one[:, :, LA - 2] = np.where(k % 2 == 1, 2, 1)
    one = np.broadcast_to(one, (N, 8, LA, C)).copy(); m = np.zeros((N, 8, LA, C), bool); m[:, :, LA * 3 // 10:] = True
    for q in range(1, N, 2):
        m[q, :3] = True; m[q, 3] = False; one[q, :2] = 0
        one[q, 1, rng.integers(0, LA - 1), rng.integers(0, C)] = 1; one[q, 2] = rng.integers(0, 3, (LA, C))
        m[q, 3, LA - 1] = True; one[q, 2:4, LA - 1] = 0; one[q, 4:, LA - 1] = np.where(k % 2 == 1, 1, 0)
    b = np.where(m, np.take_along_axis(x, one.reshape(N, 8, -1), 2).reshape(N, 8, LA, C), b); c = np.where(m, rng.integers(0, 4, c.shape), c)
    return pack(w, l, d, o, b, c)
def check_inputs(d):
    bad = []
    for k, lo, hi in (("wp", 0, 255), ("rl", 1, LX), ("dm", 0, V - 1), ("om", 0, LX - 1), ("cb", 0, V - 1), ("co", 0, LX - 1)):
        a = np.asarray(d[k]).astype(np.float64)
        if not (np.min(a) >= lo and np.max(a) <= hi): bad.append("range of " + k)
        elif np.any(a != np.floor(a)): bad.append("whole numbers in " + k)
    return bad
def reference(wp, rl, dm, om, cb, co):
    w = wp.astype(np.float32).reshape(N, 8, 16, V); ln = rl.astype(np.int64); dd = dm.astype(np.int64); oo = om.astype(np.int64)
    b = np.stack([gentries(a) for a in cb]).astype(np.int64); o = np.stack([gentries(a) for a in co]).astype(np.int64)
    e = np.zeros((N, 8, 16, LA), np.float32)
    for t in range(T):
        q = (np.arange(N) + t) % N; nx = (q + 1) % N
        x = np.take_along_axis(w[q], b[:, :, None, :], 3).reshape(N, 8, 16, LA, C)
        e = np.maximum(e, np.max(x, axis=4))
        a = np.add.reduce((x > np.roll(x, -1, axis=4)).astype(np.int64).reshape(N, 128, LA, C), axis=1)
        m = np.add.reduce((a[..., None] >= TH).astype(np.int64), axis=3).reshape(N, 1, K)
        ix = m * V + b
        b = np.take_along_axis(dd[q], ix, 2); o = o + np.take_along_axis(oo[q], ix, 2)
        for h in range(H):
            lb = np.take_along_axis(ln[nx], b, 2); hop = o >= lb
            o = np.where(hop, o - lb, o); b = np.where(hop, (b + 1) % V, b)
        o = np.minimum(o, np.take_along_axis(ln[nx], b, 2) - 1)
    return {"yb": np.stack([gtable(a) for a in b]).astype(np.float32), "yo": np.stack([gtable(a) for a in o]).astype(np.float32), "ye": e.reshape(N, 128, LA).astype(BF)}

@@ -1,0 +1,459 @@
+from concourse.bass import DstId, RemoteDMATransfer
+from concourse.mybir import AluOpType, ActivationFunctionType
+
+V, STEPS, NCH = 4096, 6, 4
+MS = 4128
+NM = (STEPS - 1) * NCH
+BF, F32, I32, U16, F16 = "bfloat16", "float32", "int32", "uint16", "float16"
+
+SCRATCH = {
+    "WP": ("sbuf", [128, V + 16], BF), "RLW": ("sbuf", [128, MS], BF), "TAB": ("sbuf", [128, 2 * MS], BF),
+    "RLI": ("sbuf", [128, 256], I32), "RLB": ("sbuf", [128, 256], BF), "RLL": ("sbuf", [128, 256], BF),
+    "CBI": ("sbuf", [128, 256], I32), "COI": ("sbuf", [128, 256], I32), "CB16": ("sbuf", [128, 256], U16),
+    "COX": ("sbuf", [128, 520], BF),
+    "DMI": ("sbuf", [128, 2, 16, 16], I32), "DMR": ("sbuf", [128, 16, 32], F32),
+    "DMU": ("sbuf", [128, 16, 32], F32), "DMZ": ("sbuf", [128, 512], U16),
+    "OMI": ("sbuf", [128, 512], I32), "OMB": ("sbuf", [128, 512], BF),
+    "PI": ("sbuf", [128, 128], F32), "PC": ("sbuf", [128, 4], I32), "PD": ("sbuf", [128, 4], I32),
+    "PF": ("sbuf", [128, 4], F32), "LO": ("sbuf", [128, 256], BF), "HI": ("sbuf", [128, 256], BF),
+    "ID": ("sbuf", [128, 128], BF), "IB": ("sbuf", [128, 16, 8], BF), "IF": ("sbuf", [128, 128], F32),
+    "IH": ("sbuf", [128, 128], F16), "IK": ("sbuf", [128, 128], BF),
+    "ONE": ("sbuf", [128, 128], BF), "C16": ("sbuf", [128, 64], BF), "MASK": ("sbuf", [128, MS // 4], BF),
+    "FS": ("sbuf", [128, 72], BF),
+    "X": ("sbuf", [128, 129, 8], BF), "TH": ("sbuf", [128, 17, 8], F16),
+    "BO": ("sbuf", [128, NCH, 128], F32),
+    "W": ("sbuf", [128, V], BF), "IND": ("sbuf", [128, V], BF), "SC": ("sbuf", [128, V], BF),
+    "GT": ("sbuf", [128, V], BF), "IDX": ("sbuf", [128, 256], U16),
+    "MSG": ("sbuf", [128, (NM + 1) * 128], U16), "OUT": ("sbuf", [128, (NM + 1) * 128], U16),
+    "PK": ("sbuf", [128, STEPS * 256], BF), "EIN": ("sbuf", [128, 4 * 256], BF),
+    "ZW": ("sbuf", [128, 64], F32), "YO": ("sbuf", [128, NCH * 128], F32), "YI": ("sbuf", [128, NCH * 128], F32),
+    "R0": ("psum", [128, 512], F32), "R1": ("psum", [128, 512], F32), "R2": ("psum", [128, 512], F32),
+    "VB": ("psum", [128, 512], F32), "JB": ("psum", [128, 512], F32), "F0": ("psum", [128, 512], F32),
+    "F1": ("psum", [128, 512], F32), "BB": ("psum", [128, 512], F32),
+}
+SEMAPHORES = (["cA", "cV", "cP", "cG", "sent", "outs", "a_rl"] + ["d%d" % i for i in range(28)]
+              + ["m%d" % n for n in range(NM + 1)] + ["y%d" % c for c in range(NCH)] + ["e%d" % i for i in range(4)])
+
+COST = dict(r=1.56, ov=30.0, pe=0.5, hop=120.0, lat=4200.0, call=700.0, dma0=2300.0, dmab=0.0045, look=70.0,
+            xv=14, xl={0: 32, 22: 24, 23: 32}, ta=(128, 128), pre=3, mid=4, lead=1.5, first=3.2, wv=(), loads="wdco", sw=1024,
+            bias={"PIK": -700.0, "Vmb": 2200.0, "VSC": 900.0, "Ppp": 2100.0, "VIDX": -200.0, "VTAB": 1500.0,
+                  "VPK": -800.0, "Voc": 900.0, "VIND": -800.0, "Vh1": 900.0, "PGT": 900.0, "VO": -600.0})
+
+
+def build(g, T, to_next, to_prev, cost):
+    ops = []
+    A, M = AluOpType, ActivationFunctionType
+    v, s, pe = g.vector, g.scalar, g.tensor
+    nd = [0]
+
+    def op(eng, fn, rd, wr, dur, banks=(), kind="c", sem=None, after=None, lat=0.0):
+        ops.append(dict(eng=eng, fn=fn, rd=rd, wr=wr, dur=dur, banks=banks, kind=kind, sem=sem, after=after,
+                        lat=lat, i=len(ops)))
+        return len(ops) - 1
+
+    def vec(fn, rd, wr, n, banks=()):
+        return op("V", lambda: [fn()], rd, wr, max(64.0, n) + cost["ov"], banks)
+
+    def act(fn, rd, wr, n):
+        return op("A", lambda: [fn()], rd, wr, max(64.0, n) + cost["ov"])
+
+    def gather(eng, out, win, rd, wr, n, slot=None):
+        if eng == "A":
+            i = op("A", lambda: [s.activation(out, win, M.Copy)], rd, wr, 78 + cost["r"] * n)
+            ops[i]["slot"] = slot
+            return i
+        return op("V", lambda: [v.tensor_copy(out, win)], rd, wr, 60 + cost["r"] * n)
+
+    def mm(lst, rd, banks):
+        n = sum(x[5] for x in lst)
+        return op("P", lambda: [pe.matmul(x[0], x[1], x[2], x[3], x[4]) for x in lst], rd, [], n * cost["pe"] + 30, banks)
+
+    def dma(out, in_, rd, wr, nbytes, q="S", sem=None, order=False):
+        if sem is None:
+            sem = "d%d" % nd[0]
+            nd[0] += 1
+        qu = g.sync if q == "S" else g.scalar
+        i = op(q, lambda: [qu.dma_start(out, in_)], rd, wr, 100.0, kind="dma", sem=sem, lat=nbytes * cost["dmab"])
+        if order:
+            ops[i]["slot"] = i
+        return i
+
+    calls = {}
+
+    def send(dst, srcs, peer, sem, rd, wr, more=0.0, after=None):
+        rid, pid, mask = peer
+
+        def fn():
+            if len(srcs) == 1:
+                g.remote_dma(dst, srcs[0], T.sem[sem], T.sem.sent, pid, rid, mask)
+            else:
+                g.remote_dma_fused([RemoteDMATransfer(dst_ids=[DstId(rid=rid, pnc=pid)], dma_engine_mask=mask,
+                                                      remote_sem=T.sem[sem], srcs=srcs, dsts=[dst], alu_op=2)],
+                                   local_sem=T.sem.sent)
+            return []
+        i = op("G", fn, rd, [], cost["call"], kind="send", after=after)
+        calls[sem] = i
+        op(None, None, [], wr, 0.0, kind="arr", sem=sem, after=i, lat=cost["lat"] + more)
+
+    X = T.X
+
+    def xv(f, n=1):
+        return X[:, f * 16 + 1:(f + n) * 16:2, :]
+
+    def xt(buf, f, kh):
+        return buf[:, f * 16 + 1 - kh:f * 16 + 17 - kh, :]
+
+    dma(T.RLI[:], T.rl[:], [], ["RLI"], 131072, order=True)
+    dma(T.CBI[:], T.cb[:], [], ["CBI"], 131072, q="A")
+    for what in cost["loads"]:
+        if what == "w":
+            dma(T.WP[:, 0:V], T.wp[:], [], ["WP"], 1048576, order=True)
+        elif what == "d":
+            for g0 in range(2):
+                for m in range(2):
+                    dma(T.DMI[:, g0, m * 8:(m + 1) * 8, :], T.dm[g0::2, m * V:(m + 1) * V], [], [("DMI", g0, m)], 65536, order=True)
+        elif what == "o":
+            for m in range(2):
+                dma(T.OMI[:, m * 256:(m + 1) * 256], T.om[:, m * V:(m + 1) * V], [], [("OMI", m)], 131072, order=True)
+        else:
+            dma(T.COI[:], T.co[:], [], ["COI"], 131072, order=True)
+    dma(T.WP[:, V:V + 16], T.wp[:, 0:16], [], ["WPw"], 65536, q="A")
+
+    vec(lambda: v.tensor_copy(T.RLB[:], T.RLI[:]), ["RLI"], ["RLB"], 256)
+    send(T.RLL[:], [T.RLB[:]], to_prev, "a_rl", ["RLB"], ["RLL"], more=3000.0)
+
+    op("G", lambda: [g.iota(T.PI[:], [[-1, 128]], 0, 1, allow_small_or_imprecise_dtypes=True)], [], ["PI"], 420.0)
+    op("G", lambda: [g.iota(T.PC[:, 0:1], [[0, 1]], 0, 1)], [], ["PC"], 160.0)
+    op("G", lambda: [g.iota(T.LO[:], [[1, 256]], 0, 0, allow_small_or_imprecise_dtypes=True)], [], ["LO"], 670.0)
+    vec(lambda: v.memset(T.MASK[:], 1.0), [], ["MASK"], MS // 8)
+    for k in range(4):
+        q = MS // 4
+        act(lambda k=k, q=q: s.activation(T.RLW[:, k * q:(k + 1) * q], T.MASK[:], M.Copy), ["MASK"], [("RLW0", k)], q)
+    vec(lambda: v.memset(T.MASK[:, 0:1024:16], 0.0), [], ["MASK"], 64)
+    vec(lambda: v.memset(T.ONE[:], 1.0), [], ["ONE"], 64)
+    vec(lambda: v.memset(T.C16[:], 16.0), [], ["C16"], 64)
+    vec(lambda: v.memset(X[:], 0.0), [], ["X0"], 516)
+    vec(lambda: v.memset(xv(0), 1.0), ["X0"], ["Xone"], 64)
+    vec(lambda: v.tensor_copy(T.TH[:], X[:, 16:33, :]), ["X0"], ["TH0"], 68)
+    vec(lambda: v.memset(T.COX[:], 0.0), [], ["COX"], 260)
+    vec(lambda: v.tensor_scalar(T.ID[:], T.PI[:], 0.0, None, A.is_equal), ["PI"], ["ID"], 128)
+    vec(lambda: v.tensor_copy(T.IB[:], T.ID[:]), ["ID"], ["IB"], 64)
+    vec(lambda: v.tensor_copy(T.IH[:], T.ID[:]), ["ID"], ["IH"], 64)
+    act(lambda: s.activation(T.IF[:], T.ID[:], M.Copy), ["ID"], ["IF"], 128)
+    act(lambda: s.activation(T.IK[:], T.ID[:], M.Copy, scale=float(MS)), ["ID"], ["IK"], 128)
+
+    def row(f):
+        return T.ID[:, f::16]
+
+    def fs(f):
+        return T.FS[:, f * 8:(f + 1) * 8]
+    vec(lambda: v.tensor_copy(fs(0), row(5)), ["ID"], [("FS", 0)], 8)
+    vec(lambda: v.tensor_scalar(fs(1), row(0), -1.0, None, A.mult), ["ID"], [("FS", 1)], 8)
+    vec(lambda: v.tensor_scalar(fs(2), row(1), -1.0, None, A.mult), ["ID"], [("FS", 2)], 8)
+    vec(lambda: v.tensor_tensor(fs(3), row(0), row(5), A.subtract), ["ID"], [("FS", 3)], 8)
+    vec(lambda: v.tensor_tensor(fs(7), row(2), row(6), A.subtract), ["ID"], [("FS", 7)], 8)
+    vec(lambda: v.tensor_scalar(fs(8), row(3), 256.0, None, A.mult), ["ID"], [("FS", 8)], 8)
+    vec(lambda: v.tensor_tensor(fs(4), fs(3), row(1), A.add), ["ID", ("FS", 3)], [("FS", 4)], 8)
+    vec(lambda: v.tensor_tensor(fs(6), fs(8), row(4), A.add), ["ID", ("FS", 8)], [("FS", 6)], 8)
+    vec(lambda: v.tensor_tensor(fs(5), fs(4), fs(7), A.add), [("FS", 4), ("FS", 7)], [("FS", 5)], 8)
+    FSK = [("FS", f) for f in range(7)]
+    vec(lambda: v.tensor_scalar(T.PD[:, 0:1], T.PC[:, 0:1], 15, None, A.bitwise_and), ["PC"], ["PD"], 1)
+    vec(lambda: v.tensor_scalar(T.PF[:, 0:1], T.PD[:, 0:1], -8.0, None, A.add), ["PD"], ["PF"], 1)
+    vec(lambda: v.tensor_scalar(T.HI[:], T.LO[:], 0.0, T.PF[:, 0:1], A.mult, A.add), ["PF", "LO"], ["HI"], 128)
+
+    R0K = [("RLW0", k) for k in range(4)]
+    dma(T.RLW[3::16, 16:16 + V], T.HI[:], R0K + ["HI"], [("RLW", 3)], 65536)
+    dma(T.RLW[4::16, 16:16 + V], T.LO[:], R0K + ["LO"], [("RLW", 4)], 65536)
+    for f in range(3):
+        dma(T.RLW[f::16, 16 - f:16 - f + V], T.RLL[:], R0K + ["RLL"], [("RLW", f)], 65536)
+    for f in (1, 2):
+        dma(T.RLW[f::16, 16 - f + V:18 - f + V], T.RLL[0::16, 0:2], R0K + ["RLL"], [("RLW", 10 + f)], 100)
+    RLK = R0K + [("RLW", f) for f in (0, 1, 2, 3, 4, 11, 12)]
+
+    for g0 in range(2):
+        vec(lambda g0=g0: v.tensor_copy(T.DMR[:, :, g0 * 16:(g0 + 1) * 16], T.DMI[:, g0, :, :]),
+            [("DMI", g0, 0), ("DMI", g0, 1)], [("DMR", g0)], 256)
+    vec(lambda: v.transpose(T.DMU[:], T.DMR[:]), [("DMR", 0), ("DMR", 1)], ["DMU"], 512)
+    for b in range(8):
+        vec(lambda b=b: v.tensor_copy(T.DMZ[:, b::8], T.DMU[:, b::8, :]), ["DMU"], [("DMZ", b)], 64)
+    ZK = [("DMZ", b) for b in range(8)]
+    vec(lambda: v.tensor_copy(T.OMB[:], T.OMI[:]), [("OMI", 0), ("OMI", 1)], ["OMB"], 512)
+
+    vec(lambda: v.tensor_copy(T.CB16[:], T.CBI[:]), ["CBI"], ["CB16"], 256)
+    vec(lambda: v.tensor_copy(T.BO[:, :, 0:64], T.CBI[:]), ["CBI"], [("B", c) for c in range(NCH)], 256)
+    vec(lambda: v.tensor_copy(T.COX[:, 1:513:2], T.COI[:]), ["COI"], ["COX"], 256)
+    mm([(T.F1[:, (c + 1) % NCH * 64:(c + 1) % NCH * 64 + 64], T.COX[:, 128 * c + 1 - kh:128 * c + 129 - kh], T.IB[:, kh::2, :],
+         kh == 0, kh == 1, 64) for c in range(NCH) for kh in range(2)], ["COX", "IB"], ["F1"])
+    vec(lambda: v.tensor_copy(T.BO[:, :, 64:128], T.F1[:, 0:256]), [], [("O", c) for c in range(NCH)], 256, ["F1"])
+
+    TK = []
+    for m in range(2):
+        pk = []
+        na = cost["ta"][m]
+        for eng, a, b in (("A", 0, na), ("V", na, (na + 256) // 4 * 2), ("V", (na + 256) // 4 * 2, 256)):
+            gather(eng, T.TAB[:, m * MS + a * 16:m * MS + b * 16],
+                   T.RLW[:, 16:16 + V].indirect(T.DMZ[:, m * 256 + a:m * 256 + b]),
+                   RLK + ZK, [("TAB", m, a * 16)], (b - a) * 16, slot=-50 + m)
+            pk.append(("TAB", m, a * 16))
+        gather("A", T.TAB[:, m * MS + V:(m + 1) * MS], T.RLW[:, 16:16 + V].indirect(T.DMZ[:, m * 256:m * 256 + 2]),
+               RLK + ZK, [("TAB", m, V)], 32, slot=-51 + m * 0.1)
+        dma(T.TAB[5::16, m * MS:m * MS + V], T.OMB[:, m * 256:(m + 1) * 256], ["OMB"], pk, 65536)
+        dma(T.TAB[5::16, m * MS + V:m * MS + V + 2], T.OMB[0::16, m * 256:m * 256 + 2], ["OMB"], [("TAB", m, V)], 100)
+        TK += pk + [("TAB", m, V)]
+
+    nr = [0]
+    for t in range(STEPS):
+        last = t == STEPS - 1
+        for c in range(NCH):
+            w0 = c * 1024
+            n = t * NCH + c
+            if t == 0:
+                lst, l0, lk = T.CB16, c * 64, "CB16"
+            else:
+                lst, l0, lk = T.MSG, (n - NCH) * 128, ("MSG", n - NCH)
+            for h in range(2):
+                a = w0 + h * 512
+                gather("V" if (n, h) in cost["wv"] else "A", T.W[:, a:a + 512],
+                       T.WP[:, 0:V + 16].indirect(lst[:, l0 + h * 32:l0 + h * 32 + 32]),
+                       ["WP", "WPw", lk], [("W", c, h)], 512,
+                       slot=(n - 100 if n < cost["pre"] else n - 40 if n < cost["mid"] else
+                             max(n - cost["lead"], cost["first"] + 0.01 * n)) + 0.001 * h)
+                rb = "R%d" % (nr[0] % 3)
+                nr[0] += 1
+                mm([(T[rb][:, 0:511], T.ID[:], T.W[:, a + 1:a + 512], True, True, 511),
+                    (T[rb][:, 15:512:16], T.ID[:], T.W[:, a:a + 512:16], True, True, 64)], ["ID", ("W", c, h)], [rb])
+                vec(lambda a=a, rb=rb: v.tensor_tensor(T.IND[:, a:a + 512], T.W[:, a:a + 512], T[rb][:], A.is_gt),
+                    [("W", c, h)], [("IND", c, h)], 512, [rb])
+            sw = cost["sw"]
+            for a in range(w0, w0 + 1024, sw):
+                vec(lambda a=a, sw=sw: v.tensor_tensor_scan(T.SC[:, a:a + sw], T.MASK[:, 0:sw], T.W[:, a:a + sw],
+                                                            0.0, A.mult, A.max),
+                    ["MASK"] + [("W", c, h) for h in range((a - w0) // 512, (a - w0 + sw) // 512)], [("SC", a)], sw // 2)
+            if c == NCH - 1:
+                vec(lambda t=t: v.tensor_copy(T.PK[:, t * 256:(t + 1) * 256], T.SC[:, 15::16]),
+                    [("SC", a) for a in range(0, V, sw)], [("PK", t, k) for k in range(NCH)], 128)
+            mm([(T.VB[:, kl:64:8], T.IND[:, w0 + kl:w0 + 1024:8], T.ONE[:, 0:8], True, True, 64) for kl in range(8)],
+               ["ONE", ("IND", c, 0), ("IND", c, 1)], ["VB"])
+            mm([(T.JB[:, 0:64], T.IF[:], T.BO[:, c, 0:64], True, False, 256)], ["IF", ("B", c)], ["JB"])
+            vec(lambda: v.tensor_scalar(xv(7), T.VB[:, 0:64], 65.0, None, A.is_ge), ["X0"], ["mb"], 64, ["VB"])
+            mm([(T.JB[:, 0:64], xt(X, 7, kh), T.IK[:, kh::2], False, kh == 1, 64) for kh in range(2)],
+               ["X0", "mb", "IK"], ["JB"])
+            vec(lambda c=c: v.tensor_copy(T.IDX[:, c * 64:(c + 1) * 64], T.JB[:, 0:64]), [], [("IDX", c)], 64, ["JB"])
+            nv = cost["xl"].get(n, cost["xv"])
+            na = 64 - nv
+            gather("A", T.GT[:, w0:w0 + na * 16], T.TAB[:].indirect(T.IDX[:, c * 64:c * 64 + na]),
+                   TK + [("IDX", c)], [("GT", c, 0)], na * 16, slot=n)
+            if nv:
+                gather("V", T.GT[:, w0 + na * 16:w0 + 1024], T.TAB[:].indirect(T.IDX[:, c * 64 + na:c * 64 + 64]),
+                       TK + [("IDX", c)], [("GT", c, 1)], nv * 16)
+            fb = "F%d" % (c % 2)
+            F = T[fb]
+            mm([(F[:, kl:448:8], T.GT[:, w0 + kl:w0 + 1024:8], T.FS[:, 0:56], True, True, 64) for kl in range(8)],
+               FSK + [("GT", c, 0), ("GT", c, 1)], [fb])
+            if n >= NCH - 1:
+                k = n - NCH + 1
+                lo, hi = (64 if k == NM else 0), (64 if k == 0 else 128)
+                vec(lambda k=k, lo=lo, hi=hi: v.tensor_copy(T.BO[:, k % NCH, lo:hi], T.MSG[:, k * 128 + lo:k * 128 + hi]),
+                    [("MSG", k)], [("B", k % NCH)] * (lo == 0) + [("O", c)] * (hi == 128), hi - lo)
+            o32 = T.BO[:, (c + 1) % NCH, 64:128]
+            vec(lambda F=F, o32=o32: v.tensor_tensor(xv(1), o32, F[:, 192:256], A.is_ge), ["X0", "TH0", ("O", c)], ["h1"], 64, [fb])
+            vec(lambda F=F, o32=o32: v.tensor_tensor(xv(2), o32, F[:, 256:320], A.is_ge), ["X0", "TH0", ("O", c)], ["h2"], 64, [fb])
+            vec(lambda F=F, o32=o32: v.tensor_tensor(xv(6), o32, F[:, 320:384], A.min), ["X0", ("O", c)], ["oc"], 64, [fb])
+            vec(lambda F=F: v.tensor_tensor(T.TH[:, 1:16:2, :], xv(1), F[:, 384:448], A.add), ["TH0", "h1"], ["th"], 64, [fb])
+            vec(lambda F=F: v.tensor_tensor(xv(3, 3), xv(0, 3), F[:, 0:192], A.mult), ["X0", "Xone", "h1", "h2"], ["pp"], 192, [fb])
+            mm([(T.BB[:, 0:64], T.ONE[:], T.C16[:], True, False, 64)]
+               + [(T.BB[:, 0:64], xt(X, 2, kh), T.ID[:, kh::2], False, False, 64) for kh in range(2)]
+               + [(T.BB[:, 0:64], xt(T.TH, 0, kh), T.IH[:, kh::2], False, kh == 1, 64) for kh in range(2)],
+               ["ONE", "C16", "ID", "IH", "X0", "TH0", "h2", "th"], ["BB"])
+            if not last:
+                def message(k, lo, hi):
+                    a, b = k * 128 + lo, k * 128 + hi
+                    vec(lambda: v.tensor_copy(T.OUT[:, a:b], T.BB[:, lo:hi]), [], [("OUT", k)], hi - lo, ["BB"])
+                    send(T.MSG[:, a:b], [T.OUT[:, a:b]], to_next, "m%d" % k, [("OUT", k)], [("MSG", k)])
+                message(n, 0, 128 if n else 64)
+                mm([(T.BB[:, 64:128], T.ID[:], xv(f), f == 6, f == 5, 64) for f in (6, 3, 4, 5)],
+                   ["ID", "oc", "pp"], ["BB"])
+                if n == NM - 1:
+                    message(NM, 64, 128)
+            else:
+                mm([(T.BB[:, 64:128], xt(X, f, kh), T.ID[:, kh::2], (f, kh) == (6, 0), (f, kh) == (5, 1), 64)
+                    for f in (6, 3, 4, 5) for kh in range(2)], ["ID", "X0", "oc", "pp"], ["BB"])
+                y0 = c * 128
+                vec(lambda: v.tensor_scalar(T.ZW[:], T.BB[:, 0:64], float(V), -float(V), A.is_ge, A.mult), [], ["ZW"], 64, ["BB"])
+                vec(lambda y0=y0: v.tensor_copy(T.YO[:, y0 + 64:y0 + 128], T.BB[:, 64:128]), [], [("YO", c, 1)], 64, ["BB"])
+                vec(lambda y0=y0: v.tensor_tensor(T.YO[:, y0:y0 + 64], T.ZW[:], T.BB[:, 0:64], A.add), ["ZW"], [("YO", c, 0)], 64, ["BB"])
+                send(T.YI[:, y0:y0 + 128], [T.YO[:, y0:y0 + 128]], to_prev, "y%d" % c,
+                     [("YO", c, 0), ("YO", c, 1)], [("YI", c)], more=500.0)
+                dma(T.yb[:, c * 64:(c + 1) * 64], T.YI[:, y0:y0 + 64], [("YI", c)], [], 32768, sem="outs")
+                dma(T.yo[:, c * 64:(c + 1) * 64], T.YI[:, y0 + 64:y0 + 128], [("YI", c)], [], 32768,
+                    q="A" if c == NCH - 1 else "S", sem="outs")
+        if t >= 2:
+            e = t - 2
+            srcs = [T.PK[:, t * 256:(t + 1) * 256]]
+            rd = [("PK", t, c) for c in range(NCH)]
+            if t >= 3:
+                srcs.append(T.EIN[:, (e - 1) * 256:e * 256])
+                rd.append(("EIN", e - 1))
+            if t >= 4:
+                srcs.append(T.PK[:, (t - 4) * 256:(t - 3) * 256])
+                rd += [("PK", t - 4, c) for c in range(NCH)]
+            send(T.EIN[:, e * 256:(e + 1) * 256], srcs, to_prev if last else to_next, "e%d" % e, rd, [("EIN", e)], more=1500.0,
+                 after=None if last else calls["m%d" % (NM if t == STEPS - 2 else t * NCH + NCH - 1)])
+    dma(T.ye[:], T.EIN[:, 768:1024], [("EIN", 3)], [], 65536, sem="outs")
+    return ops
+
+
+def link(ops):
+    wr, rd, bank = {}, {}, {}
+    for o in ops:
+        d = {}
+        for k in o["rd"]:
+            if k in wr:
+                d[wr[k]] = True
+        for k in o["wr"]:
+            if k in wr:
+                d[wr[k]] = True
+            for j in rd.get(k, []):
+                d[j] = True
+        for b in o["banks"]:
+            eng, cur, prev = bank.get(b, (None, [], []))
+            if eng != o["eng"]:
+                eng, cur, prev = o["eng"], [], cur
+            for j in prev:
+                d[j] = True
+            if eng == "P" and cur:
+                d.setdefault(cur[-1], False)
+            bank[b] = (eng, cur + [o["i"]], prev)
+        if o["after"] is not None:
+            d[o["after"]] = False
+        for k in o["rd"]:
+            rd.setdefault(k, []).append(o["i"])
+        for k in o["wr"]:
+            wr[k] = o["i"]
+            rd[k] = []
+        d.pop(o["i"], None)
+        o["deps"] = [(j, w and not (o["eng"] == "P" and ops[j]["eng"] == "P")) for j, w in d.items()]
+    for e in "AS":
+        seq = sorted((o["slot"], o["i"]) for o in ops if o.get("slot") is not None and o["eng"] == e)
+        for (_, i), (_, j) in zip(seq, seq[1:]):
+            if i not in [x for x, w in ops[j]["deps"]]:
+                ops[j]["deps"].append((i, False))
+
+
+def plan(ops, cost, order=None):
+    n = len(ops)
+    succ = [[] for _ in range(n)]
+    for o in ops:
+        for j, w in o["deps"]:
+            succ[j].append(o["i"])
+    tail = [0.0] * n
+    left = [len(o["deps"]) for o in ops]
+    topo_order = [i for i in range(n) if left[i] == 0]
+    for i in topo_order:
+        for j in succ[i]:
+            left[j] -= 1
+            if left[j] == 0:
+                topo_order.append(j)
+    assert len(topo_order) == n
+    for o in [ops[i] for i in reversed(topo_order)]:
+        x = o["dur"] + o["lat"] + (cost["dma0"] if o["kind"] == "dma" else 0.0)
+        tail[o["i"]] = max([tail[j] + (x + cost["hop"] if (o["i"], True) in ops[j]["deps"] or not ops[j]["eng"] else o["dur"])
+                            for j in succ[o["i"]]] + [x])
+    for o in ops:
+        k = (o["wr"] or o["rd"])[-1] if o["eng"] in ("V", "P") else None
+        tail[o["i"]] += cost["bias"].get(o["eng"] + (k[0] if isinstance(k, tuple) else k), 0.0) if k else 0.0
+    left = [len(o["deps"]) for o in ops]
+    done = [0.0] * n
+    free = {}
+    dmaq = [0.0]
+    ready = [i for i in range(n) if left[i] == 0]
+    out = []
+
+    def est(i):
+        o = ops[i]
+        x = free.get(o["eng"], 0.0) if o["eng"] else 0.0
+        for j, w in o["deps"]:
+            if w or not o["eng"]:
+                x = max(x, done[j] + (cost["hop"] if w else 0.0))
+        return x
+    while len(out) < n:
+        if order is not None:
+            i = order[len(out)]
+        else:
+            es = [(est(i), i) for i in ready]
+            t0, i0 = min(es)
+            e0 = ops[i0]["eng"]
+            i = max([(tail[k], -k) for x, k in es if ops[k]["eng"] == e0 and x <= t0 + cost["look"]])[1] * -1
+            ready.remove(i)
+        o = ops[i]
+        st = est(i)
+        if o["eng"]:
+            free[o["eng"]] = st + o["dur"]
+        if o["kind"] == "dma":
+            dmaq[0] = max(dmaq[0], st + o["dur"]) + o["lat"]
+            done[i] = dmaq[0] + cost["dma0"]
+        else:
+            done[i] = st + o["dur"] + o["lat"]
+        o["st"] = st
+        out.append(i)
+        if order is None:
+            for j in succ[i]:
+                left[j] -= 1
+                if left[j] == 0:
+                    ready.append(j)
+    return out, max(done)
+
+
+def emit(g, T, ops, order, engines):
+    queue = {"A": g.scalar, "V": g.vector, "P": g.tensor, "G": g, "S": g.sync}
+    know = {e: {} for e in queue}
+    count = {}
+    for i in order:
+        o = ops[i]
+        if o["kind"] == "arr":
+            o["mark"], o["know"] = (o["sem"], engines), {o["sem"]: engines}
+            continue
+        e = o["eng"]
+        need = {}
+        for j, w in o["deps"]:
+            if w:
+                sem, n = ops[j]["mark"]
+                if need.get(sem, (0, 0))[0] < n:
+                    need[sem] = (n, j)
+        for sem, (n, j) in sorted(need.items(), key=lambda x: -ops[x[1][1]]["st"]):
+            if know[e].get(sem, 0) < n:
+                queue[e].wait_ge(T.sem[sem], n)
+                for k, x in ops[j]["know"].items():
+                    if know[e].get(k, 0) < x:
+                        know[e][k] = x
+        ins = o["fn"]()
+        if o["kind"] == "send":
+            count["sent"] = count.get("sent", 0) + engines
+            continue
+        sem, inc = (o["sem"], 16) if o["kind"] == "dma" else ("c" + e, 1)
+        for x in ins:
+            x.then_inc(T.sem[sem], inc)
+            count[sem] = count.get(sem, 0) + inc
+        o["mark"] = (sem, count[sem])
+        o["know"] = dict(know[e])
+        o["know"][sem] = count[sem]
+    for sem in ("cG", "cP", "cA", "cV", "sent", "outs"):
+        g.wait_ge(T.sem[sem], count[sem])
+
+
+def rank_program(g, core, T, topo):
+    rank = T.rank_of(core)
+    if rank is None:
+        return
+    n = len(T.cores)
+    peers = []
+    for other in (T.cores[(rank + 1) % n], T.cores[(rank - 1) % n]):
+        assert topo.may_write(core, other)
+        rid, pid, _ = topo.addr(other)
+        peers.append((rid, pid, topo.mask(core, other)))
+    engines = len(topo.engines(core, T.cores[(rank + 1) % n]))
+    assert engines == len(topo.engines(core, T.cores[(rank - 1) % n]))
+    ops = build(g, T, peers[0], peers[1], COST)
+    link(ops)
+    order, _ = plan(ops, COST)
+    emit(g, T, ops, order, engines)

@@ -7,37 +7,49 @@ NM = (STEPS - 1) * NCH
 BF, F32, I32, U16, F16 = "bfloat16", "float32", "int32", "uint16", "float16"
 
 SCRATCH = {
-    "WP": ("sbuf", [128, V + 16], BF), "RLW": ("sbuf", [128, MS], BF), "TAB": ("sbuf", [128, 2 * MS], BF),
+    "WP": ("sbuf", [128, V + 16], BF), "RLW": ("sbuf", [128, V + 32], BF), "TAB": ("sbuf", [128, 2 * MS], BF),
     "RLI": ("sbuf", [128, 256], I32), "RLB": ("sbuf", [128, 256], BF), "RLL": ("sbuf", [128, 256], BF),
     "CBI": ("sbuf", [128, 256], I32), "COI": ("sbuf", [128, 256], I32), "CB16": ("sbuf", [128, 256], U16),
     "COX": ("sbuf", [128, 520], BF),
-    "DMI": ("sbuf", [128, 2, 16, 16], I32), "DMR": ("sbuf", [128, 16, 32], F32),
-    "DMU": ("sbuf", [128, 16, 32], F32), "DMZ": ("sbuf", [128, 512], U16),
+    "DMI": ("sbuf", [128, 2, 16, 16], I32), "DMR": ("sbuf", [128, 16, 32], F16),
+    "DMU": ("sbuf", [128, 16, 32], F16), "DMZ": ("sbuf", [128, 512], U16),
     "OMI": ("sbuf", [128, 512], I32), "OMB": ("sbuf", [128, 512], BF),
     "PI": ("sbuf", [128, 128], F32), "PC": ("sbuf", [128, 4], I32), "PD": ("sbuf", [128, 4], I32),
     "PF": ("sbuf", [128, 4], F32), "LO": ("sbuf", [128, 256], BF), "HI": ("sbuf", [128, 256], BF),
     "ID": ("sbuf", [128, 128], BF), "IB": ("sbuf", [128, 16, 8], BF), "IF": ("sbuf", [128, 128], F32),
-    "IH": ("sbuf", [128, 128], F16), "IK": ("sbuf", [128, 128], BF),
-    "ONE": ("sbuf", [128, 128], BF), "C16": ("sbuf", [128, 64], BF), "MASK": ("sbuf", [128, MS // 4], BF),
-    "FS": ("sbuf", [128, 72], BF),
-    "X": ("sbuf", [128, 129, 8], BF), "TH": ("sbuf", [128, 17, 8], F16),
-    "BO": ("sbuf", [128, NCH, 128], F32),
-    "W": ("sbuf", [128, V], BF), "IND": ("sbuf", [128, V], BF), "SC": ("sbuf", [128, V], BF),
+    "IH": ("sbuf", [128, 128], F16), "IK": ("sbuf", [128, 128], BF), "IS": ("sbuf", [128, 128], BF),
+    "IM": ("sbuf", [128, 128], BF), "IP": ("sbuf", [128, 128], F16), "IN": ("sbuf", [128, 128], F16),
+    "ZR": ("sbuf", [128, 192], BF),
+    "ONE": ("sbuf", [128, 128], BF), "C16": ("sbuf", [128, 64], BF), "MASK": ("sbuf", [128, 1024], BF),
+    "FS": ("sbuf", [128, 64], BF), "THR": ("sbuf", [128, 4], F32),
+    "X0": ("sbuf", [128, 129, 8], F16), "X1": ("sbuf", [128, 129, 8], F16),
+    "XM0": ("sbuf", [128, 17, 8], BF), "XM1": ("sbuf", [128, 17, 8], BF),
+    "B": ("sbuf", [128, 256], F32),
+    "W0": ("sbuf", [128, V], BF), "W1": ("sbuf", [128, V], BF), "IND": ("sbuf", [128, V], BF), "SC": ("sbuf", [128, V], BF),
     "GT": ("sbuf", [128, V], BF), "IDX": ("sbuf", [128, 256], U16),
-    "MSG": ("sbuf", [128, (NM + 1) * 128], U16), "OUT": ("sbuf", [128, (NM + 1) * 128], U16),
+    "MSG": ("sbuf", [128, NM * 64], U16), "OUT": ("sbuf", [128, NM * 64], U16),
+    "OIN": ("sbuf", [128, STEPS * 256], BF), "OOUT": ("sbuf", [128, NM * 64], BF),
     "PK": ("sbuf", [128, STEPS * 256], BF), "EIN": ("sbuf", [128, 4 * 256], BF),
     "ZW": ("sbuf", [128, 64], F32), "YO": ("sbuf", [128, NCH * 128], F32), "YI": ("sbuf", [128, NCH * 128], F32),
-    "R0": ("psum", [128, 512], F32), "R1": ("psum", [128, 512], F32), "R2": ("psum", [128, 512], F32),
+    "R0": ("psum", [128, 512], F32), "R1": ("psum", [128, 512], F32),
     "VB": ("psum", [128, 512], F32), "JB": ("psum", [128, 512], F32), "F0": ("psum", [128, 512], F32),
-    "F1": ("psum", [128, 512], F32), "BB": ("psum", [128, 512], F32),
+    "F1": ("psum", [128, 512], F32), "BB": ("psum", [128, 512], F32), "OB": ("psum", [128, 512], F32),
 }
-SEMAPHORES = (["cA", "cV", "cP", "cG", "sent", "outs", "a_rl"] + ["d%d" % i for i in range(28)]
-              + ["m%d" % n for n in range(NM + 1)] + ["y%d" % c for c in range(NCH)] + ["e%d" % i for i in range(4)])
+SEMAPHORES = (["cA", "cV", "cP", "cG", "sent", "outs", "a_rl"] + ["d%d" % i for i in range(32)]
+              + ["m%d" % n for n in range(NM)] + ["o%d" % n for n in range(NM)]
+              + ["y%d" % c for c in range(NCH)] + ["e%d" % i for i in range(4)])
 
-COST = dict(r=1.56, ov=30.0, pe=0.5, hop=120.0, lat=4200.0, call=700.0, dma0=2300.0, dmab=0.0045, look=70.0,
-            xv=14, xl={0: 32, 22: 24, 23: 32}, ta=(128, 128), pre=3, mid=4, lead=1.5, first=3.2, wv=(), loads="wdco", sw=1024,
-            bias={"PIK": -700.0, "Vmb": 2200.0, "VSC": 900.0, "Ppp": 2100.0, "VIDX": -200.0, "VTAB": 1500.0,
-                  "VPK": -800.0, "Voc": 900.0, "VIND": -800.0, "Vh1": 900.0, "PGT": 900.0, "VO": -600.0})
+FRONT = ("w0", "w1", "w2", "d0", "d1", "c0", "c1", "fix", "sc", "vote", "jb", "mb", "jm", "idx")
+
+COST = dict(r=1.56, ov=3.0, ova=3.0, pe=0.63, hop=60.0, lat=3300.0, first=2000.0, call=700.0, dma0=2000.0, dmab=0.0045, look=70.0,
+            cmp="VV", wa=40, ga=64, ta=128, loads="wdco", og=2, nr=0, split=1, zc=1, sp=1, pkg=0,
+            wx={0: 32, 1: 64, 2: 64, 22: 48, 23: 48}, gx={0: 32, 1: 48, 22: 48, 23: 32},
+            tau={'first0': 0, 'first1': 1, 'back0': 0, 'back1': 1, 'tab0': 0.45, 'tab1': 0.01, 'Vw11': -0.8, 'Sy': 4, 'Se': 4.5, 'from': 9,
+                 'Amb': 0.54, 'Aw0': -0.19, 'Agt': 1.43, 'Aoo': 2.47, 'Ay': 2.84, 'Ays': 10.07, 'Vw1': 0.07, 'Vh': 2.35, 'Vth': 2.35,
+                 'Vrs': 2.38, 'Vidx': 1.35, 'Vpp': 2.37, 'Vb': 0.77, 'Vout': 2.52, 'Vzw': 2.73, 'Vy': 3.04, 'Vc0': 0.58, 'Vfix': 0.78,
+                 'Vsc': 0.94, 'Vpk': 1.4, 'Vgt': 1.85, 'Pvote': 0.5, 'Pf': 1.53, 'Pjm': 0.95, 'Pbb': 2.28, 'Poa': 1.49, 'Pos': 2.28,
+                 'Pob': 2.44, 'Pjb': 0.76, 'Gout': 3.35, 'Goo': 3.89, 'Ge': 4.62, 'Gy': 5.69,
+                 'om': -8.73, 'co': 0.42, 'Aw01': -12.32, 'Pf2': 0.45, 'Vsc3': -0.39, 'Vc00': -8.86, 'Vth4': -0.36, 'Vgt0': -0.21, 'Atab2': -3.92, 'Pf3': 0.26, 'Vout0': -0.3, 'Vsc1': -1.41, 'Vth0': -0.28, 'Vw13': -2.32, 'Amb1': -1.68, 'Atab0': -5.11, 'Pjb4': 0.03, 'Pvote1': -2.08, 'Aw03': -0.33, 'Vw10': -11.42, 'Agt0': -1.0, 'Vc04': 0.1, 'Pjb0': -2.41, 'Vfix0': -6.42, 'Amb0': -3.44, 'Atab1': -9.97, 'Aw02': -2.49, 'Poa1': -0.15, 'Pjm1': -0.95, 'Pvote0': -7.09, 'Vh0': -0.43, 'Pjb1': -7.19, 'Vc01': -2.84, 'Vidx2': -0.17, 'Vidx1': -1.42, 'Vout1': -0.18, 'Vc03': -0.65, 'Vw14': -0.46, 'Vth2': -0.33, 'Vh1': -0.6, 'Vtab0': -6.94, 'Atab-1': -4.46, 'Aw00': -9.64, 'Vtab3': -1.92, 'Atab3': -3.57, 'Vtab1': -4.96, 'Vgt1': -0.65, 'Amb3': -0.43, 'Vidx0': -2.04, 'Vfix3': -0.39, 'Pjm0': -2.24, 'Pf1': -0.07, 'Vsc0': 0.72, 'Agt2': -0.52, 'Vsc2': 0.53, 'Vth1': -0.57, 'Vfix1': -1.69, 'Vtab2': -2.2, 'Vh4': -0.3, 'Vc022': -0.19, 'Pbb22': 2.55, 'Vrs23': 4.28, 'Vpk23': 0.48, 'Gy23': 6.88, 'Aw021': 0.09, 'Gy20': -1.21, 'Vzw21': 0.08, 'Pf20': 0.59, 'Vh23': 1.72, 'Vpp22': 1.88, 'Vfix22': -0.36, 'Pbb23': 3.49, 'Pf22': 2.42, 'Vzw22': 1.81, 'Vpp23': 5.2, 'Pob22': 3.76, 'Vzw23': 5.03, 'Pvote23': 1.26, 'Pjm21': 0.35, 'Pob23': 3.77, 'Aw022': 0.49, 'Gy22': 4.89, 'Pjb21': 0.49, 'Vsc23': 0.28, 'Vy23': 9.17, 'Vrs22': 1.21, 'Pf23': 3.07, 'Pjb23': 0.98, 'Pbb20': 0.08, 'Vth23': 1.41, 'Vgt23': 0.45, 'Vy22': 2.96, 'Pjm23': 2.69})
 
 
 def build(g, T, to_next, to_prev, cost):
@@ -45,28 +57,31 @@ def build(g, T, to_next, to_prev, cost):
     A, M = AluOpType, ActivationFunctionType
     v, s, pe = g.vector, g.scalar, g.tensor
     nd = [0]
+    now = [None, None]
 
     def op(eng, fn, rd, wr, dur, banks=(), kind="c", sem=None, after=None, lat=0.0):
         ops.append(dict(eng=eng, fn=fn, rd=rd, wr=wr, dur=dur, banks=banks, kind=kind, sem=sem, after=after,
-                        lat=lat, i=len(ops)))
+                        lat=lat, i=len(ops), n=now[0], tag=now[1]))
         return len(ops) - 1
+
+    def at(tag):
+        now[1] = tag
 
     def vec(fn, rd, wr, n, banks=()):
         return op("V", lambda: [fn()], rd, wr, max(64.0, n) + cost["ov"], banks)
 
-    def act(fn, rd, wr, n):
-        return op("A", lambda: [fn()], rd, wr, max(64.0, n) + cost["ov"])
+    def act(fn, rd, wr, n, banks=()):
+        return op("A", lambda: [fn()], rd, wr, max(64.0, n) + cost["ova"], banks)
 
-    def gather(eng, out, win, rd, wr, n, slot=None):
+    def gather(eng, out, win, rd, wr, n):
         if eng == "A":
-            i = op("A", lambda: [s.activation(out, win, M.Copy)], rd, wr, 78 + cost["r"] * n)
-            ops[i]["slot"] = slot
-            return i
+            return op("A", lambda: [s.activation(out, win, M.Copy)], rd, wr, 78 + cost["r"] * n)
         return op("V", lambda: [v.tensor_copy(out, win)], rd, wr, 60 + cost["r"] * n)
 
     def mm(lst, rd, banks):
         n = sum(x[5] for x in lst)
-        return op("P", lambda: [pe.matmul(x[0], x[1], x[2], x[3], x[4]) for x in lst], rd, [], n * cost["pe"] + 30, banks)
+        return op("P", lambda: [pe.matmul(x[0], x[1], x[2], x[3], x[4]) for x in lst], rd, [],
+                  n * cost["pe"] + 30 + len(lst) * cost.get("ovp", 0.0), banks)
 
     def dma(out, in_, rd, wr, nbytes, q="S", sem=None, order=False):
         if sem is None:
@@ -95,10 +110,8 @@ def build(g, T, to_next, to_prev, cost):
         calls[sem] = i
         op(None, None, [], wr, 0.0, kind="arr", sem=sem, after=i, lat=cost["lat"] + more)
 
-    X = T.X
-
-    def xv(f, n=1):
-        return X[:, f * 16 + 1:(f + n) * 16:2, :]
+    def xv(buf, f, n=1):
+        return buf[:, f * 16 + 1:(f + n) * 16:2, :]
 
     def xt(buf, f, kh):
         return buf[:, f * 16 + 1 - kh:f * 16 + 17 - kh, :]
@@ -120,45 +133,60 @@ def build(g, T, to_next, to_prev, cost):
     dma(T.WP[:, V:V + 16], T.wp[:, 0:16], [], ["WPw"], 65536, q="A")
 
     vec(lambda: v.tensor_copy(T.RLB[:], T.RLI[:]), ["RLI"], ["RLB"], 256)
-    send(T.RLL[:], [T.RLB[:]], to_prev, "a_rl", ["RLB"], ["RLL"], more=3000.0)
+    send(T.RLL[:], [T.RLB[:]], to_prev, "a_rl", ["RLB"], ["RLL"], more=cost["first"])
 
     op("G", lambda: [g.iota(T.PI[:], [[-1, 128]], 0, 1, allow_small_or_imprecise_dtypes=True)], [], ["PI"], 420.0)
     op("G", lambda: [g.iota(T.PC[:, 0:1], [[0, 1]], 0, 1)], [], ["PC"], 160.0)
     op("G", lambda: [g.iota(T.LO[:], [[1, 256]], 0, 0, allow_small_or_imprecise_dtypes=True)], [], ["LO"], 670.0)
-    vec(lambda: v.memset(T.MASK[:], 1.0), [], ["MASK"], MS // 8)
+    vec(lambda: v.memset(T.MASK[:], 1.0), [], ["MASK"], 512)
     for k in range(4):
-        q = MS // 4
-        act(lambda k=k, q=q: s.activation(T.RLW[:, k * q:(k + 1) * q], T.MASK[:], M.Copy), ["MASK"], [("RLW0", k)], q)
-    vec(lambda: v.memset(T.MASK[:, 0:1024:16], 0.0), [], ["MASK"], 64)
+        act(lambda k=k: s.activation(T.RLW[:, 16 + k * 1024:16 + (k + 1) * 1024], T.MASK[:], M.Copy), ["MASK"], [("RLW0", k)], 1024)
+    vec(lambda: v.memset(T.MASK[:, 0::16], 0.0), [], ["MASK"], 64)
     vec(lambda: v.memset(T.ONE[:], 1.0), [], ["ONE"], 64)
     vec(lambda: v.memset(T.C16[:], 16.0), [], ["C16"], 64)
-    vec(lambda: v.memset(X[:], 0.0), [], ["X0"], 516)
-    vec(lambda: v.memset(xv(0), 1.0), ["X0"], ["Xone"], 64)
-    vec(lambda: v.tensor_copy(T.TH[:], X[:, 16:33, :]), ["X0"], ["TH0"], 68)
     vec(lambda: v.memset(T.COX[:], 0.0), [], ["COX"], 260)
+    vec(lambda: v.memset(T.ZR[:], 0.0), [], ["ZR"], 96)
+    vec(lambda: v.tensor_scalar(T.X0[:, 0:65, :], T.COX[:], 0.0, None, A.mult), ["COX"], [("X0", 0, 0)], 260)
+    vec(lambda: v.tensor_scalar(T.X0[:, 64:129, :], T.COX[:], 0.0, None, A.mult), ["COX"], [("X0", 0, 0)], 260)
+    if not cost["split"]:
+        vec(lambda: v.tensor_copy(xv(T.X0, 0), T.ONE[:, 0:64]), ["ONE"], [("X0", 0, 0)], 64)
+    vec(lambda: v.tensor_copy(T.X1[:], T.X0[:]), [("X0", 0, 0)], [("X0", 1, 0)], 516)
+    for p in range(2):
+        act(lambda p=p: s.activation(T["XM%d" % p][:], T.ZR[:, 0:136], M.Copy), ["ZR"], [("XM0", p)], 136)
+    for j, (lo, hi) in enumerate(("AA", "AV", "VA", "VV")):
+        if lo + hi in [cost["cmp"][k:k + 2] for k in range(0, len(cost["cmp"]), 2)]:
+            if lo == hi:
+                vec(lambda j=j, lo=lo: v.memset(T.THR[:, j:j + 1], -1.0 if lo == "A" else -64.5), [], [("THR", j, 0), ("THR", j, 1)], 1)
+            else:
+                vec(lambda j=j, lo=lo: v.memset(T.THR[0:64, j:j + 1], -1.0 if lo == "A" else -64.5), [], [("THR", j, 0)], 1)
+                vec(lambda j=j, hi=hi: v.memset(T.THR[64:128, j:j + 1], -1.0 if hi == "A" else -64.5), [], [("THR", j, 1)], 1)
     vec(lambda: v.tensor_scalar(T.ID[:], T.PI[:], 0.0, None, A.is_equal), ["PI"], ["ID"], 128)
-    vec(lambda: v.tensor_copy(T.IB[:], T.ID[:]), ["ID"], ["IB"], 64)
     vec(lambda: v.tensor_copy(T.IH[:], T.ID[:]), ["ID"], ["IH"], 64)
+    vec(lambda: v.tensor_scalar(T.IP[:], T.ID[:], 512.0, None, A.mult), ["ID"], ["IP"], 64)
+    vec(lambda: v.tensor_scalar(T.IN[:], T.ID[:], -512.0, None, A.mult), ["ID"], ["IN"], 64)
+    act(lambda: s.activation(T.IB[:], T.ID[:], M.Copy), ["ID"], ["IB"], 128)
+    if "A" in cost["cmp"]:
+        act(lambda: s.activation(T.IM[:], T.ID[:], M.Copy, scale=-1.0), ["ID"], ["IM"], 128)
     act(lambda: s.activation(T.IF[:], T.ID[:], M.Copy), ["ID"], ["IF"], 128)
-    act(lambda: s.activation(T.IK[:], T.ID[:], M.Copy, scale=float(MS)), ["ID"], ["IK"], 128)
+    act(lambda: s.activation(T.IK[:], T.ID[:], M.Copy, scale=MS / 2.0), ["ID"], ["IK"], 128)
+    act(lambda: s.activation(T.IS[:], T.ID[:], M.Copy, scale=1.0 / 512), ["ID"], ["IS"], 128)
 
     def row(f):
         return T.ID[:, f::16]
 
     def fs(f):
         return T.FS[:, f * 8:(f + 1) * 8]
-    vec(lambda: v.tensor_copy(fs(0), row(5)), ["ID"], [("FS", 0)], 8)
-    vec(lambda: v.tensor_scalar(fs(1), row(0), -1.0, None, A.mult), ["ID"], [("FS", 1)], 8)
-    vec(lambda: v.tensor_scalar(fs(2), row(1), -1.0, None, A.mult), ["ID"], [("FS", 2)], 8)
-    vec(lambda: v.tensor_tensor(fs(3), row(0), row(5), A.subtract), ["ID"], [("FS", 3)], 8)
-    vec(lambda: v.tensor_tensor(fs(7), row(2), row(6), A.subtract), ["ID"], [("FS", 7)], 8)
-    vec(lambda: v.tensor_scalar(fs(8), row(3), 256.0, None, A.mult), ["ID"], [("FS", 8)], 8)
-    vec(lambda: v.tensor_tensor(fs(4), fs(3), row(1), A.add), ["ID", ("FS", 3)], [("FS", 4)], 8)
-    vec(lambda: v.tensor_tensor(fs(6), fs(8), row(4), A.add), ["ID", ("FS", 8)], [("FS", 6)], 8)
-    vec(lambda: v.tensor_tensor(fs(5), fs(4), fs(7), A.add), [("FS", 4), ("FS", 7)], [("FS", 5)], 8)
+    vec(lambda: v.tensor_tensor(fs(0), row(5), row(0), A.subtract), ["ID"], [("FS", 0)], 8)
+    vec(lambda: v.tensor_tensor(fs(1), fs(0), row(1), A.subtract), ["ID", ("FS", 0)], [("FS", 1)], 8)
+    vec(lambda: v.tensor_tensor(fs(7), fs(1), row(2), A.subtract), ["ID", ("FS", 1)], [("FS", 7)], 8)
+    vec(lambda: v.tensor_tensor(fs(4), row(3), row(4), A.add), ["ID"], [("FS", 4)], 8)
+    act(lambda: s.activation(fs(2), fs(7), M.Copy, scale=1.0 / 512), [("FS", 7)], [("FS", 2)], 8)
+    act(lambda: s.activation(fs(3), row(5), M.Copy, scale=1.0 / 512), ["ID"], [("FS", 3)], 8)
+    act(lambda: s.activation(fs(5), row(0), M.Copy, scale=-1.0 / 512), ["ID"], [("FS", 5)], 8)
+    act(lambda: s.activation(fs(6), row(1), M.Copy, scale=-1.0 / 512), ["ID"], [("FS", 6)], 8)
     FSK = [("FS", f) for f in range(7)]
     vec(lambda: v.tensor_scalar(T.PD[:, 0:1], T.PC[:, 0:1], 15, None, A.bitwise_and), ["PC"], ["PD"], 1)
-    vec(lambda: v.tensor_scalar(T.PF[:, 0:1], T.PD[:, 0:1], -8.0, None, A.add), ["PD"], ["PF"], 1)
+    vec(lambda: v.tensor_scalar(T.PF[:, 0:1], T.PD[:, 0:1], -8.0, 256.0, A.add, A.mult), ["PD"], ["PF"], 1)
     vec(lambda: v.tensor_scalar(T.HI[:], T.LO[:], 0.0, T.PF[:, 0:1], A.mult, A.add), ["PF", "LO"], ["HI"], 128)
 
     R0K = [("RLW0", k) for k in range(4)]
@@ -171,134 +199,221 @@ def build(g, T, to_next, to_prev, cost):
     RLK = R0K + [("RLW", f) for f in (0, 1, 2, 3, 4, 11, 12)]
 
     for g0 in range(2):
-        vec(lambda g0=g0: v.tensor_copy(T.DMR[:, :, g0 * 16:(g0 + 1) * 16], T.DMI[:, g0, :, :]),
+        vec(lambda g0=g0: v.tensor_scalar(T.DMR[:, :, g0 * 16:(g0 + 1) * 16], T.DMI[:, g0, :, :], -2048.0, None, A.add),
             [("DMI", g0, 0), ("DMI", g0, 1)], [("DMR", g0)], 256)
-    vec(lambda: v.transpose(T.DMU[:], T.DMR[:]), [("DMR", 0), ("DMR", 1)], ["DMU"], 512)
+    vec(lambda: v.transpose(T.DMU[:], T.DMR[:]), [("DMR", 0), ("DMR", 1)], ["DMU"], 256)
     for b in range(8):
-        vec(lambda b=b: v.tensor_copy(T.DMZ[:, b::8], T.DMU[:, b::8, :]), ["DMU"], [("DMZ", b)], 64)
+        vec(lambda b=b: v.tensor_scalar(T.DMZ[:, b::8], T.DMU[:, b::8, :], 2048.0, None, A.add), ["DMU"], [("DMZ", b)], 32)
     ZK = [("DMZ", b) for b in range(8)]
-    vec(lambda: v.tensor_copy(T.OMB[:], T.OMI[:]), [("OMI", 0), ("OMI", 1)], ["OMB"], 512)
 
     vec(lambda: v.tensor_copy(T.CB16[:], T.CBI[:]), ["CBI"], ["CB16"], 256)
-    vec(lambda: v.tensor_copy(T.BO[:, :, 0:64], T.CBI[:]), ["CBI"], [("B", c) for c in range(NCH)], 256)
-    vec(lambda: v.tensor_copy(T.COX[:, 1:513:2], T.COI[:]), ["COI"], ["COX"], 256)
-    mm([(T.F1[:, (c + 1) % NCH * 64:(c + 1) % NCH * 64 + 64], T.COX[:, 128 * c + 1 - kh:128 * c + 129 - kh], T.IB[:, kh::2, :],
-         kh == 0, kh == 1, 64) for c in range(NCH) for kh in range(2)], ["COX", "IB"], ["F1"])
-    vec(lambda: v.tensor_copy(T.BO[:, :, 64:128], T.F1[:, 0:256]), [], [("O", c) for c in range(NCH)], 256, ["F1"])
-
-    TK = []
+    vec(lambda: v.tensor_copy(T.B[:], T.CBI[:]), ["CBI"], [("B", c) for c in range(NCH)], 256)
+    at("co")
+    vec(lambda: v.tensor_scalar(T.COX[:, 1:513:2], T.COI[:], 1.0, None, A.add), ["COI"], ["COX"], 256)
+    mm([(T.OB[:, c * 64:c * 64 + 64], T.COX[:, 128 * c + 1 - kh:128 * c + 129 - kh], T.IB[:, kh::2, :],
+         kh == 0, kh == 1, 64) for c in range(NCH) for kh in range(2)], ["COX", "IB"], ["OB"])
+    act(lambda: s.activation(T.OIN[:, 0:256], T.OB[:, 0:256], M.Copy), [], [("OIN", c) for c in range(NCH)], 256, ["OB"])
+    at("om")
     for m in range(2):
+        vec(lambda m=m: v.tensor_copy(T.OMB[:, m * 256:(m + 1) * 256], T.OMI[:, m * 256:(m + 1) * 256]), [("OMI", m)], [("OMB", m)], 256)
+
+    at("tab")
+    TK = []
+    na = cost["ta"]
+    for m in range(2):
+        now[0] = -1
+        gather("A", T.TAB[:, m * MS + V:(m + 1) * MS], T.RLW[:, 16:16 + V].indirect(T.DMZ[:, m * 256:m * 256 + 2]),
+               RLK + ZK, [("TAB", m, V)], 32)
+        dma(T.TAB[5::16, m * MS + V:m * MS + V + 2], T.OMB[0::16, m * 256:m * 256 + 2], [("OMB", m)], [("TAB", m, V)], 100)
         pk = []
-        na = cost["ta"][m]
-        for eng, a, b in (("A", 0, na), ("V", na, (na + 256) // 4 * 2), ("V", (na + 256) // 4 * 2, 256)):
+        for k, (eng, a, b) in enumerate((("A", 0, na // 4 * 2), ("V", na, (na + 256) // 4 * 2), ("A", na // 4 * 2, na), ("V", (na + 256) // 4 * 2, 256))):
+            now[0] = 2 * m + k // 2
             gather(eng, T.TAB[:, m * MS + a * 16:m * MS + b * 16],
                    T.RLW[:, 16:16 + V].indirect(T.DMZ[:, m * 256 + a:m * 256 + b]),
-                   RLK + ZK, [("TAB", m, a * 16)], (b - a) * 16, slot=-50 + m)
+                   RLK + ZK, [("TAB", m, a * 16)], (b - a) * 16)
             pk.append(("TAB", m, a * 16))
-        gather("A", T.TAB[:, m * MS + V:(m + 1) * MS], T.RLW[:, 16:16 + V].indirect(T.DMZ[:, m * 256:m * 256 + 2]),
-               RLK + ZK, [("TAB", m, V)], 32, slot=-51 + m * 0.1)
-        dma(T.TAB[5::16, m * MS:m * MS + V], T.OMB[:, m * 256:(m + 1) * 256], ["OMB"], pk, 65536)
-        dma(T.TAB[5::16, m * MS + V:m * MS + V + 2], T.OMB[0::16, m * 256:m * 256 + 2], ["OMB"], [("TAB", m, V)], 100)
+        dma(T.TAB[5::16, m * MS:m * MS + V], T.OMB[:, m * 256:(m + 1) * 256], [("OMB", m)], pk, 65536)
         TK += pk + [("TAB", m, V)]
 
     nr = [0]
+    spare = ["R0", "R1"][cost["nr"]:]
     for t in range(STEPS):
         last = t == STEPS - 1
         for c in range(NCH):
-            w0 = c * 1024
+            w0, l0 = c * 1024, c * 64
             n = t * NCH + c
+            now[0] = n
+            W = T["W%d" % (t % 2)]
+            X, XM, xp = T["X%d" % (n % 2)], T["XM%d" % (n % 2)], n % 2
+            jb = spare[0] if spare and n % 2 else "JB"
+            vb = spare[1] if len(spare) > 1 and n % 2 else "VB"
+            JB, VB = T[jb], T[vb]
             if t == 0:
-                lst, l0, lk = T.CB16, c * 64, "CB16"
+                lst, c0, lk = T.CB16, l0, "CB16"
             else:
-                lst, l0, lk = T.MSG, (n - NCH) * 128, ("MSG", n - NCH)
+                lst, c0, lk = T.MSG, (n - NCH) * 64, ("MSG", n - NCH)
+                at("b")
+                vec(lambda c0=c0, l0=l0: v.tensor_copy(T.B[:, l0:l0 + 64], T.MSG[:, c0:c0 + 64]), [lk], [("B", c)], 64)
+
+            def wk(a, b):
+                return [("W", t % 2, c, k) for k in range(a // 2, b // 2)]
+            cmp = cost["cmp"][2 * n % len(cost["cmp"]):][:2]
+            wa = cost.get("wx", {}).get(n, cost["wa"])
+            cuts = sorted({0, wa, 64} | ({32} if cmp != "VV" or cost.get("halves") else set()))
+            for k, (a, b) in enumerate(zip(cuts, cuts[1:])):
+                at("w%d" % k)
+                gather("A" if b <= wa else "V", W[:, w0 + a * 16:w0 + b * 16], T.WP[:, 0:V + 16].indirect(lst[:, c0 + a:c0 + b]),
+                       ["WP", "WPw", lk], wk(a, b), (b - a) * 16)
             for h in range(2):
-                a = w0 + h * 512
-                gather("V" if (n, h) in cost["wv"] else "A", T.W[:, a:a + 512],
-                       T.WP[:, 0:V + 16].indirect(lst[:, l0 + h * 32:l0 + h * 32 + 32]),
-                       ["WP", "WPw", lk], [("W", c, h)], 512,
-                       slot=(n - 100 if n < cost["pre"] else n - 40 if n < cost["mid"] else
-                             max(n - cost["lead"], cost["first"] + 0.01 * n)) + 0.001 * h)
-                rb = "R%d" % (nr[0] % 3)
-                nr[0] += 1
-                mm([(T[rb][:, 0:511], T.ID[:], T.W[:, a + 1:a + 512], True, True, 511),
-                    (T[rb][:, 15:512:16], T.ID[:], T.W[:, a:a + 512:16], True, True, 64)], ["ID", ("W", c, h)], [rb])
-                vec(lambda a=a, rb=rb: v.tensor_tensor(T.IND[:, a:a + 512], T.W[:, a:a + 512], T[rb][:], A.is_gt),
-                    [("W", c, h)], [("IND", c, h)], 512, [rb])
-            sw = cost["sw"]
-            for a in range(w0, w0 + 1024, sw):
-                vec(lambda a=a, sw=sw: v.tensor_tensor_scan(T.SC[:, a:a + sw], T.MASK[:, 0:sw], T.W[:, a:a + sw],
-                                                            0.0, A.mult, A.max),
-                    ["MASK"] + [("W", c, h) for h in range((a - w0) // 512, (a - w0 + sw) // 512)], [("SC", a)], sw // 2)
+                a, b = w0 + h * 512, w0 + h * 512 + 512
+                if cmp[h] == "A":
+                    rb = "R%d" % (nr[0] % cost["nr"])
+                    nr[0] += 1
+                    R = T[rb]
+                    at("d%d" % h)
+                    mm([(R[:], T.ID[:], W[:, a:b], True, False, 512),
+                        (R[:, 0:511], T.IM[:], W[:, a + 1:b], False, False, 511),
+                        (R[:, 15:511:16], T.ID[:], W[:, a + 16:b:16], False, False, 64),
+                        (R[:, 15:512:16], T.IM[:], W[:, a:b:16], False, True, 64)], ["ID", "IM"] + wk(h * 32, h * 32 + 32), [rb])
+                    at("c%d" % h)
+                    act(lambda a=a, b=b, R=R: s.activation(T.IND[:, a:b], R[:], M.Sign, bias=-0.5), [], [("IND", c, h)], 512, [rb])
+                elif cmp != "VV" or cost.get("halves") or h == 0:
+                    hs = [0, 1] if cmp == "VV" and not cost.get("halves") else [h]
+                    b = w0 + hs[-1] * 512 + 512
+                    at("c%d" % h)
+                    vec(lambda a=a, b=b, W=W: v.tensor_tensor(T.IND[:, a:b - 1], W[:, a:b - 1], W[:, a + 1:b], A.is_gt),
+                        wk(h * 32, hs[-1] * 32 + 32), [("IND", c, k) for k in hs], b - a)
+            hs = [h for h in range(2) if cmp[h] == "V"]
+            if hs:
+                a, b = w0 + hs[0] * 512, w0 + hs[-1] * 512 + 512
+                at("fix")
+                vec(lambda a=a, b=b, W=W: v.tensor_tensor(T.IND[:, a + 15:b:16], W[:, a + 15:b:16], W[:, a:b:16], A.is_gt),
+                    wk(hs[0] * 32, hs[-1] * 32 + 32), [("IND", c, k) for k in hs], (b - a) // 16)
+            at("sc")
+            vec(lambda w0=w0, W=W: v.tensor_tensor_scan(T.SC[:, w0:w0 + 1024], T.MASK[:], W[:, w0:w0 + 1024], 0.0, A.mult, A.max),
+                ["MASK"] + wk(0, 64), [("SC", c)], 512)
             if c == NCH - 1:
-                vec(lambda t=t: v.tensor_copy(T.PK[:, t * 256:(t + 1) * 256], T.SC[:, 15::16]),
-                    [("SC", a) for a in range(0, V, sw)], [("PK", t, k) for k in range(NCH)], 128)
-            mm([(T.VB[:, kl:64:8], T.IND[:, w0 + kl:w0 + 1024:8], T.ONE[:, 0:8], True, True, 64) for kl in range(8)],
-               ["ONE", ("IND", c, 0), ("IND", c, 1)], ["VB"])
-            mm([(T.JB[:, 0:64], T.IF[:], T.BO[:, c, 0:64], True, False, 256)], ["IF", ("B", c)], ["JB"])
-            vec(lambda: v.tensor_scalar(xv(7), T.VB[:, 0:64], 65.0, None, A.is_ge), ["X0"], ["mb"], 64, ["VB"])
-            mm([(T.JB[:, 0:64], xt(X, 7, kh), T.IK[:, kh::2], False, kh == 1, 64) for kh in range(2)],
-               ["X0", "mb", "IK"], ["JB"])
-            vec(lambda c=c: v.tensor_copy(T.IDX[:, c * 64:(c + 1) * 64], T.JB[:, 0:64]), [], [("IDX", c)], 64, ["JB"])
-            nv = cost["xl"].get(n, cost["xv"])
-            na = 64 - nv
-            gather("A", T.GT[:, w0:w0 + na * 16], T.TAB[:].indirect(T.IDX[:, c * 64:c * 64 + na]),
-                   TK + [("IDX", c)], [("GT", c, 0)], na * 16, slot=n)
-            if nv:
-                gather("V", T.GT[:, w0 + na * 16:w0 + 1024], T.TAB[:].indirect(T.IDX[:, c * 64 + na:c * 64 + 64]),
-                       TK + [("IDX", c)], [("GT", c, 1)], nv * 16)
-            fb = "F%d" % (c % 2)
+                at("pk")
+                if cost["pkg"] and not last:
+                    op("G", lambda t=t: [g.affine_select(T.PK[:, t * 256:(t + 1) * 256], T.SC[:, 15::16], [[0, 256]], A.is_ge, 0.0, 0, 0)],
+                       [("SC", k) for k in range(NCH)], [("PK", t)], 720.0)
+                else:
+                    vec(lambda t=t: v.tensor_copy(T.PK[:, t * 256:(t + 1) * 256], T.SC[:, 15::16]),
+                        [("SC", k) for k in range(NCH)], [("PK", t)], 128)
+            at("vote")
+            mm([(VB[:, kl:64:8], T.IND[:, w0 + kl:w0 + 1024:8], T.ONE[:, 0:8], True, True, 64) for kl in range(8)],
+               ["ONE"] + [("IND", c, h) for h in range(2)], [vb])
+            at("jb")
+            mm([(JB[:, 0:64], T.IF[:], T.B[:, l0:l0 + 64], True, False, 256)], ["IF", ("B", c)], [jb])
+            j = ["AA", "AV", "VA", "VV"].index(cmp)
+            at("mb")
+            act(lambda j=j, XM=XM, VB=VB: s.activation(xv(XM, 0), VB[:, 0:64], M.Sign, bias=T.THR[:, j:j + 1]),
+                [("XM0", xp), ("THR", j, 0), ("THR", j, 1)], [("mb", xp)], 64, [vb])
+            at("jm")
+            mm([(JB[:, 0:64], xt(XM, 0, kh), T.IK[:, kh::2], False, kh == 1, 64) for kh in range(2)],
+               [("XM0", xp), ("mb", xp), "IK"], [jb])
+            at("idx")
+            vec(lambda l0=l0, JB=JB: v.tensor_scalar(T.IDX[:, l0:l0 + 64], JB[:, 0:64], MS / 2.0, None, A.add), [], [("IDX", c)], 64, [jb])
+            na = cost.get("gx", {}).get(n, cost["ga"])
+            na += na % 2 * (1 if n % 2 else -1)
+            gk = []
+            at("gt")
+            for eng, a, b in (("A", 0, na), ("V", na, 64)):
+                if b > a:
+                    gather(eng, T.GT[:, w0 + a * 16:w0 + b * 16], T.TAB[:].indirect(T.IDX[:, l0 + a:l0 + b]),
+                           TK + [("IDX", c)], [("GT", c, eng)], (b - a) * 16)
+                    gk.append(("GT", c, eng))
+            fb = "F%d" % (n % 2)
             F = T[fb]
-            mm([(F[:, kl:448:8], T.GT[:, w0 + kl:w0 + 1024:8], T.FS[:, 0:56], True, True, 64) for kl in range(8)],
-               FSK + [("GT", c, 0), ("GT", c, 1)], [fb])
-            if n >= NCH - 1:
-                k = n - NCH + 1
-                lo, hi = (64 if k == NM else 0), (64 if k == 0 else 128)
-                vec(lambda k=k, lo=lo, hi=hi: v.tensor_copy(T.BO[:, k % NCH, lo:hi], T.MSG[:, k * 128 + lo:k * 128 + hi]),
-                    [("MSG", k)], [("B", k % NCH)] * (lo == 0) + [("O", c)] * (hi == 128), hi - lo)
-            o32 = T.BO[:, (c + 1) % NCH, 64:128]
-            vec(lambda F=F, o32=o32: v.tensor_tensor(xv(1), o32, F[:, 192:256], A.is_ge), ["X0", "TH0", ("O", c)], ["h1"], 64, [fb])
-            vec(lambda F=F, o32=o32: v.tensor_tensor(xv(2), o32, F[:, 256:320], A.is_ge), ["X0", "TH0", ("O", c)], ["h2"], 64, [fb])
-            vec(lambda F=F, o32=o32: v.tensor_tensor(xv(6), o32, F[:, 320:384], A.min), ["X0", ("O", c)], ["oc"], 64, [fb])
-            vec(lambda F=F: v.tensor_tensor(T.TH[:, 1:16:2, :], xv(1), F[:, 384:448], A.add), ["TH0", "h1"], ["th"], 64, [fb])
-            vec(lambda F=F: v.tensor_tensor(xv(3, 3), xv(0, 3), F[:, 0:192], A.mult), ["X0", "Xone", "h1", "h2"], ["pp"], 192, [fb])
-            mm([(T.BB[:, 0:64], T.ONE[:], T.C16[:], True, False, 64)]
-               + [(T.BB[:, 0:64], xt(X, 2, kh), T.ID[:, kh::2], False, False, 64) for kh in range(2)]
-               + [(T.BB[:, 0:64], xt(T.TH, 0, kh), T.IH[:, kh::2], False, kh == 1, 64) for kh in range(2)],
-               ["ONE", "C16", "ID", "IH", "X0", "TH0", "h2", "th"], ["BB"])
-            if not last:
-                def message(k, lo, hi):
-                    a, b = k * 128 + lo, k * 128 + hi
-                    vec(lambda: v.tensor_copy(T.OUT[:, a:b], T.BB[:, lo:hi]), [], [("OUT", k)], hi - lo, ["BB"])
-                    send(T.MSG[:, a:b], [T.OUT[:, a:b]], to_next, "m%d" % k, [("OUT", k)], [("MSG", k)])
-                message(n, 0, 128 if n else 64)
-                mm([(T.BB[:, 64:128], T.ID[:], xv(f), f == 6, f == 5, 64) for f in (6, 3, 4, 5)],
-                   ["ID", "oc", "pp"], ["BB"])
-                if n == NM - 1:
-                    message(NM, 64, 128)
+            o1 = T.OIN[:, n * 64:n * 64 + 64]
+            if cost["zc"]:
+                at("oa")
+                mm([(F[:, f * 64:f * 64 + 64], (T.ID if f < 2 else T.IS)[:], o1, f == 0, False, 64) for f in range(4)]
+                   + [(F[:, 256:448], T.ID[:], T.ZR[:], False, False, 192)], ["ID", "IS", "ZR", ("OIN", n)], [fb])
+                at("f")
+                mm([(F[:, kl:448:8], T.GT[:, w0 + kl:w0 + 1024:8], T.FS[:, 0:56], False, kl == 7, 64) for kl in range(8)],
+                   FSK + gk, [fb])
             else:
-                mm([(T.BB[:, 64:128], xt(X, f, kh), T.ID[:, kh::2], (f, kh) == (6, 0), (f, kh) == (5, 1), 64)
-                    for f in (6, 3, 4, 5) for kh in range(2)], ["ID", "X0", "oc", "pp"], ["BB"])
+                at("f")
+                mm([(F[:, kl:448:8], T.GT[:, w0 + kl:w0 + 1024:8], T.FS[:, 0:56], kl == 0, False, 64) for kl in range(8)]
+                   + [(F[:, f * 64:f * 64 + 64], (T.ID if f < 2 else T.IS)[:], o1, False, f == 3, 64) for f in range(4)],
+                   FSK + gk + ["ID", "IS", ("OIN", n)], [fb])
+            x0 = ("X0", xp, 0)
+            if cost["split"]:
+                at("h")
+                vec(lambda F=F, X=X: v.tensor_scalar(xv(X, 1, 2), F[:, 0:128], 0.0, 1.0, A.max, A.min), [x0], [("h", xp)], 128, [fb])
+                at("th")
+                vec(lambda F=F, X=X: v.tensor_copy(xv(X, 5), F[:, 256:320]), [x0], [("th", xp)], 64, [fb])
+                at("rs")
+                nf = 1 if cost["sp"] and not last else 2
+                vec(lambda F=F, X=X, nf=nf: v.tensor_scalar(xv(X, 3, nf), F[:, 128:128 + 64 * nf], 0.0, None, A.max), [x0], [("rs", xp)], 64 * nf, [fb])
+                at("pp")
+                vec(lambda F=F, X=X: v.tensor_tensor(xv(X, 6, 2), xv(X, 1, 2), F[:, 320:448], A.mult), [x0, ("h", xp)], [("pp", xp)], 128, [fb])
+            else:
+                at("h")
+                vec(lambda F=F, X=X: v.tensor_scalar(xv(X, 1, 4), F[:, 0:256], 0.0, 1.0, A.max, A.min), [x0], [("h", xp), ("rs", xp)], 256, [fb])
+                at("pp")
+                vec(lambda F=F, X=X: v.tensor_tensor(xv(X, 5, 3), xv(X, 0, 3), F[:, 256:448], A.mult), [x0, ("h", xp)], [("th", xp), ("pp", xp)], 192, [fb])
+            lst = [(T.BB[:, 0:64], xt(X, f, kh), T.IH[:, kh::2], False, False, 64) for f in (1, 2, 5) for kh in range(2)]
+            if last:
+                lst = [(T.BB[:, 0:64], T.ONE[:], T.C16[:], False, False, 64)] + lst
+            lst[0] = lst[0][:3] + (True, False, 64)
+            lst[-1] = lst[-1][:3] + (False, True, 64)
+            at("bb")
+            mm(lst, ["ONE", "C16", "IH", x0, ("h", xp), ("th", xp)], ["BB"])
+            xk = ["IN", "IP", x0, ("rs", xp), ("pp", xp)]
+            if not last:
+                at("out")
+                vec(lambda n=n: v.tensor_scalar(T.OUT[:, n * 64:n * 64 + 64], T.BB[:, 0:64], 2048.0, None, A.add), [], [("OUT", n)], 64, ["BB"])
+                send(T.MSG[:, n * 64:n * 64 + 64], [T.OUT[:, n * 64:n * 64 + 64]], to_next, "m%d" % n, [("OUT", n)], [("MSG", n)])
+                at("ob")
+                if cost["sp"]:
+                    at("os")
+                    mm([(T.OB[:, l0:l0 + 64], T.ID[:], o1, True, False, 64)]
+                       + [(T.OB[:, l0 + kl:l0 + 64:8], T.GT[:, w0 + kl:w0 + 1024:8], row(5), False, False, 64) for kl in range(8)],
+                       ["ID", ("OIN", n)] + gk, ["OB"])
+                    at("ob")
+                    mm([(T.OB[:, l0:l0 + 64], (T.IN if f == 3 else T.IP)[:], xv(X, f), False, f == 7, 64) for f in (3, 6, 7)], xk, ["OB"])
+                else:
+                    mm([(T.OB[:, l0:l0 + 64], (T.IN if f == 3 else T.IP)[:], xv(X, f), f == 3, f == 7, 64) for f in (3, 4, 6, 7)], xk, ["OB"])
+                og = cost["og"]
+                if c % og == og - 1:
+                    a, b = (c + 1 - og) * 64, (c + 1) * 64
+                    at("oo")
+                    act(lambda t=t, a=a, b=b: s.activation(T.OOUT[:, t * 256 + a:t * 256 + b], T.OB[:, a:b], M.Copy),
+                        [], [("OOUT", n)], b - a, ["OB"])
+                    send(T.OIN[:, (t + 1) * 256 + a:(t + 1) * 256 + b], [T.OOUT[:, t * 256 + a:t * 256 + b]], to_next, "o%d" % n,
+                         [("OOUT", n)], [("OIN", k + NCH) for k in range(n + 1 - og, n + 1)], after=calls["m%d" % n])
+            else:
+                at("ob")
+                mm([(T.OB[:, l0:l0 + 64], xt(X, f, kh), (T.IN if f == 3 else T.IP)[:, kh::2], (f, kh) == (3, 0), (f, kh) == (7, 1), 64)
+                    for f in (3, 4, 6, 7) for kh in range(2)], xk, ["OB"])
                 y0 = c * 128
+                at("zw")
                 vec(lambda: v.tensor_scalar(T.ZW[:], T.BB[:, 0:64], float(V), -float(V), A.is_ge, A.mult), [], ["ZW"], 64, ["BB"])
-                vec(lambda y0=y0: v.tensor_copy(T.YO[:, y0 + 64:y0 + 128], T.BB[:, 64:128]), [], [("YO", c, 1)], 64, ["BB"])
+                at("y")
+                act(lambda y0=y0, l0=l0: s.activation(T.YO[:, y0 + 64:y0 + 128], T.OB[:, l0:l0 + 64], M.Identity, bias=-1.0),
+                    [], [("YO", c, 1)], 64, ["OB"])
                 vec(lambda y0=y0: v.tensor_tensor(T.YO[:, y0:y0 + 64], T.ZW[:], T.BB[:, 0:64], A.add), ["ZW"], [("YO", c, 0)], 64, ["BB"])
                 send(T.YI[:, y0:y0 + 128], [T.YO[:, y0:y0 + 128]], to_prev, "y%d" % c,
                      [("YO", c, 0), ("YO", c, 1)], [("YI", c)], more=500.0)
-                dma(T.yb[:, c * 64:(c + 1) * 64], T.YI[:, y0:y0 + 64], [("YI", c)], [], 32768, sem="outs")
-                dma(T.yo[:, c * 64:(c + 1) * 64], T.YI[:, y0 + 64:y0 + 128], [("YI", c)], [], 32768,
+                dma(T.yb[:, l0:l0 + 64], T.YI[:, y0:y0 + 64], [("YI", c)], [], 32768, sem="outs")
+                at("ys" if c == NCH - 1 else "y")
+                dma(T.yo[:, l0:l0 + 64], T.YI[:, y0 + 64:y0 + 128], [("YI", c)], [], 32768,
                     q="A" if c == NCH - 1 else "S", sem="outs")
         if t >= 2:
             e = t - 2
             srcs = [T.PK[:, t * 256:(t + 1) * 256]]
-            rd = [("PK", t, c) for c in range(NCH)]
+            rd = [("PK", t)]
             if t >= 3:
                 srcs.append(T.EIN[:, (e - 1) * 256:e * 256])
                 rd.append(("EIN", e - 1))
             if t >= 4:
                 srcs.append(T.PK[:, (t - 4) * 256:(t - 3) * 256])
-                rd += [("PK", t - 4, c) for c in range(NCH)]
-            send(T.EIN[:, e * 256:(e + 1) * 256], srcs, to_prev if last else to_next, "e%d" % e, rd, [("EIN", e)], more=1500.0,
-                 after=None if last else calls["m%d" % (NM if t == STEPS - 2 else t * NCH + NCH - 1)])
+                rd.append(("PK", t - 4))
+            at("e")
+            send(T.EIN[:, e * 256:(e + 1) * 256], srcs, to_prev if last else to_next, "e%d" % e, rd, [("EIN", e)], more=1500.0)
+    now[0] -= 2
     dma(T.ye[:], T.EIN[:, 768:1024], [("EIN", 3)], [], 65536, sem="outs")
     return ops
 
@@ -333,41 +448,49 @@ def link(ops):
             rd[k] = []
         d.pop(o["i"], None)
         o["deps"] = [(j, w and not (o["eng"] == "P" and ops[j]["eng"] == "P")) for j, w in d.items()]
-    for e in "AS":
-        seq = sorted((o["slot"], o["i"]) for o in ops if o.get("slot") is not None and o["eng"] == e)
-        for (_, i), (_, j) in zip(seq, seq[1:]):
-            if i not in [x for x, w in ops[j]["deps"]]:
-                ops[j]["deps"].append((i, False))
+    seq = sorted((o["slot"], o["i"]) for o in ops if o.get("slot") is not None)
+    for (_, i), (_, j) in zip(seq, seq[1:]):
+        if i not in [x for x, w in ops[j]["deps"]]:
+            ops[j]["deps"].append((i, False))
 
 
-def plan(ops, cost, order=None):
+def plan(ops, cost):
     n = len(ops)
     succ = [[] for _ in range(n)]
     for o in ops:
         for j, w in o["deps"]:
-            succ[j].append(o["i"])
+            succ[j].append((o["i"], w))
     tail = [0.0] * n
-    left = [len(o["deps"]) for o in ops]
-    topo_order = [i for i in range(n) if left[i] == 0]
-    for i in topo_order:
-        for j in succ[i]:
-            left[j] -= 1
-            if left[j] == 0:
-                topo_order.append(j)
-    assert len(topo_order) == n
-    for o in [ops[i] for i in reversed(topo_order)]:
+    for o in reversed(ops):
         x = o["dur"] + o["lat"] + (cost["dma0"] if o["kind"] == "dma" else 0.0)
-        tail[o["i"]] = max([tail[j] + (x + cost["hop"] if (o["i"], True) in ops[j]["deps"] or not ops[j]["eng"] else o["dur"])
-                            for j in succ[o["i"]]] + [x])
+        tail[o["i"]] = max([tail[j] + (x + cost["hop"] if w or not ops[j]["eng"] else o["dur"]) for j, w in succ[o["i"]]] + [x])
+    tau = cost["tau"]
     for o in ops:
-        k = (o["wr"] or o["rd"])[-1] if o["eng"] in ("V", "P") else None
-        tail[o["i"]] += cost["bias"].get(o["eng"] + (k[0] if isinstance(k, tuple) else k), 0.0) if k else 0.0
+        k = (o["eng"] or "") + (o["tag"] or "")
+        if cost.get("early") and (o["n"] is None or o["tag"] == "tab" or o["n"] < NCH and k + str(o["n"]) not in cost["early"]):
+            o["tau"] = None
+            tail[o["i"]] += cost["bias"].get(k, 0.0) + cost["bias"].get("%s%s" % (k, o["n"]), 0.0)
+        elif o["tag"] == "tab":
+            o["tau"] = tau["tab0"] + tau["tab1"] * o["n"]
+        elif o["n"] is None:
+            o["tau"] = tau.get(o["tag"])
+        elif o["n"] < NCH and o["tag"] in FRONT:
+            o["tau"] = tau["first0"] + tau["first1"] * o["n"] + tau.get(k, 0.0) + tau.get("first" + k, 0.0) + tau.get("late", 0.0) * (o["n"] >= tau.get("from", 9))
+        elif o["n"] < NCH:
+            o["tau"] = tau["back0"] + tau["back1"] * o["n"] + tau.get(k, 0.0)
+        elif o["n"] >= NM + NCH - 2 and o["tag"] not in FRONT:
+            o["tau"] = o["n"] + tau.get(k, 0.0) + tau.get("last" + k, 0.0)
+        else:
+            o["tau"] = o["n"] + tau.get(k, 0.0) + tau.get("o" + k, 0.0) * (o["n"] % 2)
+        if o["tau"] is not None:
+            o["tau"] += tau.get("%s%s" % (k, o["n"]), 0.0)
     left = [len(o["deps"]) for o in ops]
     done = [0.0] * n
     free = {}
     dmaq = [0.0]
     ready = [i for i in range(n) if left[i] == 0]
     out = []
+    heads = {}
 
     def est(i):
         o = ops[i]
@@ -377,14 +500,19 @@ def plan(ops, cost, order=None):
                 x = max(x, done[j] + (cost["hop"] if w else 0.0))
         return x
     while len(out) < n:
-        if order is not None:
-            i = order[len(out)]
-        else:
-            es = [(est(i), i) for i in ready]
+        es = [(est(i), i) for i in ready if ops[i]["tau"] is None]
+        if es:
             t0, i0 = min(es)
             e0 = ops[i0]["eng"]
             i = max([(tail[k], -k) for x, k in es if ops[k]["eng"] == e0 and x <= t0 + cost["look"]])[1] * -1
-            ready.remove(i)
+        else:
+            if not heads:
+                for x, k in sorted((o["tau"], o["i"]) for o in ops if o["tau"] is not None and o["eng"])[::-1]:
+                    heads.setdefault(ops[k]["eng"], []).append(k)
+            i = min([(est(k), k) for k in ready if not ops[k]["eng"] or heads[ops[k]["eng"]][-1] == k])[1]
+            if ops[i]["eng"]:
+                heads[ops[i]["eng"]].pop()
+        ready.remove(i)
         o = ops[i]
         st = est(i)
         if o["eng"]:
@@ -396,11 +524,10 @@ def plan(ops, cost, order=None):
             done[i] = st + o["dur"] + o["lat"]
         o["st"] = st
         out.append(i)
-        if order is None:
-            for j in succ[i]:
-                left[j] -= 1
-                if left[j] == 0:
-                    ready.append(j)
+        for j, w in succ[i]:
+            left[j] -= 1
+            if left[j] == 0:
+                ready.append(j)
     return out, max(done)
 
 

@@ -2,101 +2,263 @@ from concourse.bass import DstId, RemoteDMATransfer
 from concourse.mybir import AluOpType, ActivationFunctionType
 
 V, STEPS, NCH = 4096, 6, 4
-MS = 4128
 NM = (STEPS - 1) * NCH
+NF = STEPS - 1
+SIDE = 2
+PAIR = 1
+BIG = 12582912.0
 BF, F32, I32, U16, F16 = "bfloat16", "float32", "int32", "uint16", "float16"
 
 SCRATCH = {
-    "WP": ("sbuf", [128, V + 16], BF), "RLW": ("sbuf", [128, V + 32], BF), "TAB": ("sbuf", [128, 2 * MS], BF),
+    "WP": ("sbuf", [128, V + 16], BF), "RLW": ("sbuf", [128, V + 32], BF), "TAB": ("sbuf", [128, 2 * V + 32], BF),
     "RLI": ("sbuf", [128, 256], I32), "RLB": ("sbuf", [128, 256], BF), "RLL": ("sbuf", [128, 256], BF),
-    "CBI": ("sbuf", [128, 256], I32), "COI": ("sbuf", [128, 256], I32), "CB16": ("sbuf", [128, 256], U16),
+    "CBI": ("sbuf", [128, 256], I32), "COI": ("sbuf", [128, 256], I32), "L0": ("sbuf", [128, 256], U16),
+    "CY": ("sbuf", [128, 16, 32], F16), "CZ": ("sbuf", [128, 16, 32], F16), "CS": ("sbuf", [128, 16, 16], F16),
+    "OY": ("sbuf", [128, 16, 32], F16), "OZ": ("sbuf", [128, 16, 32], F16), "OS": ("sbuf", [128, 16, 16], F16),
     "COX": ("sbuf", [128, 520], BF),
     "DMI": ("sbuf", [128, 2, 16, 16], I32), "DMR": ("sbuf", [128, 16, 32], F16),
     "DMU": ("sbuf", [128, 16, 32], F16), "DMZ": ("sbuf", [128, 512], U16),
     "OMI": ("sbuf", [128, 512], I32), "OMB": ("sbuf", [128, 512], BF),
-    "PI": ("sbuf", [128, 128], F32), "PC": ("sbuf", [128, 4], I32), "PD": ("sbuf", [128, 4], I32),
-    "PF": ("sbuf", [128, 4], F32), "LO": ("sbuf", [128, 256], BF), "HI": ("sbuf", [128, 256], BF),
-    "ID": ("sbuf", [128, 128], BF), "IB": ("sbuf", [128, 16, 8], BF), "IF": ("sbuf", [128, 128], F32),
-    "IH": ("sbuf", [128, 128], F16), "IK": ("sbuf", [128, 128], BF), "IS": ("sbuf", [128, 128], BF),
-    "IM": ("sbuf", [128, 128], BF), "IP": ("sbuf", [128, 128], F16), "IN": ("sbuf", [128, 128], F16),
-    "ZR": ("sbuf", [128, 192], BF),
-    "ONE": ("sbuf", [128, 128], BF), "C16": ("sbuf", [128, 64], BF), "MASK": ("sbuf", [128, 1024], BF),
-    "FS": ("sbuf", [128, 64], BF), "THR": ("sbuf", [128, 4], F32),
-    "X0": ("sbuf", [128, 129, 8], F16), "X1": ("sbuf", [128, 129, 8], F16),
-    "XM0": ("sbuf", [128, 17, 8], BF), "XM1": ("sbuf", [128, 17, 8], BF),
-    "B": ("sbuf", [128, 256], F32),
-    "W0": ("sbuf", [128, V], BF), "W1": ("sbuf", [128, V], BF), "IND": ("sbuf", [128, V], BF), "SC": ("sbuf", [128, V], BF),
-    "GT": ("sbuf", [128, V], BF), "IDX": ("sbuf", [128, 256], U16),
+    "PI": ("sbuf", [128, 128], F32), "PC": ("sbuf", [128, 4], I32), "PD": ("sbuf", [128, 4], I32), "PG": ("sbuf", [128, 4], I32),
+    "PF": ("sbuf", [128, 4], F32), "MK": ("sbuf", [128, 4], F32), "LO": ("sbuf", [128, 256], BF), "HI": ("sbuf", [128, 256], BF),
+    "ID": ("sbuf", [128, 128], BF), "IB": ("sbuf", [128, 16, 8], BF), "IF": ("sbuf", [128, 128], F32), "IS": ("sbuf", [128, 128], BF),
+    "IH": ("sbuf", [128, 128], F16), "IN": ("sbuf", [128, 128], F16), "IP": ("sbuf", [128, 128], F16),
+    "ZR": ("sbuf", [128, 1024], BF), "SEL": ("sbuf", [128, 144], BF), "FS": ("sbuf", [128, 64], BF),
+    "TI": ("sbuf", [128, 256], F32), "MV": ("sbuf", [128, 256], F16), "MN": ("sbuf", [128, 256], F16), "MP": ("sbuf", [128, 256], F16),
+    "PA": ("sbuf", [128, 4, 32], BF), "PB": ("sbuf", [128, 4, 32], BF), "PO": ("sbuf", [128, 4, 32], BF),
+    "X0": ("sbuf", [128, 113, 8], F16), "X1": ("sbuf", [128, 113, 8], F16),
+    "IND": ("sbuf", [128, 2048], BF), "GT": ("sbuf", [128, 2048], BF), "TR": ("sbuf", [128, 2048], BF),
+    "B": ("sbuf", [128, 256], F32), "IDX": ("sbuf", [128, 256], U16),
     "MSG": ("sbuf", [128, NM * 64], U16), "OUT": ("sbuf", [128, NM * 64], U16),
-    "OIN": ("sbuf", [128, STEPS * 256], BF), "OOUT": ("sbuf", [128, NM * 64], BF),
-    "PK": ("sbuf", [128, STEPS * 256], BF), "EIN": ("sbuf", [128, 4 * 256], BF),
-    "ZW": ("sbuf", [128, 64], F32), "YO": ("sbuf", [128, NCH * 128], F32), "YI": ("sbuf", [128, NCH * 128], F32),
-    "R0": ("psum", [128, 512], F32), "R1": ("psum", [128, 512], F32),
-    "VB": ("psum", [128, 512], F32), "JB": ("psum", [128, 512], F32), "F0": ("psum", [128, 512], F32),
-    "F1": ("psum", [128, 512], F32), "BB": ("psum", [128, 512], F32), "OB": ("psum", [128, 512], F32),
+    "OIN": ("sbuf", [128, STEPS * NCH * 64], BF), "OOUT": ("sbuf", [128, NM * 64], BF),
+    "PK": ("sbuf", [128, 256], BF), "EIN": ("sbuf", [128, 2560], BF), "HE": ("sbuf", [128, 2432], BF), "YE": ("sbuf", [128, 1024], BF),
+    "ZB": ("sbuf", [128, 4, 32], F32), "ZO": ("sbuf", [128, 4, 32], F32), "YN": ("sbuf", [128, 128], I32),
+    "YO": ("sbuf", [128, 512], F32), "YI": ("sbuf", [128, 512], F32),
+    "JB0": ("psum", [128, 512], F32), "JB1": ("psum", [128, 512], F32), "BB0": ("psum", [128, 512], F32), "BB1": ("psum", [128, 512], F32),
+    "F0": ("psum", [128, 512], F32), "F1": ("psum", [128, 512], F32), "OB0": ("psum", [128, 512], F32), "OB1": ("psum", [128, 512], F32),
 }
-SEMAPHORES = (["cA", "cV", "cP", "cG", "sent", "outs", "a_rl"] + ["d%d" % i for i in range(32)]
-              + ["m%d" % n for n in range(NM)] + ["o%d" % n for n in range(NM)]
-              + ["y%d" % c for c in range(NCH)] + ["e%d" % i for i in range(4)])
+SCRATCH.update({"W%d" % t: ("sbuf", [128, V], BF) for t in range(STEPS)})
+SEMAPHORES = (["cA", "cV", "cP", "cG", "sent", "outs", "a_rl"] + ["d%d" % i for i in range(36)]
+              + ["m%d" % n for n in range(NM)] + ["o%d" % n for n in range(NM)] + ["y%d" % c for c in range(NCH)]
+              + ["e%d" % t for t in range(STEPS + 1)] + ["f%d" % t for t in range(STEPS)]
+              + ["g%d" % t for t in range(1, NF)] + ["b%d" % t for t in range(1, NF)])
 
-FRONT = ("w0", "w1", "w2", "d0", "d1", "c0", "c1", "fix", "sc", "vote", "jb", "mb", "jm", "idx")
+COST = dict(r=1.4, f=1.0, ov=5.0, ova=30.0, pe=0.63, hop=70.0, lat=3300.0, first=2000.0, call=700.0, dma0=2000.0, dmab=0.0045,
+            fold=11000.0, loads="wdo|c", wa=10, ga=64, ooa=0, sv=0, zc=1, ne=2, jl=0, hr=0, cv=0, og=1, vs=4, rsa=(), cx={},
+            vx={0: 16, 1: 16, 2: 16, 3: 16, 23: 16}, wx={0: 8, 1: 16, 2: 16, 3: 16, 20: 12, 21: 12, 22: 14, 23: 8},
+            gx={0: 32, 1: 40, 23: 32}, ta="AVAVAVAV")
+COST.update(wa=9, vs=3, vx={0: 16, 1: 16, 2: 16, 3: 16, 20: 16, 21: 16, 22: 16, 23: 16}, wx={0: 8, 1: 16, 2: 16, 3: 16, 20: 12, 21: 13, 22: 13, 23: 11},
+            gx={0: 32, 1: 40, 23: 40}, rsa=(20, 21))
+ORDER = dict(turns=(5, 20), queues=dict(
+    A=('setup mat fs late w0 w1 w2 tab.2 tw tab w3 co gt0 gt1 gt2 w4 gt3',
+       'w0 gt-1',
+       'w20 gt19 w21 gt20 w22 gt21 rs20 w23 gt22 rs21 gt23 y23'),
+    V=('setup mat rl cb fs x b1 late w0 dm.4 b0 dm.1 om.1 dm.5 c0.1 dm.2 cw0 om.1 dm.3 om.1 dm.2 om dm c0 cw1 tab co.2 idx0 b2 co.1 cw2 co c1 c2.1 gt0 c2 th0 h0 rs0 idx1 cw3 out0 b3 gt1 idx2 c3.1 th1 pp0 h1 c3 out1 pp1 idx3 oo0 rs1 th2 h2 rs2 pp2 out2 w4 wb4 b4 c4.1 oo1 cw4 c4',
+       'oo-3 wb0 th-2 h-2 b0 idx-1 pp-2 rs-2 out-2 w0 cw0 c0',
+       'oo17 w20 th18 h18 b20 idx19 rs18 out18 pp18 cw20 c20 oo18 w21 th19 h19 b21 idx20 pp19 out19 rs19 c21.1 cw21 oo19 c21 w22 b22 h20 th20 pp20 idx21 c22.1 cw22 c22 tree22.1 b23 y20.1 tree22.1 y20.1 w23 h21 th21 idx22 pp21 y20.1 c23.1 cw23 c23 y20.1 y21.1 tree23.1 y21.1 y20 idx23 th22 h22 gt23 pp22 y21.1 rs22 tree22.1 y21.1 y22.1 y21 th23 y22.1 tree23.1 h23 y22 rs23 tree22 pp23 tree23.1 y23.1 tree23 y23 em23 ef23'),
+    P=('jb0 jb1 vote0 jb2 co vote1 vote2.1 oa0 f0 oa1 bb0 vote2 os0 f1 jb3 vote3.1 bb1 oa2 ob0 vote3 f2 os1 bb2 os2 oa3 ob2 ob1 jb4 vote4.1 f3 vote4',
+       'bb-2 oa-1 os-2 ob-2 jb0 vote0.1 f-1 vote0',
+       'bb18 os18 ob18 jb20 oa19 vote20.1 f19 vote20 bb19 jb21 os19 oa20 ym20 ob19 vote21.1 f20 vote21 bb20.1 oa21 jb22 vote22.1 bb20 vote22 ob20.1 f21 ym21.1 ob20 ym21 oa22 bb21.1 ym22.1 bb21 jb23 vote23 ym23.1 f22 ob21 bb22.1 ym22 bb22 oa23 f23 ob22 ym23 bb23 ob23'),
+    G=('setup late rl fold3 out0 out1 oo0 out2 oo1',
+       'oo-3 out-2 fold0 side-1',
+       'oo17 out18 side19 out19 oo18 oo19 fold21 y20 y21 y22 e23 y23')))
+COST.update(og=2)
+ORDER = dict(turns=(5, 20), queues=dict(
+    A=('setup mat fs late w0 w2 w1 tab.3 tw tab w3 co gt0 gt1 gt2 w4 gt3',
+       'w0 gt-1',
+       'w20 gt19 w21 gt20 w22 rs20 gt21 w23 gt22 rs21 gt23 y23'),
+    V=('setup mat rl cb fs x late b0 w0 dm.4 b1 dm.1 om.1 dm.4 om.1 dm.6 c0.1 dm.2 om.1 dm.2 cw0 om dm.1 c0 dm c1.1 tab co.2 cw1 co.1 cw2 co b2 idx0 c2.1 c1 gt0 b3 c2 th0 h0 cw3 idx1 out0 rs0 gt1 pp0 idx2 h1 th1 c3.1 out1 c3 pp1 rs1 h2 th2 pp2 oo0 idx3 oo1 w4 out2 wb4 b4 rs2 cw4 c4 oo2',
+       'wb0 th-2 h-2 b0 idx-1 pp-2 rs-2 out-2 w0 cw0 c0.1 oo-2 c0',
+       'h18 th18 w20 b20 idx19 out18 cw20 pp18 c20.1 rs18 c20 oo18 w21 b21 th19 rs19 h19 idx20 pp19 cw21 out19 c21 oo19 th20 h20 w22 b22 pp20 idx21 c22.1 cw22 c22 y20.1 tree22.1 y20.1 b23 idx22 w23 th21 h21 y20.1 tree22.1 y20.1 cw23 c23 y21.1 y20 pp21 y21.1 idx23 tree23.1 th22 h22 gt23 y21.1 rs22 y21 pp22 y22.1 tree23.1 y22 th23 rs23 tree23.1 h23 tree22.1 tree23 pp23 tree22 y23 em23 ef23'),
+    P=('jb0 jb1 vote0 vote1.1 jb2 co vote2.1 vote1 oa0 f0 oa1 bb0 vote2 os0 jb3 f1 ob0 oa2 bb1 os1 f2 vote3 ob1 bb2 os2 ob2 jb4 oa3 vote4.1 f3 vote4',
+       'bb-2 os-2 jb0 ob-2 oa-1 vote0.1 f-1 vote0',
+       'bb18 oa19 os18 jb20 vote20.1 ob18 f19 vote20 os19 bb19 ob19 oa20 ym20.1 jb21 f20 ym20 vote21 jb22 bb20 oa21 vote22 ob20.1 f21 ob20 jb23 ym21.1 bb21.1 oa22 bb21 vote23.1 ym22 vote23 ym21 f22 ob21.1 oa23 ob21 bb22 ob22 f23 ym23 bb23.1 ob23.1 bb23 ob23'),
+    G=('setup late rl fold3 out0 out1 oo1 out2',
+       'out-2 fold-1 oo-2',
+       'out18 fold19 out19 oo19 fold21 y20 y21 y22 e23 y23')))
+COST["wx"].update({20: 13, 21: 14, 22: 14, 23: 12})
+COST["rsa"] = (20, 21, 22)
+ORDER = dict(turns=(5, 20), queues=dict(
+    A=('setup mat fs late w0 w1 w2 tab.3 tw tab w3 co gt0 gt1 gt2 w4 gt3',
+       'w0 gt-1',
+       'w20 gt19 w21 gt20 w22 rs20 gt21 w23 gt22 rs21 gt23 rs22 y23'),
+    V=('setup mat rl cb fs x late w0 dm.4 b2 b0 dm.1 om.1 dm.2 b1 dm.3 c0.1 dm.7 om.1 dm.3 cw0 om cw1 dm c0 tab co.3 idx0 co c1.1 c2.1 c1 gt0 c2 th0 h0 idx1 cw2 pp0 out0 b3 gt1 rs0 idx2 c3.1 cw3 th1 h1 c3 pp1 out1 rs1 oo1 oo0 h2 rs2 pp2 th2 w4 b4 idx3 out2 wb4 cw4 c4.1 oo2 c4',
+       'wb0 th-2 h-2 b0 idx-1 pp-2 rs-2 out-2 w0 cw0 c0.1 oo-2 c0',
+       'b20 h18 th18 pp18 w20 idx19 out18 c20.1 rs18 cw20 c20 tree20.1 b21 th19 tree20.1 h19 idx20 w21 pp19 out19 rs19 cw21 tree20.1 c21 tree21.1 oo18 oo19 tree21.1 tree20 w22 h20 th20 idx21 b22 tree21.1 pp20 c22.1 cw22 c22 y20.1 tree21 tree22.1 idx22 b23 tree22.1 th21 w23 y20.1 h21 c23.1 cw23 pp21 y20.1 c23 tree23.1 y20.1 idx23 y20.1 gt23 h22 th22 y21.1 pp22 y20 y21.2 tree23.1 y22.1 y21 y22.1 tree23.1 y22.2 th23 rs23 y22 h23 tree22.1 pp23 tree22 y23.1 tree23 y23 em23 ef23'),
+    P=('jb1 jb0 vote0 co jb2 vote1.1 oa0 vote1 f0 oa1 bb0 vote2 os0 f1 oa2 bb1 jb3 os1 ob1 ob0 f2 vote3 bb2 os2 ob2 jb4 oa3 vote4.1 f3 vote4',
+       'bb-2 os-2 jb0 ob-2 oa-1 vote0.1 f-1 vote0',
+       'bb18 jb20 oa19 os18 vote20.1 f19 vote20 bb19 ob18 ym20.1 os19 jb21 ob19 vote21.1 oa20 vote21 f20 ym20 bb20 jb22 oa21 vote22.1 ob20.1 vote22 f21 ym21.1 ob20 ym21 bb21 jb23 ym22.1 vote23.1 oa22 ym22 vote23 f22 ob21.1 oa23 ob21 bb22 ob22 f23 ym23 bb23.1 ob23.1 bb23 ob23'),
+    G=('setup late rl fold3 out0 out1 oo1 out2',
+       'out-2 fold0 oo-2',
+       'out18 out19 oo19 y20 y21 y22 e23 y23')))
+COST["wx"].update({20: 12, 21: 13, 22: 13, 23: 11})
+COST["rsa"] = (20, 21)
+ORDER = dict(turns=(5, 20), queues=dict(
+    A=('setup mat fs late w0 w2 w1 tab.3 tw tab w3 co gt0 gt1 gt2 w4 gt3',
+       'w0 gt-1',
+       'w20 gt19 w21 gt20 w22 rs20 gt21 w23 gt22 rs21 gt23 y23'),
+    V=('setup mat rl cb fs x late b0 w0 dm.4 b1 dm.1 om.1 dm.4 om.1 dm.6 c0.1 dm.2 om.1 dm.2 cw0 om dm.1 c0 dm c1.1 tab co.2 cw1 co.1 cw2 co b2 idx0 c2.1 c1 gt0 b3 c2 th0 h0 cw3 idx1 out0 rs0 gt1 pp0 idx2 h1 th1 c3.1 out1 c3 pp1 rs1 h2 th2 pp2 oo0 idx3 oo1 w4 out2 wb4 b4 rs2 cw4 c4 oo2',
+       'wb0 th-2 h-2 b0 idx-1 pp-2 rs-2 out-2 w0 cw0 c0.1 oo-2 c0',
+       'h18 th18 w20 b20 idx19 out18 cw20 pp18 c20.1 rs18 c20 oo18 w21 b21 th19 rs19 h19 idx20 pp19 cw21 out19 c21 oo19 th20 h20 w22 b22 pp20 idx21 c22.1 cw22 c22 y20.1 tree22.1 y20.1 b23 idx22 w23 th21 h21 y20.1 tree22.1 y20.1 cw23 c23 y21.1 y20 pp21 y21.1 idx23 tree23.1 th22 h22 gt23 y21.1 rs22 y21 pp22 y22.1 tree23.1 y22 th23 rs23 tree23.1 h23 tree22.1 tree23 pp23 tree22 y23 em23 ef23'),
+    P=('jb0 jb1 vote0 vote1.1 jb2 co vote2.1 vote1 oa0 f0 oa1 bb0 vote2 os0 jb3 f1 ob0 oa2 bb1 os1 f2 vote3 ob1 bb2 os2 ob2 jb4 oa3 vote4.1 f3 vote4',
+       'bb-2 os-2 jb0 ob-2 oa-1 vote0.1 f-1 vote0',
+       'bb18 oa19 os18 jb20 vote20.1 ob18 f19 vote20 os19 bb19 ob19 oa20 ym20.1 jb21 f20 ym20 vote21 jb22 bb20 oa21 vote22 ob20.1 f21 ob20 jb23 ym21.1 bb21.1 oa22 bb21 vote23.1 ym22 vote23 ym21 f22 ob21.1 oa23 ob21 bb22 ob22 f23 ym23 bb23.1 ob23.1 bb23 ob23'),
+    G=('setup late rl out0 fold3 out1 oo1 out2',
+       'out-2 fold0 side-1 oo-2',
+       'out18 side19 out19 oo19 fold21 y20 y21 y22 e23 y23')))
+COST["rsa"] = ()
+ORDER = dict(turns=(5, 20), queues=dict(
+    A=('setup w0 w1 w2 tab.1 tw tab w3 gt0 gt1 gt2 w4 gt3',
+       'w0 gt-1',
+       'w20 gt19 w21 gt20 w22 gt21 w23 gt22 gt23 y23'),
+    V=('mat.1 setup.2 mat.1 x.1 mat.2 setup.2 fs.3 setup.2 fs.1 rl late.1 fs.1 cb.2 mat.1 fs.1 mat.1 cb.1 late.1 setup cb.1 late.2 cb.2 late.1 cb.1 late.1 cb late x mat.1 b1 mat b0 fs b2 w0 dm.1 c0.1 dm.3 cw0 om.1 dm.1 c0 dm.2 om.1 dm.1 om.1 dm.7 om dm c1.1 tab co.2 cw1 cw2 idx0 co.1 c2.1 co.4 c1 b3 co gt0 c2 th0 h0 cw3 idx1 out0 pp0 gt1 rs0 idx2 th1 h1 c3.1 out1 c3 pp1 rs1 oo0 th2 h2 rs2 oo1 out2 w4 idx3 b4 wb4 pp2 cw4 c4.1 oo2 c4',
+       'wb0 th-2 h-2 b0 idx-1 pp-2 rs-2 out-2 w0 cw0 c0.1 oo-2 c0',
+       'th18 h18 w20 idx19 out18 pp18 b20 rs18 cw20 c20 th19 h19 rs19 pp19 idx20 out19 b21 oo18 w21 oo19 cw21 c21 b22 w22 rs20 h20 th20 idx21 pp20 c22 cw22 tree22.1 y20.1 b23 w23 h21 y20.1 th21 rs21 idx22 y20.1 cw23 c23 tree23.1 y21.1 y20.2 pp21 idx23 y20 y21.1 th22 rs22 h22 gt23 pp22 y21.1 tree22.1 y21 y22.1 tree23.1 y22.2 th23 y22.1 rs23 y22 h23 tree23.1 tree22.1 pp23 tree22 tree23 y23 em23 ef23'),
+    P=('jb0 jb1 vote0 vote1.1 jb2 co vote2.1 vote1 oa0 f0 bb0 os0 vote2 oa1 f1 oa2 bb1.1 jb3 bb1 os1 ob0 vote3.1 f2 ob1 bb2 vote3 os2 oa3 jb4 ob2 vote4.1 f3 vote4',
+       'bb-2 os-2 jb0 ob-2 oa-1 vote0.1 f-1 vote0',
+       'bb18 os18 oa19 jb20 ob18 vote20.1 f19 vote20 ym20.1 bb19 os19 ob19 ym21.1 oa20 ym20 jb21 ym21 vote21.1 f20 vote21 ob20.1 jb22 ob20 oa21 bb20 vote22.1 f21 vote22 jb23 ym22.1 bb21.1 oa22 ym22 bb21 vote23.1 ob21.1 vote23 f22 ob21 ob22.1 oa23 bb22 ob22 f23 ym23 bb23.1 ob23.1 bb23 ob23'),
+    G=('setup late rl out0 fold3 out1 oo1 out2',
+       'out-2 fold0 side-1 oo-2',
+       'out18 side19 out19 oo19 fold21 y20 y21 y22 e23 y23')))
+COST.update(wa=8, vs=4, wx={0: 8, 1: 16, 2: 14, 3: 10, 20: 9, 21: 10, 22: 12, 23: 10}, gx={0: 32, 1: 36, 2: 48, 23: 32})
+ORDER = dict(turns=(5, 20), queues=dict(
+    A=('setup w0 w1 w2 tw tab w3 gt0 gt1 gt2 w4 gt3',
+       'w0 gt-1',
+       'w20 gt19 w21 gt20 w22 gt21 w23 gt22 gt23 y23'),
+    V=('setup.1 mat.1 setup.1 mat.1 setup.1 x.1 mat.3 fs.1 mat.1 setup.2 late.1 setup.1 rl cb.2 mat.1 cb.2 late.1 fs.1 cb.1 fs.1 cb.2 fs.3 cb late.1 fs b1 setup b2 late.2 x mat b0 w0 dm.4 c0.1 dm.1 om.1 dm.6 w2 dm.1 b3 om.1 dm.1 late.1 dm.2 late dm.2 cw0 c0 dm c1.1 om.1 tab.3 om tab co.2 idx0 cw2 co.1 cw1 co.4 c2.1 c1 co gt0 idx1 c2 th0 h0 w3 out0 gt1 c3.1 idx2 rs0 pp0 rs1 th1 h1 cw3 c3 out1 pp1 gt2 th2 h2 oo1 rs2 oo0 out2 w4 b4 idx3 wb4 cw4 pp2 c4.1 oo2 c4',
+       'wb0 th-2 h-2 b0 idx-1 pp-2 rs-2 out-2 w0 cw0 c0.1 oo-2 c0',
+       'w20 th18 h18 b20 idx19 rs18 out18 cw20 c20 pp18 idx20 rs19 th19 h19 pp19 out19 oo18 w21 oo19 cw21 b21 c21 w22 b22 h20 rs20 th20 pp20 idx21 tree22.1 c22 cw22 y20.1 w23 rs21 th21 h21 y20.1 b23 y20.1 idx22 y20.1 c23.1 cw23 c23 pp21 y20.1 tree23.1 y21.1 tree22.1 y20 y21.1 h22 rs22 th22 pp22 idx23 y21.1 gt23 y21.1 y22.1 y21 y22.3 th23 y22 rs23 h23 tree23.1 tree22.1 tree23.1 pp23 tree23 tree22 y23 em23 ef23'),
+    P=('jb0 jb1 vote0 vote1.1 co.2 jb2 co vote1 vote2.1 oa0 f0 bb0 oa1 vote2 os0 f1 oa2 bb1 os1 ob1 jb3 f2 ob0 bb2 vote3 oa3 jb4 os2 ob2 vote4.1 f3 vote4',
+       'bb-2 os-2 jb0 ob-2 oa-1 vote0.1 f-1 vote0',
+       'bb18 jb20 os18 oa19 vote20 f19 ob18 ym20.1 bb19 os19 ob19 ym20 oa21 jb21 oa20 vote21.1 ym21.1 f20 vote21 ym21 ob20.1 bb20.1 ob20 jb22 bb20 f21 vote22 oa22 bb21 jb23 ym22.1 vote23.1 ob21 ym22 f22 vote23 oa23 bb22 ob22 f23 ym23 bb23.1 ob23.1 bb23 ob23'),
+    G=('setup late rl out0 fold3 out1 oo1 out2',
+       'out-2 fold0 side-1 oo-2',
+       'out18 side19 out19 oo19 fold21 y20 y21 y22 e23 y23')))
+COST.update(wa=10, vs=3, og=2, ta="AVAVAVAA", wx={0: 9, 1: 16, 2: 16, 3: 16, 20: 13, 21: 14, 22: 15, 23: 12}, gx={0: 32, 1: 44, 23: 44})
+ORDER = dict(turns=(5, 20), queues=dict(
+    A=('setup w0 w1 w2 tab.2 tw tab w3 gt0 gt1 gt2 gt3 w4',
+       'w0 gt-1',
+       'w20 gt19 w21 gt20 w22 gt21 w23 gt22 gt23 y23'),
+    V=('setup.1 mat.1 setup.1 mat.3 x.1 setup.1 late.1 setup.1 rl setup.2 fs.2 cb.2 mat.1 cb.1 mat.1 cb.1 mat.1 late.2 setup fs.1 cb.2 fs.1 late.1 cb x b0 late.2 mat b2 fs.1 late b1 dm.1 w0 dm.3 fs.1 c0.1 fs dm.1 cw0 dm.4 b3 dm om.1 cw1 om.1 c1.1 tab.1 co.1 c0 om.1 co.1 tab.1 c1 om idx0 tab co.1 cw2 co.2 idx1 co.2 c2 co gt0 c3.1 th0 h0 idx2 cw3 pp0 out0 gt1 rs0 c3 h1 th1 rs1 out1 oo0 idx3 pp1 th2 h2 pp2 oo1 rs2 out2 w4 wb4 b4 oo2 c4.1 cw4 c4',
+       'wb0 th-2 h-2 b0 idx-1 pp-2 out-2 w0 rs-2 cw0 c0 oo-2',
+       'w20 th18 h18 b20 idx19 out18 rs18 cw20 c20.1 pp18 c20 b21 th19 h19 w21 oo18 idx20 out19 rs19 cw21 pp19 c21.1 oo19 c21 b22 h20 w22 rs20 pp20 th20 idx21 tree22.1 c22.1 tree22.1 c22 y20.1 cw22 w23 y20.2 b23 h21 th21 idx22 y20.1 tree22.1 cw23 rs21 tree23.1 c23.1 y20.1 c23 y21.1 y20 pp21 rs22 y21.1 h22 th22 idx23 pp22 gt23 tree23.1 y21.2 y22.1 y21 y22.3 th23 h23 y22 rs23 pp23 tree23.1 y23.1 tree22 tree23 y23 em23 ef23'),
+    P=('jb0 vote0.1 jb1 vote0 jb2 vote1 co.2 jb3 co vote2 oa0 oa1 f0 bb0 vote3.1 os0 f1 ob0 oa2 bb1 vote3 os1 f2 os2 bb2.1 ob1 bb2 oa3 ob2 jb4 f3 vote4',
+       'bb-2 os-2 jb0 ob-2 oa-1 vote0.1 f-1 vote0',
+       'bb18 jb20 ym20.1 oa19 os18 ob18 f19 vote20 bb19 jb21 os19 ym20 ob19 oa20 oa21 f20 vote21 ym21.1 ob20.1 bb20.1 ym21 ob20 bb20 jb22 f21 ym22.1 vote22 oa22 bb21 jb23 ob21.1 vote23.1 f22 ym22 vote23 oa23 ob21 bb22 ob22 f23 ym23 bb23 ob23'),
+    G=('setup rl late out0 fold3 out1 oo1 out2',
+       'oo-3 out-2 fold0 side-1',
+       'oo17 out18 side19 out19 oo19 fold21 y20 y21 y22 e23 y23')))
+COST.update(wa=9, vs=4, ta="AVAVAVAV", wx={0: 8, 1: 16, 2: 16, 3: 16, 20: 12, 21: 13, 22: 14, 23: 11}, gx={0: 32, 1: 40, 23: 40})
+ORDER = dict(turns=(5, 20), queues=dict(
+    A=('setup w0 w1 w2 tab.1 tw tab w3 gt0 gt1 gt2 gt3 w4',
+       'w0 gt-1',
+       'w20 gt19 w21 gt20 w22 gt21 w23 gt22 gt23 y23'),
+    V=('late.1 mat.1 setup.1 mat.1 setup.2 mat.2 setup.2 mat.1 x.1 rl fs.1 x cb.2 fs.1 mat.1 fs.1 cb.1 mat.1 setup.1 mat cb.1 setup late.2 fs.1 late.1 cb fs.2 b0 b3 b1 late.1 b2 late.1 w0 dm.3 c0.1 dm.1 c0 cw0 om.1 dm.1 om.2 dm.3 c1.1 dm.1 idx0 dm om c1 tab co.2 cw1 fs co.1 c2.1 co.4 cw2 c2 idx1 co gt0 c3.1 th0 h0 late pp0 cw3 rs0 out0 idx2 gt1 c3 th1 h1 oo0 rs1 out1 pp1 idx3 th2 h2 oo1 rs2 pp2 out2 oo2 wb4 w4 b4 cw4 c4',
+       'b0 th-2 h-2 wb0 idx-1 out-2 w0 pp-2 rs-2 cw0 c0.1 oo-2 c0',
+       'b20 h18 th18 w20 idx19 out18 c20.1 rs18 pp18 cw20 c20 b21 oo18 th19 h19 w21 idx20 rs19 pp19 out19 c21.1 oo19 cw21 c21 w22 th20 h20 idx21 b22 rs20 pp20 y20.1 tree22.1 y20.1 cw22 c22.1 y20.1 c22 w23 b23 th21 tree22.1 h21 rs21 y20.1 idx22 pp21 cw23 tree23.1 c23.1 y21.1 c23 y20.1 tree23.1 y20 y21.2 th22 rs22 h22 idx23 y21.1 pp22 gt23 y22.1 y21 y22.4 th23 h23 y22 pp23 rs23 tree22.1 tree23 tree22 y23 em23 ef23'),
+    P=('jb1 jb0 vote0 vote1.1 jb2 vote1 co vote2.1 jb3 oa1 oa0 f0 vote2 bb0 os0 ob0 vote3.1 f1 oa2 bb1 vote3 os1 f2 ob1 os2 bb2.1 ob2 bb2 oa3 f3 jb4 vote4',
+       'bb-2 jb0 os-2 oa-1 ob-2 vote0.1 f-1 vote0',
+       'bb18 jb20 ym20.1 oa19 os18 ob18 vote20.1 f19 vote20 bb19.1 jb21 bb19 os19 ym20 ym21.1 ob19 oa20 vote21.1 oa21 f20 vote21 bb20 ob20 ym21 jb22 ym22.1 vote22.1 f21 oa22 vote22 bb21 ob21.1 jb23 ob21 vote23.1 oa23 ym22 f22 vote23 bb22 ob22.1 ym23.1 ob22 f23 ym23 bb23 ob23'),
+    G=('late.1 setup rl late out0 fold3 out1 oo1 out2',
+       'out-2 fold0 oo-2 side-1',
+       'out18 side19 out19 oo19 fold21 y20 y21 y22 e23 y23')))
+COST.update(wa=12, vs=16, ga=52, ne=3, sv=1, ta="AVAVAVAV", vx={}, wx={0: 8, 1: 16, 2: 16, 3: 16, 4: 10, 20: 13, 21: 13, 22: 14, 23: 11},
+            gx={0: 32, 1: 40, 2: 64, 3: 64, 20: 64, 21: 64, 22: 64, 23: 40})
+ORDER = dict(turns=(5, 20), queues=dict(
+    A=('setup w0 w1 w2 tw tab w3 gt0 gt1 gt2 gt3 w4',
+       'w0 gt-1',
+       'w20 gt19 w21 gt20 w22 gt21 w23 gt22 gt23 y23'),
+    V=('mat.1 setup.1 mat.1 late.1 mat.1 x.1 mat.1 setup.2 fs.1 setup.1 mat.2 rl mat.1 cb.1 setup.1 cb.1 setup.1 fs.1 x cb.1 late.1 fs.1 cb.1 late.1 fs.1 late.1 cb.2 late.1 setup cb.1 fs.1 cb mat late.1 b2 b0 b1 b3 fs.1 w0 dm.3 c0.1 dm.1 c0.1 dm.1 c0 cw0 dm.2 om.2 cw1 om.1 dm.1 om dm idx0 c1.2 tab co.2 cw2 co.1 c1 co.4 c2.1 fs c2.1 co idx1 gt0 c2 c3.1 th0 h0 cw3 idx2 pp0 rs0 out0 gt1 c3 oo0 th1 h1 rs1 out1 pp1 idx3 late h2 th2 oo1 rs2 pp2 b4 oo2 out2 w4 c4.1 cw4 c4',
+       'w0 th-2 h-2 b0 rs-2 idx-1 pp-2 out-2 c0.1 cw0 c0.1 gt-1 c0 oo-2',
+       'w20 h18 th18 rs18 pp18 idx19 out18 b20 cw20 c20.1 oo18 c20.1 gt19 c20 w21 b21 h19 th19 idx20 pp19 rs19 out19 c21.1 oo19 cw21 c21 w22 b22 th20 h20 rs20 idx21 pp20 cw22 c22 tree22.1 y20.1 w23 y20.1 idx22 rs21 tree22.1 th21 y20.1 h21 b23 cw23 pp21 tree23.1 c23.1 y20.2 c23.1 y20 y21.1 c23 y21.2 tree23.1 rs22 th22 h22 idx23 y21.1 pp22 gt23 y21.1 tree22.1 y22.1 tree22 y21 y22.3 th23 h23 y22 pp23 rs23 tree23.1 y23.1 tree23 y23 em23 ef23'),
+    P=('jb0 jb1 vote0 jb2 vote1 co vote2.2 oa0 jb3 oa1 f0 vote2 bb0 vote3.1 ob0 oa2 f1 vote3.1 bb1 vote3 f2 ob1 bb2.1 ob2 bb2 jb4 oa3 f3 vote4',
+       'bb-2 jb0 ob-2 oa-1 vote0.2 f-1 vote0',
+       'bb18 ob18 ym20.1 oa19 jb20 vote20.2 f19 vote20 jb21 bb19 ob19 ym20 ym21.1 oa20 oa21 vote21.1 f20 vote21 jb22 ym21 bb20.1 ob20.1 bb20 ob20 vote22.2 ym22.1 vote22 f21 oa22 ob21.1 bb21 oa23 ym22 jb23 ob21 vote23.1 f22 vote23 ob22.1 bb22 ob22 f23 ym23 bb23 ob23'),
+    G=('late.1 setup rl late out0 fold3 out1 oo1 out2',
+       'out-2 fold0 oo-2 side-1',
+       'out18 side19 out19 oo19 fold21 y20 y21 y22 e23 y23')))
+ORDER = dict(turns=(5, 20), queues=dict(
+    A=('setup w0 w1 w2 tab.2 tw tab w3 gt0 gt1 gt2 gt3 w4',
+       'w0 gt-1',
+       'w20 gt19 w21 gt20 w22 gt21 w23 gt22 gt23 y23'),
+    V=('setup.1 mat.2 x.1 mat.1 setup.1 mat.1 late.1 setup.1 mat.3 setup.1 rl setup.1 cb.1 cb.1 fs.1 setup.1 cb.1 fs.1 x fs.1 cb.1 late.1 late.1 late.2 cb.1 fs.1 mat cb.1 fs.1 late.1 cb.1 fs.1 cb setup fs b0 b2 b1 b3 w0 dm.1 c0.1 dm.2 om.1 c0.1 om.1 dm.1 c0 dm.1 om dm.2 c1.1 dm.1 cw0 dm.3 c1.1 cw1 dm c1 tab.2 idx0 tab co.2 idx1 co.1 cw2 co.4 c2 co gt0 gt1 h0 th0 cw3 idx2 out0 c3.1 rs0 pp0 h1 th1 c3 out1 rs1 oo0 idx3 late pp1 h2 th2 oo1 pp2 out2 rs2 oo2 b4 w4 c4.1 cw4 c4',
+       'w0 h-2 b0 th-2 rs-2 idx-1 pp-2 out-2 c0.1 cw0 c0.1 gt-1 c0 oo-2',
+       'b20 w20 h18 pp18 th18 idx19 cw20 out18 rs18 c20.1 gt19 c20 oo18 w21 b21 h19 rs19 idx20 th19 pp19 cw21 out19 c21.2 oo19 w22 c21 b22 h20 rs20 th20 idx21 pp20 c22.1 cw22 c22 tree22.1 y20.1 w23 y20.2 rs21 h21 idx22 tree22.1 th21 pp21 c23.1 b23 y20.1 tree23.1 cw23 y21.1 c23 y20.1 y21.1 tree23.1 y21.1 rs22 h22 idx23 y20 pp22 tree22.1 th22 y21.1 gt23 y21 y22.1 tree22 y22.2 h23 rs23 th23 y22 pp23 tree23.1 y23.2 tree23 y23 em23 ef23'),
+    P=('jb0 vote0.2 jb1 vote0 jb2 vote1 co vote2.2 oa0 jb3 f0 vote2 bb0 oa1 f1 vote3.1 bb1 ob0 vote3 oa2 f2 ob1 bb2 ob2 oa3 jb4 f3 vote4',
+       'bb-2 jb0 ob-2 oa-1 vote0.2 f-1 vote0',
+       'jb20 bb18 oa19 ob18 ym20.1 vote20.1 f19 vote20 jb21 bb19 ob19 oa20 ym20 oa21 vote21.1 f20 vote21 jb22 ym21.1 ob20.1 bb20.1 ym21 ob20 bb20 vote22 f21 ym22.1 oa22 ob21.1 bb21 oa23 ob21 jb23 vote23.1 f22 vote23 ym22 bb22.1 ob22.1 bb22 ob22 f23 ym23 bb23 ob23'),
+    G=('setup rl late out0 out1 fold3 oo1 out2',
+       'out-2 fold0 oo-2 side-1',
+       'out18 side19 out19 oo19 fold21 y20 y21 y22 e23 y23')))
+ORDER = dict(turns=(5, 20), queues=dict(
+    A=('setup w0 w1 w2 tw tab w3 gt0 gt1 gt2 gt3 w4',
+       'w0 gt-1',
+       'w20 gt19 w21 gt20 w22 gt21 w23 gt22 gt23 y23'),
+    V=('mat.1 setup.1 mat.1 late.1 mat.1 x.1 mat.1 setup.2 fs.1 setup.1 mat.2 rl mat.1 cb.1 setup.1 cb.1 setup.1 fs.1 x cb.1 late.1 fs.1 cb.1 late.1 fs.1 late.1 cb.2 late.1 setup cb.1 fs.1 cb mat late.1 b2 b0 b1 b3 fs.1 w0 dm.3 c0.1 dm.1 c0.1 dm.1 c0 cw0 dm.2 om.2 cw1 om.1 dm.1 om dm idx0 c1.2 tab co.2 cw2 co.1 c1 co.4 c2.1 fs c2.1 co idx1 gt0 c2 c3.1 th0 h0 cw3 idx2 pp0 rs0 out0 gt1 c3 oo0 th1 h1 rs1 out1 pp1 idx3 late h2 th2 oo1 rs2 pp2 b4 oo2 out2 w4 c4.1 cw4 c4',
+       'w0 th-2 h-2 b0 rs-2 idx-1 pp-2 out-2 c0.1 cw0 c0.1 gt-1 c0 oo-2',
+       'b20 w20 th18 h18 rs18 pp18 idx19 out18 cw20 c20.1 gt19 c20 w21 th19 b21 h19 rs19 idx20 oo18 pp19 out19 c21.1 cw21 oo19 c21 w22 b22 h20 rs20 th20 pp20 idx21 c22.1 cw22 tree22.1 y20.1 oo20 c22 y20.1 w23 b23 rs21 th21 y20.1 h21 idx22 c23.1 cw23 pp21 c23.1 y20.1 c23 y21.1 tree23.1 tree22.1 oo21 y21.1 y20.1 h22 idx23 y20 th22 pp22 rs22 gt23 y21.2 tree22.1 y21.1 y22.1 oo22 y21 tree23.1 th23 y22.1 h23 y22.2 rs23 y22 tree22 tree23.1 pp23 y23.1 tree23 y23 em23 ef23'),
+    P=('jb0 jb1 vote0 jb2 vote1 co vote2.2 oa0 jb3 oa1 f0 vote2 bb0 vote3.1 ob0 oa2 f1 vote3.1 bb1 vote3 f2 ob1 bb2.1 ob2 bb2 jb4 oa3 f3 vote4',
+       'bb-2 jb0 ob-2 oa-1 vote0.2 f-1 vote0',
+       'bb18 oa19 ob18 jb20 ym20 vote20.1 f19 vote20 bb19 jb21 ob19 oa20 vote21.1 oa21 f20 vote21 jb22 ym21 bb20.1 ob20.1 bb20 vote22.1 ob20 vote22.1 f21 vote22 ym22 jb23 oa22 bb21 vote23 ob21.1 f22 oa23 ob21 bb22 ob22.1 ym23.1 f23 ob22 bb23.1 ym23 bb23 ob23'),
+    G=('late.1 setup rl late out0 fold3 out1 oo1 out2',
+       'out-2 fold0 oo-2 side-1',
+       'out18 side19 out19 oo19 fold21 y20 y21 y22 e23 y23')))
+COST.update(og=2)
+ORDER["queues"].update(
+    V=ORDER["queues"]["V"][:2] + ('w20 h18 th18 rs18 pp18 idx19 out18 b20 cw20 c20.1 oo18 c20.1 gt19 c20 w21 b21 h19 th19 idx20 pp19 rs19 out19 c21.1 oo19 cw21 c21 w22 b22 th20 h20 rs20 idx21 pp20 cw22 c22 tree22.1 y20.1 w23 y20.1 idx22 rs21 tree22.1 th21 y20.1 h21 b23 cw23 pp21 tree23.1 c23.1 y20.2 c23.1 y20 y21.1 c23 y21.2 tree23.1 rs22 th22 h22 idx23 y21.1 pp22 gt23 y21.1 tree22.1 y22.1 tree22 y21 y22.3 th23 h23 y22 pp23 rs23 tree23.1 y23.1 tree23 y23 em23 ef23',),
+    P=ORDER["queues"]["P"][:2] + ('bb18 ob18 ym20.1 oa19 jb20 vote20.2 f19 vote20 jb21 bb19 ob19 ym20 ym21.1 oa20 oa21 vote21.1 f20 vote21 jb22 ym21 bb20.1 ob20.1 bb20 ob20 vote22.2 ym22.1 vote22 f21 oa22 ob21.1 bb21 oa23 ym22 jb23 ob21 vote23.1 f22 vote23 ob22.1 bb22 ob22 f23 ym23 bb23 ob23',),
+    G=('late.1 setup rl late out0 fold3 out1 oo1 out2',
+       'out-2 fold0 side-1 oo-2',
+       'out18 side19 out19 oo19 fold21 y20 y21 y22 e23 y23'))
+COST.update(wa=13, ga=48)
 
-COST = dict(r=1.56, ov=3.0, ova=3.0, pe=0.63, hop=60.0, lat=3300.0, first=2000.0, call=700.0, dma0=2000.0, dmab=0.0045, look=70.0,
-            cmp="VV", wa=40, ga=64, ta=128, loads="wdco", og=2, nr=0, split=1, zc=1, sp=1, pkg=0,
-            wx={0: 32, 1: 64, 2: 64, 22: 48, 23: 48}, gx={0: 32, 1: 48, 22: 48, 23: 32},
-            tau={'first0': 0, 'first1': 1, 'back0': 0, 'back1': 1, 'tab0': 0.45, 'tab1': 0.01, 'Vw11': -0.8, 'Sy': 4, 'Se': 4.5, 'from': 9,
-                 'Amb': 0.54, 'Aw0': -0.19, 'Agt': 1.43, 'Aoo': 2.47, 'Ay': 2.84, 'Ays': 10.07, 'Vw1': 0.07, 'Vh': 2.35, 'Vth': 2.35,
-                 'Vrs': 2.38, 'Vidx': 1.35, 'Vpp': 2.37, 'Vb': 0.77, 'Vout': 2.52, 'Vzw': 2.73, 'Vy': 3.04, 'Vc0': 0.58, 'Vfix': 0.78,
-                 'Vsc': 0.94, 'Vpk': 1.4, 'Vgt': 1.85, 'Pvote': 0.5, 'Pf': 1.53, 'Pjm': 0.95, 'Pbb': 2.28, 'Poa': 1.49, 'Pos': 2.28,
-                 'Pob': 2.44, 'Pjb': 0.76, 'Gout': 3.35, 'Goo': 3.89, 'Ge': 4.62, 'Gy': 5.69,
-                 'om': -8.73, 'co': 0.42, 'Aw01': -12.32, 'Pf2': 0.45, 'Vsc3': -0.39, 'Vc00': -8.86, 'Vth4': -0.36, 'Vgt0': -0.21, 'Atab2': -3.92, 'Pf3': 0.26, 'Vout0': -0.3, 'Vsc1': -1.41, 'Vth0': -0.28, 'Vw13': -2.32, 'Amb1': -1.68, 'Atab0': -5.11, 'Pjb4': 0.03, 'Pvote1': -2.08, 'Aw03': -0.33, 'Vw10': -11.42, 'Agt0': -1.0, 'Vc04': 0.1, 'Pjb0': -2.41, 'Vfix0': -6.42, 'Amb0': -3.44, 'Atab1': -9.97, 'Aw02': -2.49, 'Poa1': -0.15, 'Pjm1': -0.95, 'Pvote0': -7.09, 'Vh0': -0.43, 'Pjb1': -7.19, 'Vc01': -2.84, 'Vidx2': -0.17, 'Vidx1': -1.42, 'Vout1': -0.18, 'Vc03': -0.65, 'Vw14': -0.46, 'Vth2': -0.33, 'Vh1': -0.6, 'Vtab0': -6.94, 'Atab-1': -4.46, 'Aw00': -9.64, 'Vtab3': -1.92, 'Atab3': -3.57, 'Vtab1': -4.96, 'Vgt1': -0.65, 'Amb3': -0.43, 'Vidx0': -2.04, 'Vfix3': -0.39, 'Pjm0': -2.24, 'Pf1': -0.07, 'Vsc0': 0.72, 'Agt2': -0.52, 'Vsc2': 0.53, 'Vth1': -0.57, 'Vfix1': -1.69, 'Vtab2': -2.2, 'Vh4': -0.3, 'Vc022': -0.19, 'Pbb22': 2.55, 'Vrs23': 4.28, 'Vpk23': 0.48, 'Gy23': 6.88, 'Aw021': 0.09, 'Gy20': -1.21, 'Vzw21': 0.08, 'Pf20': 0.59, 'Vh23': 1.72, 'Vpp22': 1.88, 'Vfix22': -0.36, 'Pbb23': 3.49, 'Pf22': 2.42, 'Vzw22': 1.81, 'Vpp23': 5.2, 'Pob22': 3.76, 'Vzw23': 5.03, 'Pvote23': 1.26, 'Pjm21': 0.35, 'Pob23': 3.77, 'Aw022': 0.49, 'Gy22': 4.89, 'Pjb21': 0.49, 'Vsc23': 0.28, 'Vy23': 9.17, 'Vrs22': 1.21, 'Pf23': 3.07, 'Pjb23': 0.98, 'Pbb20': 0.08, 'Vth23': 1.41, 'Vgt23': 0.45, 'Vy22': 2.96, 'Pjm23': 2.69})
 
-
-def build(g, T, to_next, to_prev, cost):
+def build(g, T, peers, cost):
     ops = []
     A, M = AluOpType, ActivationFunctionType
     v, s, pe = g.vector, g.scalar, g.tensor
     nd = [0]
-    now = [None, None]
+    now = [0, "setup"]
 
-    def op(eng, fn, rd, wr, dur, banks=(), kind="c", sem=None, after=None, lat=0.0):
-        ops.append(dict(eng=eng, fn=fn, rd=rd, wr=wr, dur=dur, banks=banks, kind=kind, sem=sem, after=after,
+    def op(eng, fn, rd, wr, dur, banks=(), kind="c", sem=None, after=None, lat=0.0, inc=0):
+        ops.append(dict(eng=eng, fn=fn, rd=rd, wr=wr, dur=dur, banks=banks, kind=kind, sem=sem, after=after, inc=inc,
                         lat=lat, i=len(ops), n=now[0], tag=now[1]))
         return len(ops) - 1
 
     def at(tag):
         now[1] = tag
 
-    def vec(fn, rd, wr, n, banks=()):
-        return op("V", lambda: [fn()], rd, wr, max(64.0, n) + cost["ov"], banks)
+    def vec(fn, rd, wr, n, banks=(), two=0):
+        return op("V", lambda: [fn()], rd, wr, max(64.0, n) * cost["f"] + cost["ov"] + cost.get("ps", 0) * len(banks) + cost.get("tt", 0) * two, banks)
 
     def act(fn, rd, wr, n, banks=()):
-        return op("A", lambda: [fn()], rd, wr, max(64.0, n) + cost["ova"], banks)
+        return op("A", lambda: [fn()], rd, wr, max(64.0, n) * cost["f"] + cost["ova"], banks)
+
+    def tt(out, a, b, alu, rd, wr, n, banks=()):
+        return vec(lambda: v.tensor_tensor(out, a, b, alu), rd, wr, n, banks, 1)
+
+    def ts(out, a, s1, s2, ops2, rd, wr, n, banks=()):
+        return vec(lambda: v.tensor_scalar(out, a, s1, s2, *ops2), rd, wr, n, banks)
 
     def gather(eng, out, win, rd, wr, n):
         if eng == "A":
-            return op("A", lambda: [s.activation(out, win, M.Copy)], rd, wr, 78 + cost["r"] * n)
-        return op("V", lambda: [v.tensor_copy(out, win)], rd, wr, 60 + cost["r"] * n)
+            return op("A", lambda: [s.activation(out, win, M.Copy)], rd, wr, (78 + cost["r"] * n) * cost["f"])
+        return op("V", lambda: [v.tensor_copy(out, win)], rd, wr, (60 + cost["r"] * n) * cost["f"])
 
-    def mm(lst, rd, banks):
-        n = sum(x[5] for x in lst)
-        return op("P", lambda: [pe.matmul(x[0], x[1], x[2], x[3], x[4]) for x in lst], rd, [],
-                  n * cost["pe"] + 30 + len(lst) * cost.get("ovp", 0.0), banks)
+    def mm(lst, rd, banks, first=True, last=True):
+        n = sum(x[3] for x in lst)
+        return op("P", lambda: [pe.matmul(x[0], x[1], x[2], first and k == 0, last and k == len(lst) - 1) for k, x in enumerate(lst)],
+                  rd, [], n * cost["pe"] * cost["f"] + 30, banks)
 
-    def dma(out, in_, rd, wr, nbytes, q="S", sem=None, order=False):
+    def dma(out, in_, rd, wr, nbytes, q="S", sem=None):
         if sem is None:
             sem = "d%d" % nd[0]
             nd[0] += 1
         qu = g.sync if q == "S" else g.scalar
-        i = op(q, lambda: [qu.dma_start(out, in_)], rd, wr, 100.0, kind="dma", sem=sem, lat=nbytes * cost["dmab"])
-        if order:
-            ops[i]["slot"] = i
-        return i
+        return op(q, lambda: [qu.dma_start(out, in_)], rd, wr, cost.get("sq", 100.0), kind="dma", sem=sem, lat=nbytes * cost["dmab"] + cost.get("dr", 0.0))
 
-    calls = {}
-
-    def send(dst, srcs, peer, sem, rd, wr, more=0.0, after=None):
-        rid, pid, mask = peer
+    def send(dst, srcs, peer, sem, rd, after=None):
+        rid, pid, mask, engines = peers[peer]
 
         def fn():
             if len(srcs) == 1:
@@ -106,89 +268,74 @@ def build(g, T, to_next, to_prev, cost):
                                                       remote_sem=T.sem[sem], srcs=srcs, dsts=[dst], alu_op=2)],
                                    local_sem=T.sem.sent)
             return []
-        i = op("G", fn, rd, [], cost["call"], kind="send", after=after)
-        calls[sem] = i
-        op(None, None, [], wr, 0.0, kind="arr", sem=sem, after=i, lat=cost["lat"] + more)
+        return op("G", fn, rd, [], cost["call"], kind="send", after=after, inc=engines)
+
+    def arrive(i, sem, wr, engines, lat, kind="arr"):
+        op(None, None, [], wr, 0.0, kind=kind, sem=sem, after=i, lat=lat, inc=engines)
+
+    def post(dst, srcs, peer, sem, rd, wr, more=0.0, after=None):
+        i = send(dst, srcs, peer, sem, rd, after)
+        arrive(i, sem, wr, peers[peer][3], cost["lat"] + more)
+        return i
 
     def xv(buf, f, n=1):
         return buf[:, f * 16 + 1:(f + n) * 16:2, :]
 
-    def xt(buf, f, kh):
-        return buf[:, f * 16 + 1 - kh:f * 16 + 17 - kh, :]
+    def xt(buf, f, bit):
+        return buf[:, f * 16 + 1 - bit:f * 16 + 17 - bit, :]
 
-    dma(T.RLI[:], T.rl[:], [], ["RLI"], 131072, order=True)
-    dma(T.CBI[:], T.cb[:], [], ["CBI"], 131072, q="A")
-    for what in cost["loads"]:
+    dma(T.RLI[:], T.rl[:], [], ["RLI"], 131072)
+    dma(T.CBI[:], T.cb[:], [], ["CBI"], 131072)
+    dma(T.WP[:, V:V + 16], T.wp[:, 0:16], [], ["WPw"], 16384)
+
+    def load(what):
         if what == "w":
-            dma(T.WP[:, 0:V], T.wp[:], [], ["WP"], 1048576, order=True)
+            dma(T.WP[:, 0:V], T.wp[:], [], ["WP"], 1048576)
         elif what == "d":
             for g0 in range(2):
-                for m in range(2):
-                    dma(T.DMI[:, g0, m * 8:(m + 1) * 8, :], T.dm[g0::2, m * V:(m + 1) * V], [], [("DMI", g0, m)], 65536, order=True)
+                for k in range(4):
+                    dma(T.DMI[:, g0, k * 4:k * 4 + 4, :], T.dm[g0::2, k * 2048:(k + 1) * 2048], [], [("DMI", g0, k)], 32768)
         elif what == "o":
-            for m in range(2):
-                dma(T.OMI[:, m * 256:(m + 1) * 256], T.om[:, m * V:(m + 1) * V], [], [("OMI", m)], 131072, order=True)
+            for k in range(4):
+                a = k % 2 * V + k // 2 * 2048
+                dma(T.OMI[:, k * 128:(k + 1) * 128], T.om[:, a:a + 2048], [], [("OMI", k)], 65536)
         else:
-            dma(T.COI[:], T.co[:], [], ["COI"], 131072, order=True)
-    dma(T.WP[:, V:V + 16], T.wp[:, 0:16], [], ["WPw"], 65536, q="A")
+            dma(T.COI[:], T.co[:], [], ["COI"], 131072)
+    early, late = cost["loads"].split("|")
+    for what in early:
+        load(what)
 
+    at("rl")
     vec(lambda: v.tensor_copy(T.RLB[:], T.RLI[:]), ["RLI"], ["RLB"], 256)
-    send(T.RLL[:], [T.RLB[:]], to_prev, "a_rl", ["RLB"], ["RLL"], more=cost["first"])
+    post(T.RLL[:], [T.RLB[:]], "prev", "a_rl", ["RLB"], ["RLL"], more=cost["first"])
+    at("setup")
 
-    op("G", lambda: [g.iota(T.PI[:], [[-1, 128]], 0, 1, allow_small_or_imprecise_dtypes=True)], [], ["PI"], 420.0)
     op("G", lambda: [g.iota(T.PC[:, 0:1], [[0, 1]], 0, 1)], [], ["PC"], 160.0)
+    op("G", lambda: [g.iota(T.PI[:], [[-1, 128]], 0, 1, allow_small_or_imprecise_dtypes=True)], [], ["PI"], 420.0)
     op("G", lambda: [g.iota(T.LO[:], [[1, 256]], 0, 0, allow_small_or_imprecise_dtypes=True)], [], ["LO"], 670.0)
-    vec(lambda: v.memset(T.MASK[:], 1.0), [], ["MASK"], 512)
+    vec(lambda: v.memset(T.ZR[:], 0.0), [], ["ZR"], 512)
     for k in range(4):
-        act(lambda k=k: s.activation(T.RLW[:, 16 + k * 1024:16 + (k + 1) * 1024], T.MASK[:], M.Copy), ["MASK"], [("RLW0", k)], 1024)
-    vec(lambda: v.memset(T.MASK[:, 0::16], 0.0), [], ["MASK"], 64)
-    vec(lambda: v.memset(T.ONE[:], 1.0), [], ["ONE"], 64)
-    vec(lambda: v.memset(T.C16[:], 16.0), [], ["C16"], 64)
-    vec(lambda: v.memset(T.COX[:], 0.0), [], ["COX"], 260)
-    vec(lambda: v.memset(T.ZR[:], 0.0), [], ["ZR"], 96)
-    vec(lambda: v.tensor_scalar(T.X0[:, 0:65, :], T.COX[:], 0.0, None, A.mult), ["COX"], [("X0", 0, 0)], 260)
-    vec(lambda: v.tensor_scalar(T.X0[:, 64:129, :], T.COX[:], 0.0, None, A.mult), ["COX"], [("X0", 0, 0)], 260)
-    if not cost["split"]:
-        vec(lambda: v.tensor_copy(xv(T.X0, 0), T.ONE[:, 0:64]), ["ONE"], [("X0", 0, 0)], 64)
-    vec(lambda: v.tensor_copy(T.X1[:], T.X0[:]), [("X0", 0, 0)], [("X0", 1, 0)], 516)
-    for p in range(2):
-        act(lambda p=p: s.activation(T["XM%d" % p][:], T.ZR[:, 0:136], M.Copy), ["ZR"], [("XM0", p)], 136)
-    for j, (lo, hi) in enumerate(("AA", "AV", "VA", "VV")):
-        if lo + hi in [cost["cmp"][k:k + 2] for k in range(0, len(cost["cmp"]), 2)]:
-            if lo == hi:
-                vec(lambda j=j, lo=lo: v.memset(T.THR[:, j:j + 1], -1.0 if lo == "A" else -64.5), [], [("THR", j, 0), ("THR", j, 1)], 1)
-            else:
-                vec(lambda j=j, lo=lo: v.memset(T.THR[0:64, j:j + 1], -1.0 if lo == "A" else -64.5), [], [("THR", j, 0)], 1)
-                vec(lambda j=j, hi=hi: v.memset(T.THR[64:128, j:j + 1], -1.0 if hi == "A" else -64.5), [], [("THR", j, 1)], 1)
-    vec(lambda: v.tensor_scalar(T.ID[:], T.PI[:], 0.0, None, A.is_equal), ["PI"], ["ID"], 128)
-    vec(lambda: v.tensor_copy(T.IH[:], T.ID[:]), ["ID"], ["IH"], 64)
-    vec(lambda: v.tensor_scalar(T.IP[:], T.ID[:], 512.0, None, A.mult), ["ID"], ["IP"], 64)
-    vec(lambda: v.tensor_scalar(T.IN[:], T.ID[:], -512.0, None, A.mult), ["ID"], ["IN"], 64)
-    act(lambda: s.activation(T.IB[:], T.ID[:], M.Copy), ["ID"], ["IB"], 128)
-    if "A" in cost["cmp"]:
-        act(lambda: s.activation(T.IM[:], T.ID[:], M.Copy, scale=-1.0), ["ID"], ["IM"], 128)
-    act(lambda: s.activation(T.IF[:], T.ID[:], M.Copy), ["ID"], ["IF"], 128)
-    act(lambda: s.activation(T.IK[:], T.ID[:], M.Copy, scale=MS / 2.0), ["ID"], ["IK"], 128)
-    act(lambda: s.activation(T.IS[:], T.ID[:], M.Copy, scale=1.0 / 512), ["ID"], ["IS"], 128)
+        act(lambda k=k: s.activation(T.RLW[:, 16 + k * 1024:16 + (k + 1) * 1024], T.ZR[:], M.Copy), ["ZR"], [("RLW0", k)], 1024)
+    ts(T.PG[:, 0:1], T.PC[:, 0:1], 4, 1, (A.logical_shift_right, A.bitwise_and), ["PC"], ["PG"], 1)
+    ts(T.PD[:, 0:1], T.PC[:, 0:1], 15, None, (A.bitwise_and,), ["PC"], ["PD"], 1)
+    for x in range(2):
+        ts(T.MK[:, x:x + 1], T.PG[:, 0:1], float(x), None, (A.is_equal,), ["PG"], [("MK", x)], 1)
+    ts(T.PF[:, 0:1], T.PD[:, 0:1], -8.0, 256.0, (A.add, A.mult), ["PD"], ["PF"], 1)
+    ts(T.HI[:], T.LO[:], 0.0, T.PF[:, 0:1], (A.mult, A.add), ["PF", "LO"], ["HI"], 128)
 
-    def row(f):
-        return T.ID[:, f::16]
+    def turn(src, key, add, Y, Z):
+        for x in range(2):
+            ts(Y[:, :, x * 16:x * 16 + 16], src[:], add, T.MK[:, x:x + 1], (A.add, A.mult), [key, ("MK", x)], [(key, "Y", x)], 256)
+        vec(lambda: v.transpose(Z[:], Y[:]), [(key, "Y", 0), (key, "Y", 1)], [(key, "Z")], 256)
 
-    def fs(f):
-        return T.FS[:, f * 8:(f + 1) * 8]
-    vec(lambda: v.tensor_tensor(fs(0), row(5), row(0), A.subtract), ["ID"], [("FS", 0)], 8)
-    vec(lambda: v.tensor_tensor(fs(1), fs(0), row(1), A.subtract), ["ID", ("FS", 0)], [("FS", 1)], 8)
-    vec(lambda: v.tensor_tensor(fs(7), fs(1), row(2), A.subtract), ["ID", ("FS", 1)], [("FS", 7)], 8)
-    vec(lambda: v.tensor_tensor(fs(4), row(3), row(4), A.add), ["ID"], [("FS", 4)], 8)
-    act(lambda: s.activation(fs(2), fs(7), M.Copy, scale=1.0 / 512), [("FS", 7)], [("FS", 2)], 8)
-    act(lambda: s.activation(fs(3), row(5), M.Copy, scale=1.0 / 512), ["ID"], [("FS", 3)], 8)
-    act(lambda: s.activation(fs(5), row(0), M.Copy, scale=-1.0 / 512), ["ID"], [("FS", 5)], 8)
-    act(lambda: s.activation(fs(6), row(1), M.Copy, scale=-1.0 / 512), ["ID"], [("FS", 6)], 8)
-    FSK = [("FS", f) for f in range(7)]
-    vec(lambda: v.tensor_scalar(T.PD[:, 0:1], T.PC[:, 0:1], 15, None, A.bitwise_and), ["PC"], ["PD"], 1)
-    vec(lambda: v.tensor_scalar(T.PF[:, 0:1], T.PD[:, 0:1], -8.0, 256.0, A.add, A.mult), ["PD"], ["PF"], 1)
-    vec(lambda: v.tensor_scalar(T.HI[:], T.LO[:], 0.0, T.PF[:, 0:1], A.mult, A.add), ["PF", "LO"], ["HI"], 128)
+    at("cb")
+    turn(T.CBI, "CBI", -2048.0, T.CY, T.CZ)
+    tt(T.CS[:], T.CZ[:, :, 0:16], T.CZ[:, :, 16:32], A.add, [("CBI", "Z")], [("CBI", "S")], 256)
+    for h in range(4):
+        ts(T.L0[:, h::4], T.CS[:, h::4, :], 2048.0, None, (A.add,), [("CBI", "S")], [("L0", h)], 32)
+    L0K = [("L0", h) for h in range(4)]
 
+    at("rlw")
     R0K = [("RLW0", k) for k in range(4)]
     dma(T.RLW[3::16, 16:16 + V], T.HI[:], R0K + ["HI"], [("RLW", 3)], 65536)
     dma(T.RLW[4::16, 16:16 + V], T.LO[:], R0K + ["LO"], [("RLW", 4)], 65536)
@@ -196,225 +343,274 @@ def build(g, T, to_next, to_prev, cost):
         dma(T.RLW[f::16, 16 - f:16 - f + V], T.RLL[:], R0K + ["RLL"], [("RLW", f)], 65536)
     for f in (1, 2):
         dma(T.RLW[f::16, 16 - f + V:18 - f + V], T.RLL[0::16, 0:2], R0K + ["RLL"], [("RLW", 10 + f)], 100)
+    for what in late:
+        load(what)
     RLK = R0K + [("RLW", f) for f in (0, 1, 2, 3, 4, 11, 12)]
 
+    at("dm")
     for g0 in range(2):
-        vec(lambda g0=g0: v.tensor_scalar(T.DMR[:, :, g0 * 16:(g0 + 1) * 16], T.DMI[:, g0, :, :], -2048.0, None, A.add),
-            [("DMI", g0, 0), ("DMI", g0, 1)], [("DMR", g0)], 256)
-    vec(lambda: v.transpose(T.DMU[:], T.DMR[:]), [("DMR", 0), ("DMR", 1)], ["DMU"], 256)
-    for b in range(8):
-        vec(lambda b=b: v.tensor_scalar(T.DMZ[:, b::8], T.DMU[:, b::8, :], 2048.0, None, A.add), ["DMU"], [("DMZ", b)], 32)
-    ZK = [("DMZ", b) for b in range(8)]
+        for m in range(2):
+            ts(T.DMR[:, :, g0 * 16 + m:g0 * 16 + 16:2], T.DMI[:, g0, m * 8:m * 8 + 8, :], -2048.0, None, (A.add,),
+               [("DMI", g0, 2 * m), ("DMI", g0, 2 * m + 1)], [("DMR", g0, m)], 128)
+    vec(lambda: v.transpose(T.DMU[:], T.DMR[:]), [("DMR", g0, m) for g0 in range(2) for m in range(2)], ["DMU"], 256)
+    for q in range(8):
+        ts(T.DMZ[:, q::8], T.DMU[:, q::8, :], 2048.0, None, (A.add,), ["DMU"], [("DMZ", q)], 32)
+    ZK = [("DMZ", q) for q in range(8)]
 
-    vec(lambda: v.tensor_copy(T.CB16[:], T.CBI[:]), ["CBI"], ["CB16"], 256)
-    vec(lambda: v.tensor_copy(T.B[:], T.CBI[:]), ["CBI"], [("B", c) for c in range(NCH)], 256)
-    at("co")
-    vec(lambda: v.tensor_scalar(T.COX[:, 1:513:2], T.COI[:], 1.0, None, A.add), ["COI"], ["COX"], 256)
-    mm([(T.OB[:, c * 64:c * 64 + 64], T.COX[:, 128 * c + 1 - kh:128 * c + 129 - kh], T.IB[:, kh::2, :],
-         kh == 0, kh == 1, 64) for c in range(NCH) for kh in range(2)], ["COX", "IB"], ["OB"])
-    act(lambda: s.activation(T.OIN[:, 0:256], T.OB[:, 0:256], M.Copy), [], [("OIN", c) for c in range(NCH)], 256, ["OB"])
+    at("mat")
+    vec(lambda: v.memset(T.SEL[:], 0.0), [], ["SEL"], 72)
+    vec(lambda: v.memset(T.COX[:], 0.0), [], ["COX0"], 260)
+    vec(lambda: v.memset(T.SEL[:, 15::16], 1.0 / 128), [], ["SEL"], 9)
+    for buf, x in (("ID", 1.0), ("IF", 1.0), ("IB", 1.0), ("IH", 1.0), ("IN", -1.0)):
+        ts(T[buf][:], T.PI[:], 0.0, x, (A.is_equal, A.mult), ["PI"], [buf], 128)
+    at("x")
+    for p in range(2):
+        vec(lambda p=p: v.tensor_copy(T["X%d" % p][:], T.ZR[:, 0:904]), ["ZR"], [("X0", p)], 452)
+
+    def row(f):
+        return T.ID[:, f::16]
+
+    def fs(f):
+        return T.FS[:, f * 8:(f + 1) * 8]
+    at("fs")
+    tt(fs(0), row(5), row(0), A.subtract, ["ID"], [("FS", 0)], 8)
+    tt(fs(4), row(3), row(4), A.add, ["ID"], [("FS", 4)], 8)
+    ts(fs(3), row(5), 1.0, None, (A.mult,), ["ID"], [("FS", 3)], 8)
+    tt(fs(1), fs(0), row(1), A.subtract, ["ID", ("FS", 0)], [("FS", 1)], 8)
+    ts(fs(5), row(0), -1.0, None, (A.mult,), ["ID"], [("FS", 5)], 8)
+    ts(fs(6), row(1), -1.0, None, (A.mult,), ["ID"], [("FS", 6)], 8)
+    tt(fs(2), fs(1), row(2), A.subtract, ["ID", ("FS", 1)], [("FS", 2)], 8)
+    FSK = [("FS", f) for f in range(7)]
+
     at("om")
-    for m in range(2):
-        vec(lambda m=m: v.tensor_copy(T.OMB[:, m * 256:(m + 1) * 256], T.OMI[:, m * 256:(m + 1) * 256]), [("OMI", m)], [("OMB", m)], 256)
+    for k in range(4):
+        vec(lambda k=k: v.tensor_copy(T.OMB[:, k // 2 * 256 + k % 2:k // 2 * 256 + 256:2], T.OMI[:, k * 128:(k + 1) * 128]),
+            [("OMI", k)], [("OMB", k)], 128)
+    at("co")
+    turn(T.COI, "COI", 1.0, T.OY, T.OZ)
+    for h in range(4):
+        tt(T.COX[:, 2 * h + 1:513:8], T.OZ[:, h::4, 0:16], T.OZ[:, h::4, 16:32], A.add, [("COI", "Z"), "COX0"], [("COX", h)], 64)
+    for c in range(NCH):
+        mm([(T.OB1[:, c * 64:c * 64 + 64], T.COX[:, 128 * c + 1 - bit:128 * c + 129 - bit], T.IB[:, bit::2, :], 64)
+            for bit in range(2)], ["IB", "COX0"] + [("COX", h) for h in range(4)], ["OB1"])
+    vec(lambda: v.tensor_copy(T.OIN[:, 0:256], T.OB1[:, 0:256]), [], [("OIN", c) for c in range(NCH)], 256, ["OB1"])
 
+    at("tw")
+    TK = [("TAB", 8)]
+    gather("A", T.TAB[:, 2 * V:2 * V + 32], T.RLW[:, 16:16 + V].indirect(T.DMZ[:, 0:2]), RLK + ZK, TK, 32)
+    dma(T.TAB[5::16, 2 * V:2 * V + 4], T.OMB[0::16, 0:4], [("OMB", 0), ("OMB", 1)], TK, 100)
     at("tab")
-    TK = []
-    na = cost["ta"]
-    for m in range(2):
-        now[0] = -1
-        gather("A", T.TAB[:, m * MS + V:(m + 1) * MS], T.RLW[:, 16:16 + V].indirect(T.DMZ[:, m * 256:m * 256 + 2]),
-               RLK + ZK, [("TAB", m, V)], 32)
-        dma(T.TAB[5::16, m * MS + V:m * MS + V + 2], T.OMB[0::16, m * 256:m * 256 + 2], [("OMB", m)], [("TAB", m, V)], 100)
-        pk = []
-        for k, (eng, a, b) in enumerate((("A", 0, na // 4 * 2), ("V", na, (na + 256) // 4 * 2), ("A", na // 4 * 2, na), ("V", (na + 256) // 4 * 2, 256))):
-            now[0] = 2 * m + k // 2
-            gather(eng, T.TAB[:, m * MS + a * 16:m * MS + b * 16],
-                   T.RLW[:, 16:16 + V].indirect(T.DMZ[:, m * 256 + a:m * 256 + b]),
-                   RLK + ZK, [("TAB", m, a * 16)], (b - a) * 16)
-            pk.append(("TAB", m, a * 16))
-        dma(T.TAB[5::16, m * MS:m * MS + V], T.OMB[:, m * 256:(m + 1) * 256], [("OMB", m)], pk, 65536)
-        TK += pk + [("TAB", m, V)]
+    for half in range(2):
+        pk = [("TAB", k) for k in range(4 * half, 4 * half + 4)]
+        for _, k in pk:
+            gather(cost["ta"][k], T.TAB[:, k * 1024:(k + 1) * 1024], T.RLW[:, 16:16 + V].indirect(T.DMZ[:, k * 64:(k + 1) * 64]),
+                   RLK + ZK, [("TAB", k)], 1024)
+        dma(T.TAB[5::16, half * V:(half + 1) * V], T.OMB[:, half * 256:(half + 1) * 256], [("OMB", 2 * half), ("OMB", 2 * half + 1)], pk, 65536)
+        TK = TK + pk
 
-    nr = [0]
-    spare = ["R0", "R1"][cost["nr"]:]
+    at("late")
+    for bit in range(2):
+        op("G", lambda bit=bit: [g.iota(T.TI[:, bit * 128:bit * 128 + 128], [[2, 4], [0, 2], [8, 16]], bit, -1,
+                                        allow_small_or_imprecise_dtypes=True)], [], [("TI", bit)], 420.0)
+    vec(lambda: v.memset(T.PA[:], 0.0), [], [("PA", 0), ("PA", 1)], 64)
+    ts(T.MV[:], T.TI[:], 0.0, None, (A.is_equal,), [("TI", 0), ("TI", 1)], ["MV"], 256)
+    for x in range(2):
+        vec(lambda x=x: v.memset(T.PA[x * 64:x * 64 + 64, :, x * 16:x * 16 + 16], 1.0), [], [("PA", x)], 64)
+    ts(T.MN[:], T.MV[:], -1.0, None, (A.mult,), ["MV"], ["MN"], 128)
+    for buf, same in (("PB", 32.0), ("PO", -1.0 / 64)):
+        ts(T[buf][:], T.PA[:], 128.0 + same, -128.0, (A.mult, A.add), [("PA", 0), ("PA", 1)], [buf], 64)
+    MVK = ["MV", "MN", ("PA", 0), ("PA", 1), "PB", "PO"]
+
+    omsg = [None]
     for t in range(STEPS):
         last = t == STEPS - 1
+        W = T["W%d" % t]
         for c in range(NCH):
-            w0, l0 = c * 1024, c * 64
-            n = t * NCH + c
+            l0, n = c * 64, t * NCH + c
+            p = n % 2
             now[0] = n
-            W = T["W%d" % (t % 2)]
-            X, XM, xp = T["X%d" % (n % 2)], T["XM%d" % (n % 2)], n % 2
-            jb = spare[0] if spare and n % 2 else "JB"
-            vb = spare[1] if len(spare) > 1 and n % 2 else "VB"
-            JB, VB = T[jb], T[vb]
-            if t == 0:
-                lst, c0, lk = T.CB16, l0, "CB16"
-            else:
-                lst, c0, lk = T.MSG, (n - NCH) * 64, ("MSG", n - NCH)
-                at("b")
-                vec(lambda c0=c0, l0=l0: v.tensor_copy(T.B[:, l0:l0 + 64], T.MSG[:, c0:c0 + 64]), [lk], [("B", c)], 64)
+            X, JB, BB, F, OB = T["X%d" % p], T["JB%d" % p], T["BB%d" % p], T["F%d" % p], T["OB%d" % p]
+            jb, bb, fb, ob, x0, s0 = "JB%d" % p, "BB%d" % p, "F%d" % p, "OB%d" % p, ("X0", p), p * 1024
+            lst, c0, lk = (T.L0, l0, L0K) if t == 0 else (T.MSG, (n - NCH) * 64, [("MSG", n - NCH)])
+            wa = cost["wx"].get(n, cost["wa"])
+            side = 2 if last else NCH
 
-            def wk(a, b):
-                return [("W", t % 2, c, k) for k in range(a // 2, b // 2)]
-            cmp = cost["cmp"][2 * n % len(cost["cmp"]):][:2]
-            wa = cost.get("wx", {}).get(n, cost["wa"])
-            cuts = sorted({0, wa, 64} | ({32} if cmp != "VV" or cost.get("halves") else set()))
-            for k, (a, b) in enumerate(zip(cuts, cuts[1:])):
-                at("w%d" % k)
-                gather("A" if b <= wa else "V", W[:, w0 + a * 16:w0 + b * 16], T.WP[:, 0:V + 16].indirect(lst[:, c0 + a:c0 + b]),
-                       ["WP", "WPw", lk], wk(a, b), (b - a) * 16)
-            for h in range(2):
-                a, b = w0 + h * 512, w0 + h * 512 + 512
-                if cmp[h] == "A":
-                    rb = "R%d" % (nr[0] % cost["nr"])
-                    nr[0] += 1
-                    R = T[rb]
-                    at("d%d" % h)
-                    mm([(R[:], T.ID[:], W[:, a:b], True, False, 512),
-                        (R[:, 0:511], T.IM[:], W[:, a + 1:b], False, False, 511),
-                        (R[:, 15:511:16], T.ID[:], W[:, a + 16:b:16], False, False, 64),
-                        (R[:, 15:512:16], T.IM[:], W[:, a:b:16], False, True, 64)], ["ID", "IM"] + wk(h * 32, h * 32 + 32), [rb])
-                    at("c%d" % h)
-                    act(lambda a=a, b=b, R=R: s.activation(T.IND[:, a:b], R[:], M.Sign, bias=-0.5), [], [("IND", c, h)], 512, [rb])
-                elif cmp != "VV" or cost.get("halves") or h == 0:
-                    hs = [0, 1] if cmp == "VV" and not cost.get("halves") else [h]
-                    b = w0 + hs[-1] * 512 + 512
-                    at("c%d" % h)
-                    vec(lambda a=a, b=b, W=W: v.tensor_tensor(T.IND[:, a:b - 1], W[:, a:b - 1], W[:, a + 1:b], A.is_gt),
-                        wk(h * 32, hs[-1] * 32 + 32), [("IND", c, k) for k in hs], b - a)
-            hs = [h for h in range(2) if cmp[h] == "V"]
-            if hs:
-                a, b = w0 + hs[0] * 512, w0 + hs[-1] * 512 + 512
-                at("fix")
-                vec(lambda a=a, b=b, W=W: v.tensor_tensor(T.IND[:, a + 15:b:16], W[:, a + 15:b:16], W[:, a:b:16], A.is_gt),
-                    wk(hs[0] * 32, hs[-1] * 32 + 32), [("IND", c, k) for k in hs], (b - a) // 16)
-            at("sc")
-            vec(lambda w0=w0, W=W: v.tensor_tensor_scan(T.SC[:, w0:w0 + 1024], T.MASK[:], W[:, w0:w0 + 1024], 0.0, A.mult, A.max),
-                ["MASK"] + wk(0, 64), [("SC", c)], 512)
-            if c == NCH - 1:
-                at("pk")
-                if cost["pkg"] and not last:
-                    op("G", lambda t=t: [g.affine_select(T.PK[:, t * 256:(t + 1) * 256], T.SC[:, 15::16], [[0, 256]], A.is_ge, 0.0, 0, 0)],
-                       [("SC", k) for k in range(NCH)], [("PK", t)], 720.0)
-                else:
-                    vec(lambda t=t: v.tensor_copy(T.PK[:, t * 256:(t + 1) * 256], T.SC[:, 15::16]),
-                        [("SC", k) for k in range(NCH)], [("PK", t)], 128)
-            at("vote")
-            mm([(VB[:, kl:64:8], T.IND[:, w0 + kl:w0 + 1024:8], T.ONE[:, 0:8], True, True, 64) for kl in range(8)],
-               ["ONE"] + [("IND", c, h) for h in range(2)], [vb])
+            def wv(a, b, e=0, ne=1):
+                w0 = c // side * side * 1024 + c % side
+                return W[:, w0 + (a * 64 + e) * side:w0 + b * 64 * side - c % side:side * ne]
+            wb = min(16, wa + cost["vx"].get(n, cost["vs"]))
+            for tag, eng, a, b in (("w", "A", 0, wa), ("w", "V", wa, wb), ("wb", "V", wb, 16)):
+                at(tag)
+                if b > a:
+                    gather(eng, wv(a, b), T.WP[:, 0:V + 16].indirect(lst[:, c0 + a * 4:c0 + b * 4]),
+                           ["WP", "WPw"] + lk, [("W", n, k) for k in range(a, b)], (b - a) * 64)
+            wk = [("W", n, k) for k in range(16)]
+            at("b")
+            ts(T.B[:, l0:l0 + 64], lst[:, c0:c0 + 64], 2.0, -1.0 / 256, (A.mult, A.add), lk, [("B", c)], 64)
             at("jb")
-            mm([(JB[:, 0:64], T.IF[:], T.B[:, l0:l0 + 64], True, False, 256)], ["IF", ("B", c)], [jb])
-            j = ["AA", "AV", "VA", "VV"].index(cmp)
-            at("mb")
-            act(lambda j=j, XM=XM, VB=VB: s.activation(xv(XM, 0), VB[:, 0:64], M.Sign, bias=T.THR[:, j:j + 1]),
-                [("XM0", xp), ("THR", j, 0), ("THR", j, 1)], [("mb", xp)], 64, [vb])
-            at("jm")
-            mm([(JB[:, 0:64], xt(XM, 0, kh), T.IK[:, kh::2], False, kh == 1, 64) for kh in range(2)],
-               [("XM0", xp), ("mb", xp), "IK"], [jb])
+            if not cost["jl"]:
+                mm([(JB[:, 0:64], T.IF[:], T.B[:, l0:l0 + 64], 256)], ["IF", ("B", c)], [jb], last=False)
+            cv = cost["cx"].get(n, wa if cost["cv"] and wa < 15 else 15)
+            ne = cost["ne"]
+            for tag, a, b, a2 in (("cv", cv, 15, cv + 1), ("cw", 15, 16, 0)):
+                if b > a:
+                    at(tag)
+                    tt(T.IND[:, s0 + a * 64:s0 + b * 64], wv(a, b), wv(a2, a2 + b - a), A.is_gt, wk[a:b] + wk[a2:a2 + b - a],
+                       [("IND", p, k, e) for k in range(a, b) for e in range(4)], (b - a) * 64)
+            parts = {1: ((0, 1),), 2: ((0, 2), (1, 2)), 3: ((0, 2), (1, 4), (3, 4))}[ne]
+            for j, (e, st) in enumerate(parts):
+                at("c")
+                tt(T.IND[:, s0 + e:s0 + cv * 64:st], wv(0, cv, e, st), wv(1, cv + 1, e, st), A.is_gt, wk[:cv + 1],
+                   [("IND", p, k, x) for k in range(cv) for x in range(e, 4, st)], cv * 64 // st)
+                at("vote")
+                mm([(JB[:, 0:64], T.SEL[:, 15 - r:143 - r], T.IND[:, s0 + r:s0 + 1024:16], 64) for r in range(e, 16, st)],
+                   ["SEL"] + [("IND", p, k, x) for k in range(16) for x in range(e, 4, st)], [jb], first=j == 0 and cost["jl"] == 1, last=j == ne - 1)
+                if j == 0 and cost["jl"]:
+                    at("jb")
+                    mm([(JB[:, 0:64], T.IF[:], T.B[:, l0:l0 + 64], 256)], ["IF", ("B", c)], [jb], first=False, last=False)
             at("idx")
-            vec(lambda l0=l0, JB=JB: v.tensor_scalar(T.IDX[:, l0:l0 + 64], JB[:, 0:64], MS / 2.0, None, A.add), [], [("IDX", c)], 64, [jb])
-            na = cost.get("gx", {}).get(n, cost["ga"])
-            na += na % 2 * (1 if n % 2 else -1)
+            ts(T.IDX[:, l0:l0 + 64], JB[:, 0:64], BIG, BIG, (A.add, A.subtract), [], [("IDX", c)], 64, [jb])
+            ga = cost["gx"].get(n, cost["ga"])
             gk = []
             at("gt")
-            for eng, a, b in (("A", 0, na), ("V", na, 64)):
+            for eng, a, b in (("A", 0, ga), ("V", ga, 64)):
                 if b > a:
-                    gather(eng, T.GT[:, w0 + a * 16:w0 + b * 16], T.TAB[:].indirect(T.IDX[:, l0 + a:l0 + b]),
-                           TK + [("IDX", c)], [("GT", c, eng)], (b - a) * 16)
-                    gk.append(("GT", c, eng))
-            fb = "F%d" % (n % 2)
-            F = T[fb]
+                    gather(eng, T.GT[:, s0 + a * 16:s0 + b * 16], T.TAB[:].indirect(T.IDX[:, l0 + a:l0 + b]),
+                           TK + [("IDX", c)], [("GT", p, eng)], (b - a) * 16)
+                    gk.append(("GT", p, eng))
             o1 = T.OIN[:, n * 64:n * 64 + 64]
+            nf = 2 if last or cost["sv"] else 1
+            oa = [(F[:, f * 64:f * 64 + 64], T.ID[:], o1, 64) for f in range(2 + nf)]
+            fm = [(F[:, i:448:8], T.GT[:, s0 + i:s0 + 1024:8], T.FS[:, 0:56], 64) for i in range(8)]
             if cost["zc"]:
                 at("oa")
-                mm([(F[:, f * 64:f * 64 + 64], (T.ID if f < 2 else T.IS)[:], o1, f == 0, False, 64) for f in range(4)]
-                   + [(F[:, 256:448], T.ID[:], T.ZR[:], False, False, 192)], ["ID", "IS", "ZR", ("OIN", n)], [fb])
+                a = 128 + 64 * nf
+                mm(oa + [(F[:, a:448], T.ID[:], T.ZR[:, a:448], 448 - a)], ["ID", "IS", "ZR", ("OIN", n)], [fb], last=False)
                 at("f")
-                mm([(F[:, kl:448:8], T.GT[:, w0 + kl:w0 + 1024:8], T.FS[:, 0:56], False, kl == 7, 64) for kl in range(8)],
-                   FSK + gk, [fb])
+                mm(fm, FSK + gk, [fb], first=False)
             else:
                 at("f")
-                mm([(F[:, kl:448:8], T.GT[:, w0 + kl:w0 + 1024:8], T.FS[:, 0:56], kl == 0, False, 64) for kl in range(8)]
-                   + [(F[:, f * 64:f * 64 + 64], (T.ID if f < 2 else T.IS)[:], o1, False, f == 3, 64) for f in range(4)],
-                   FSK + gk + ["ID", "IS", ("OIN", n)], [fb])
-            x0 = ("X0", xp, 0)
-            if cost["split"]:
-                at("h")
-                vec(lambda F=F, X=X: v.tensor_scalar(xv(X, 1, 2), F[:, 0:128], 0.0, 1.0, A.max, A.min), [x0], [("h", xp)], 128, [fb])
-                at("th")
-                vec(lambda F=F, X=X: v.tensor_copy(xv(X, 5), F[:, 256:320]), [x0], [("th", xp)], 64, [fb])
+                mm(fm + oa, FSK + gk + ["ID", "IS", ("OIN", n)], [fb])
+            at("h")
+            nh = 2 + nf if cost["hr"] else 2
+            ts(xv(X, 0, nh), F[:, 0:64 * nh], 0.0, 1.0, (A.max, A.min), [x0], [("h", p)] + [("rs", p)] * cost["hr"], 64 * nh, [fb])
+            at("th")
+            vec(lambda F=F, X=X: v.tensor_copy(xv(X, 4), F[:, 256:320]), [x0], [("th", p)], 64, [fb])
+            at("rs")
+            if not cost["hr"] and n not in cost["rsa"]:
+                ts(xv(X, 2, nf), F[:, 128:128 + 64 * nf], 0.0, None, (A.max,), [x0], [("rs", p)], 64 * nf, [fb])
+            at("pp")
+            tt(xv(X, 5, 2), xv(X, 0, 2), F[:, 320:448], A.mult, [x0, ("h", p)], [("pp", p)], 128, [fb])
+            if not cost["hr"] and n in cost["rsa"]:
                 at("rs")
-                nf = 1 if cost["sp"] and not last else 2
-                vec(lambda F=F, X=X, nf=nf: v.tensor_scalar(xv(X, 3, nf), F[:, 128:128 + 64 * nf], 0.0, None, A.max), [x0], [("rs", xp)], 64 * nf, [fb])
-                at("pp")
-                vec(lambda F=F, X=X: v.tensor_tensor(xv(X, 6, 2), xv(X, 1, 2), F[:, 320:448], A.mult), [x0, ("h", xp)], [("pp", xp)], 128, [fb])
-            else:
-                at("h")
-                vec(lambda F=F, X=X: v.tensor_scalar(xv(X, 1, 4), F[:, 0:256], 0.0, 1.0, A.max, A.min), [x0], [("h", xp), ("rs", xp)], 256, [fb])
-                at("pp")
-                vec(lambda F=F, X=X: v.tensor_tensor(xv(X, 5, 3), xv(X, 0, 3), F[:, 256:448], A.mult), [x0, ("h", xp)], [("th", xp), ("pp", xp)], 192, [fb])
-            lst = [(T.BB[:, 0:64], xt(X, f, kh), T.IH[:, kh::2], False, False, 64) for f in (1, 2, 5) for kh in range(2)]
-            if last:
-                lst = [(T.BB[:, 0:64], T.ONE[:], T.C16[:], False, False, 64)] + lst
-            lst[0] = lst[0][:3] + (True, False, 64)
-            lst[-1] = lst[-1][:3] + (False, True, 64)
-            at("bb")
-            mm(lst, ["ONE", "C16", "IH", x0, ("h", xp), ("th", xp)], ["BB"])
-            xk = ["IN", "IP", x0, ("rs", xp), ("pp", xp)]
+                act(lambda F=F, X=X, nf=nf: s.activation(xv(X, 2, nf), F[:, 128:128 + 64 * nf], M.Relu), [x0], [("rs", p)], 64 * nf, [fb])
             if not last:
+                at("bb")
+                mm([(BB[:, 0:64], xt(X, 4, bit), T.IH[:, bit::2], 64) for bit in range(2)], ["IH", x0, ("th", p)], [bb], last=False)
+                mm([(BB[:, 0:64], xt(X, f, bit), T.IH[:, bit::2], 64) for f in (0, 1) for bit in range(2)], ["IH", x0, ("h", p)], [bb], first=False)
                 at("out")
-                vec(lambda n=n: v.tensor_scalar(T.OUT[:, n * 64:n * 64 + 64], T.BB[:, 0:64], 2048.0, None, A.add), [], [("OUT", n)], 64, ["BB"])
-                send(T.MSG[:, n * 64:n * 64 + 64], [T.OUT[:, n * 64:n * 64 + 64]], to_next, "m%d" % n, [("OUT", n)], [("MSG", n)])
-                at("ob")
-                if cost["sp"]:
+                ts(T.OUT[:, n * 64:n * 64 + 64], BB[:, 0:64], 2048.0, None, (A.add,), [], [("OUT", n)], 64, [bb])
+                i = post(T.MSG[:, n * 64:n * 64 + 64], [T.OUT[:, n * 64:n * 64 + 64]], "next", "m%d" % n, [("OUT", n)], [("MSG", n)])
+                if not cost["sv"]:
                     at("os")
-                    mm([(T.OB[:, l0:l0 + 64], T.ID[:], o1, True, False, 64)]
-                       + [(T.OB[:, l0 + kl:l0 + 64:8], T.GT[:, w0 + kl:w0 + 1024:8], row(5), False, False, 64) for kl in range(8)],
-                       ["ID", ("OIN", n)] + gk, ["OB"])
-                    at("ob")
-                    mm([(T.OB[:, l0:l0 + 64], (T.IN if f == 3 else T.IP)[:], xv(X, f), False, f == 7, 64) for f in (3, 6, 7)], xk, ["OB"])
+                    mm([(OB[:, 0:64], T.ID[:], o1, 64)] + [(OB[:, i:64:8], T.GT[:, s0 + i:s0 + 1024:8], row(5), 64) for i in range(8)],
+                       ["ID", ("OIN", n)] + gk, [ob], last=False)
+                at("ob")
+                mm([(OB[:, 0:64], m[:], xv(X, f), 64) for f, m in ((2, T.IN), (3, T.IH), (5, T.IH), (6, T.IH)) if f != 3 or cost["sv"]],
+                   ["IN", "IH", "IP", x0, ("rs", p), ("pp", p)], [ob], first=bool(cost["sv"]))
+                at("oo")
+                if cost["ooa"]:
+                    act(lambda n=n, OB=OB: s.activation(T.OOUT[:, n * 64:n * 64 + 64], OB[:, 0:64], M.Copy), [], [("OOUT", n)], 64, [ob])
                 else:
-                    mm([(T.OB[:, l0:l0 + 64], (T.IN if f == 3 else T.IP)[:], xv(X, f), f == 3, f == 7, 64) for f in (3, 4, 6, 7)], xk, ["OB"])
+                    vec(lambda n=n, OB=OB: v.tensor_copy(T.OOUT[:, n * 64:n * 64 + 64], OB[:, 0:64]), [], [("OOUT", n)], 64, [ob])
                 og = cost["og"]
                 if c % og == og - 1:
-                    a, b = (c + 1 - og) * 64, (c + 1) * 64
-                    at("oo")
-                    act(lambda t=t, a=a, b=b: s.activation(T.OOUT[:, t * 256 + a:t * 256 + b], T.OB[:, a:b], M.Copy),
-                        [], [("OOUT", n)], b - a, ["OB"])
-                    send(T.OIN[:, (t + 1) * 256 + a:(t + 1) * 256 + b], [T.OOUT[:, t * 256 + a:t * 256 + b]], to_next, "o%d" % n,
-                         [("OOUT", n)], [("OIN", k + NCH) for k in range(n + 1 - og, n + 1)], after=calls["m%d" % n])
+                    a, b = (n + 1 - og) * 64, (n + 1) * 64
+                    omsg[0] = post(T.OIN[:, a + 256:b + 256], [T.OOUT[:, a:b]], "next", "o%d" % n, [("OOUT", k) for k in range(n + 1 - og, n + 1)],
+                                   [("OIN", k + NCH) for k in range(n + 1 - og, n + 1)], after=i)
             else:
+                y0 = 2 * l0
+
+                def back(out, fields):
+                    return [(out[:, 0:128], xt(X, f, bit), (T.MN if f == 2 else T.MV)[:, bit * 128:bit * 128 + 128], 128)
+                            for f in fields for bit in range(2)]
+                at("ym")
+                short = True
+                for out, const, bank in ((BB, T.PB, bb), (OB, T.PO, ob))[:1 + short]:
+                    mm([(out[:, 0:128], T.PA[:], const[:], 128)], MVK, [bank], last=False)
+                at("bb")
+                mm(back(BB, (4,)), MVK + [x0, ("th", p)], [bb], first=False, last=False)
+                mm(back(BB, (0, 1)), MVK + [x0, ("h", p)], [bb], first=False)
                 at("ob")
-                mm([(T.OB[:, l0:l0 + 64], xt(X, f, kh), (T.IN if f == 3 else T.IP)[:, kh::2], (f, kh) == (3, 0), (f, kh) == (7, 1), 64)
-                    for f in (3, 4, 6, 7) for kh in range(2)], xk, ["OB"])
-                y0 = c * 128
-                at("zw")
-                vec(lambda: v.tensor_scalar(T.ZW[:], T.BB[:, 0:64], float(V), -float(V), A.is_ge, A.mult), [], ["ZW"], 64, ["BB"])
+                if short:
+                    mm(back(OB, (2, 3)), MVK + [x0, ("rs", p)], [ob], first=False, last=False)
+                    mm(back(OB, (5, 6)), MVK + [x0, ("pp", p)], [ob], first=False)
+                else:
+                    mm([(OB[:, 256:320], m[:], xv(X, f), 64) for f, m in ((2, T.IN), (3, T.IH), (5, T.IH), (6, T.IH))],
+                       ["IN", "IH", x0, ("rs", p), ("pp", p)], [ob])
+                    at("oo")
+                    vec(lambda OB=OB, X=X: v.tensor_copy(xv(X, 3), OB[:, 256:320]), [x0], [("rs", p)], 64, [ob])
+                    at("ob")
+                    mm([(OB[:, 0:128], T.PA[:], T.PO[:], 128)] + back(OB, (3,)), MVK + [x0, ("rs", p)], [ob])
                 at("y")
-                act(lambda y0=y0, l0=l0: s.activation(T.YO[:, y0 + 64:y0 + 128], T.OB[:, l0:l0 + 64], M.Identity, bias=-1.0),
-                    [], [("YO", c, 1)], 64, ["OB"])
-                vec(lambda y0=y0: v.tensor_tensor(T.YO[:, y0:y0 + 64], T.ZW[:], T.BB[:, 0:64], A.add), ["ZW"], [("YO", c, 0)], 64, ["BB"])
-                send(T.YI[:, y0:y0 + 128], [T.YO[:, y0:y0 + 128]], to_prev, "y%d" % c,
-                     [("YO", c, 0), ("YO", c, 1)], [("YI", c)], more=500.0)
+                vec(lambda BB=BB: v.transpose(T.ZB[:], BB[:, 0:128]), [], ["ZB"], 128, [bb])
+                tt(T.YN[:, 0:64], T.ZB[:, :, 0:16], T.ZB[:, :, 16:32], A.max, ["ZB"], [("YN", 0)], 128)
+                vec(lambda OB=OB: v.transpose(T.ZO[:], OB[:, 0:128]), [], ["ZO"], 128, [ob])
+                ts(T.YN[:, 64:128], T.YN[:, 0:64], V - 1, None, (A.bitwise_and,), [("YN", 0)], [("YN", 1)], 64)
+                tt(T.YO[:, y0 + 64:y0 + 128], T.ZO[:, :, 0:16], T.ZO[:, :, 16:32], A.max, ["ZO"], [("YO", c, 1)], 128)
+                vec(lambda y0=y0: v.tensor_copy(T.YO[:, y0:y0 + 64], T.YN[:, 64:128]), [("YN", 1)], [("YO", c, 0)], 64)
+                post(T.YI[:, y0:y0 + 128], [T.YO[:, y0:y0 + 128]], "prev", "y%d" % c, [("YO", c, 0), ("YO", c, 1)], [("YI", c)], more=300.0)
                 dma(T.yb[:, l0:l0 + 64], T.YI[:, y0:y0 + 64], [("YI", c)], [], 32768, sem="outs")
-                at("ys" if c == NCH - 1 else "y")
-                dma(T.yo[:, l0:l0 + 64], T.YI[:, y0 + 64:y0 + 128], [("YI", c)], [], 32768,
-                    q="A" if c == NCH - 1 else "S", sem="outs")
-        if t >= 2:
-            e = t - 2
-            srcs = [T.PK[:, t * 256:(t + 1) * 256]]
-            rd = [("PK", t)]
-            if t >= 3:
-                srcs.append(T.EIN[:, (e - 1) * 256:e * 256])
-                rd.append(("EIN", e - 1))
-            if t >= 4:
-                srcs.append(T.PK[:, (t - 4) * 256:(t - 3) * 256])
-                rd.append(("PK", t - 4))
+                dma(T.yo[:, l0:l0 + 64], T.YI[:, y0 + 64:y0 + 128], [("YI", c)], [], 32768, q="A" if c == NCH - 1 else "S", sem="outs")
+                if c < 2 and PAIR:
+                    if c == 1:
+                        at("fold")
+                        i = send(T.HE[:, 2304:2432], [W[:, k * 128:(k + 1) * 128] for k in range(16)], "pair", "f%d" % NF,
+                                 [("W", j, k) for j in (n - 1, n) for k in range(16)], after=omsg[0])
+                        arrive(i, "e6", [("EIN", 9)], peers["back"][t], 1.8 * cost["lat"])
+                        ops[-1]["hold"] = 0.65 * cost["fold"]
+                    continue
+                at("tree")
+                tt(T.TR[:, s0:s0 + 512], wv(0, 8), wv(8, 16), A.max, wk, [("TR", p, 8)], 512)
+                a = s0
+                for k in (4, 2, 1):
+                    b = a + 128 * k
+                    tt(T.TR[:, b:b + k * 64] if k > 1 else T.PK[:, l0:l0 + 64], T.TR[:, a:a + k * 64], T.TR[:, a + k * 64:a + k * 128], A.max,
+                       [("TR", p, 2 * k)], [("TR", p, k) if k > 1 else ("PK", c)], k * 64)
+                    a = b
+
+        if not last:
+            at("fold")
+            side = SIDE if t else 0
+            wall = [("W", t * NCH + c, k) for c in range(NCH) for k in range(16)]
+            i = send(T.HE[:, t * 256:(t + 1) * 256], [W[:, k * 256:(k + 1) * 256] for k in range(side, 16)], "help", "f%d" % t, wall)
+            arrive(i, "e%d" % t, [("EIN", t)], peers["back"][t], 1.6 * cost["lat"], kind="fold")
+            ops[-1]["fold"] = (16 - side) / 16
+            if side:
+                at("side")
+                i = send(T.HE[:, (4 + t) * 256:(5 + t) * 256], [W[:, k * 256:(k + 1) * 256] for k in range(side)], "pair", "g%d" % t, wall)
+                arrive(i, "b%d" % t, [("EIN", 4 + t)], peers["back"][t], 1.8 * cost["lat"])
+                ops[-1]["hold"] = side / 16 * cost["fold"]
+        else:
             at("e")
-            send(T.EIN[:, e * 256:(e + 1) * 256], srcs, to_prev if last else to_next, "e%d" % e, rd, [("EIN", e)], more=1500.0)
-    now[0] -= 2
-    dma(T.ye[:], T.EIN[:, 768:1024], [("EIN", 3)], [], 65536, sem="outs")
+            a = 128 if PAIR else 0
+            post(T.EIN[:, 2304 + a:2560], [T.PK[:, a:256]], "prev", "e5", [("PK", c) for c in range(a // 64, NCH)], [("EIN", 10)] + [("EIN", 9)] * (a == 0))
+            at("em")
+            if SIDE:
+                tt(T.YE[:, 0:512], T.EIN[:, 0:512], T.EIN[:, 1280:1792], A.max, [("EIN", j) for j in (0, 1, 5, 6)], [("YE", 0)], 512)
+                tt(T.YE[:, 512:1024], T.EIN[:, 512:1024], T.EIN[:, 1792:2304], A.max, [("EIN", j) for j in (2, 3, 7, 8)], [("YE", 1)], 512)
+                tt(T.YE[:, 0:512], T.YE[:, 0:512], T.YE[:, 512:1024], A.max, [("YE", 0), ("YE", 1)], [("YE", 0)], 512)
+            else:
+                tt(T.YE[:, 0:512], T.EIN[:, 0:512], T.EIN[:, 512:1024], A.max, [("EIN", j) for j in range(4)], [("YE", 0)], 512)
+            tt(T.YE[:, 512:768], T.YE[:, 0:256], T.YE[:, 256:512], A.max, [("YE", 0)], [("YE", 1)], 256)
+            at("ef")
+            for c in range(NCH):
+                src = T.EIN[:, 2304 + c:2432:2] if c < 2 and PAIR else T.EIN[:, 2304 + c * 64:2368 + c * 64]
+                tt(T.YE[:, c * 64:c * 64 + 64], T.YE[:, 512 + c:768:NCH], src, A.max, [("YE", 1), ("EIN", 9 + c // 2)], [("YE", 2, c)], 64)
+            for c in range(NCH):
+                tt(T.YE[:, 256 + c * 64:320 + c * 64], T.YE[:, c * 64:c * 64 + 64], T.EIN[:, 1024 + c:1280:NCH], A.max,
+                   [("YE", 2, c), ("EIN", 4)], [("YE", 3, c)], 64)
+            dma(T.ye[:], T.YE[:, 256:512], [("YE", 3, c) for c in range(NCH)], [], 65536, sem="outs")
     return ops
 
 
@@ -454,91 +650,54 @@ def link(ops):
             ops[j]["deps"].append((i, False))
 
 
-def plan(ops, cost):
-    n = len(ops)
-    succ = [[] for _ in range(n)]
+def lines(ops, order):
+    left = {}
     for o in ops:
-        for j, w in o["deps"]:
-            succ[j].append((o["i"], w))
-    tail = [0.0] * n
-    for o in reversed(ops):
-        x = o["dur"] + o["lat"] + (cost["dma0"] if o["kind"] == "dma" else 0.0)
-        tail[o["i"]] = max([tail[j] + (x + cost["hop"] if w or not ops[j]["eng"] else o["dur"]) for j, w in succ[o["i"]]] + [x])
-    tau = cost["tau"]
-    for o in ops:
-        k = (o["eng"] or "") + (o["tag"] or "")
-        if cost.get("early") and (o["n"] is None or o["tag"] == "tab" or o["n"] < NCH and k + str(o["n"]) not in cost["early"]):
-            o["tau"] = None
-            tail[o["i"]] += cost["bias"].get(k, 0.0) + cost["bias"].get("%s%s" % (k, o["n"]), 0.0)
-        elif o["tag"] == "tab":
-            o["tau"] = tau["tab0"] + tau["tab1"] * o["n"]
-        elif o["n"] is None:
-            o["tau"] = tau.get(o["tag"])
-        elif o["n"] < NCH and o["tag"] in FRONT:
-            o["tau"] = tau["first0"] + tau["first1"] * o["n"] + tau.get(k, 0.0) + tau.get("first" + k, 0.0) + tau.get("late", 0.0) * (o["n"] >= tau.get("from", 9))
-        elif o["n"] < NCH:
-            o["tau"] = tau["back0"] + tau["back1"] * o["n"] + tau.get(k, 0.0)
-        elif o["n"] >= NM + NCH - 2 and o["tag"] not in FRONT:
-            o["tau"] = o["n"] + tau.get(k, 0.0) + tau.get("last" + k, 0.0)
-        else:
-            o["tau"] = o["n"] + tau.get(k, 0.0) + tau.get("o" + k, 0.0) * (o["n"] % 2)
-        if o["tau"] is not None:
-            o["tau"] += tau.get("%s%s" % (k, o["n"]), 0.0)
-    left = [len(o["deps"]) for o in ops]
-    done = [0.0] * n
-    free = {}
-    dmaq = [0.0]
-    ready = [i for i in range(n) if left[i] == 0]
-    out = []
-    heads = {}
-
-    def est(i):
-        o = ops[i]
-        x = free.get(o["eng"], 0.0) if o["eng"] else 0.0
-        for j, w in o["deps"]:
-            if w or not o["eng"]:
-                x = max(x, done[j] + (cost["hop"] if w else 0.0))
-        return x
-    while len(out) < n:
-        es = [(est(i), i) for i in ready if ops[i]["tau"] is None]
-        if es:
-            t0, i0 = min(es)
-            e0 = ops[i0]["eng"]
-            i = max([(tail[k], -k) for x, k in es if ops[k]["eng"] == e0 and x <= t0 + cost["look"]])[1] * -1
-        else:
-            if not heads:
-                for x, k in sorted((o["tau"], o["i"]) for o in ops if o["tau"] is not None and o["eng"])[::-1]:
-                    heads.setdefault(ops[k]["eng"], []).append(k)
-            i = min([(est(k), k) for k in ready if not ops[k]["eng"] or heads[ops[k]["eng"]][-1] == k])[1]
-            if ops[i]["eng"]:
-                heads[ops[i]["eng"]].pop()
-        ready.remove(i)
-        o = ops[i]
-        st = est(i)
-        if o["eng"]:
-            free[o["eng"]] = st + o["dur"]
-        if o["kind"] == "dma":
-            dmaq[0] = max(dmaq[0], st + o["dur"]) + o["lat"]
-            done[i] = dmaq[0] + cost["dma0"]
-        else:
-            done[i] = st + o["dur"] + o["lat"]
-        o["st"] = st
-        out.append(i)
-        for j, w in succ[i]:
-            left[j] -= 1
-            if left[j] == 0:
-                ready.append(j)
-    return out, max(done)
+        left.setdefault((o["eng"], o["tag"], o["n"]), []).append(o["i"])
+    out = {}
+    for e, (first, turn, final) in order["queues"].items():
+        words = [(w, 0) for w in first.split()]
+        words += [(w, n) for n in range(*order["turns"]) for w in turn.split()] + [(w, 0) for w in final.split()]
+        out[e] = []
+        for w, n in words:
+            w, _, k = w.partition(".")
+            tag = w.rstrip("-0123456789")
+            calls = left.get((e, tag, n + int(w[len(tag):] or 0)), [])
+            k = int(k or len(calls))
+            out[e] += calls[:k]
+            del calls[:k]
+    out["S"] = [o["i"] for o in ops if o["eng"] == "S"]
+    assert sum(len(x) for x in out.values()) == len([o for o in ops if o["eng"]]), [k for k, x in left.items() if x and k[0] not in ("S", None)]
+    return out
 
 
-def emit(g, T, ops, order, engines):
+def merge(ops, line):
+    done, out, at = [False] * len(ops), [], {e: 0 for e in line}
+    landing = {o["after"]: o["i"] for o in ops if not o["eng"]}
+    while len(out) < len(ops):
+        n = len(out)
+        for e in line:
+            while at[e] < len(line[e]) and all(done[j] for j, w in ops[line[e][at[e]]]["deps"]):
+                i = line[e][at[e]]
+                at[e] += 1
+                for k in (i, landing.get(i)):
+                    if k is not None:
+                        done[k] = True
+                        ops[k]["st"] = len(out)
+                        out.append(k)
+        if len(out) == n:
+            raise ValueError([(e, ops[line[e][at[e]]]["tag"], ops[line[e][at[e]]]["n"]) for e in line if at[e] < len(line[e])])
+    return out
+
+
+def emit(g, T, ops, order):
     queue = {"A": g.scalar, "V": g.vector, "P": g.tensor, "G": g, "S": g.sync}
     know = {e: {} for e in queue}
     count = {}
     for i in order:
         o = ops[i]
-        if o["kind"] == "arr":
-            o["mark"], o["know"] = (o["sem"], engines), {o["sem"]: engines}
+        if not o["eng"]:
+            o["mark"], o["know"] = (o["sem"], o["inc"]), {o["sem"]: o["inc"]}
             continue
         e = o["eng"]
         need = {}
@@ -555,7 +714,7 @@ def emit(g, T, ops, order, engines):
                         know[e][k] = x
         ins = o["fn"]()
         if o["kind"] == "send":
-            count["sent"] = count.get("sent", 0) + engines
+            count["sent"] = count.get("sent", 0) + o["inc"]
             continue
         sem, inc = (o["sem"], 16) if o["kind"] == "dma" else ("c" + e, 1)
         for x in ins:
@@ -568,19 +727,46 @@ def emit(g, T, ops, order, engines):
         g.wait_ge(T.sem[sem], count[sem])
 
 
+def way(topo, src, dst, mask=None):
+    assert topo.may_write(src, dst)
+    rid, pid, _ = topo.addr(dst)
+    mask = topo.mask(src, dst) if mask is None else mask
+    return rid, pid, mask, len([e for e in topo.engines(src, dst) if mask >> e & 1])
+
+
+def helper_of(T, topo, rank):
+    core = T.cores[rank]
+    return [c for c in topo.cores_of(core) if T.rank_of(c) is None and topo.die(c) == topo.die(core)
+            and all(topo.may_write(c, other) for other in T.cores)][0]
+
+
+def fold_mask(T, topo, rank):
+    core = T.cores[rank]
+    return topo.mask(core, helper_of(T, topo, rank)) & ~topo.mask(core, T.cores[(rank + 1) % len(T.cores)])
+
+
 def rank_program(g, core, T, topo):
+    n = len(T.cores)
     rank = T.rank_of(core)
     if rank is None:
+        for q in range(n):
+            if helper_of(T, topo, q) == core:
+                main = way(topo, T.cores[q], core, fold_mask(T, topo, q))[3]
+                side, sent = way(topo, T.cores[q], T.cores[(q + 1) % n])[3], 0
+                jobs = [(0, "f0", main, "e0", 0, 256)]
+                for t in range(1, NF):
+                    jobs += [(t, "g%d" % t, side, "b%d" % t, (4 + t) * 256, 256)] * (SIDE > 0) + [(t, "f%d" % t, main, "e%d" % t, t * 256, 256)]
+                for t, landed, count, sem, a, width in jobs + [(NF, "f%d" % NF, side, "e6", 2304, 128)] * PAIR:
+                    rid, pid, mask, engines = way(topo, core, T.cores[(q - t) % n])
+                    g.wait_ge(T.sem[landed], count)
+                    g.remote_dma(T.EIN[:, a:a + width], T.HE[:, a:a + width], T.sem[sem], T.sem.sent, pid, rid, mask)
+                    sent += engines
+                g.wait_ge(T.sem.sent, sent)
         return
-    n = len(T.cores)
-    peers = []
-    for other in (T.cores[(rank + 1) % n], T.cores[(rank - 1) % n]):
-        assert topo.may_write(core, other)
-        rid, pid, _ = topo.addr(other)
-        peers.append((rid, pid, topo.mask(core, other)))
-    engines = len(topo.engines(core, T.cores[(rank + 1) % n]))
-    assert engines == len(topo.engines(core, T.cores[(rank - 1) % n]))
-    ops = build(g, T, peers[0], peers[1], COST)
+    peers = dict(next=way(topo, core, T.cores[(rank + 1) % n]), prev=way(topo, core, T.cores[(rank - 1) % n]),
+                 help=way(topo, core, helper_of(T, topo, rank), fold_mask(T, topo, rank)),
+                 pair=way(topo, core, helper_of(T, topo, rank), topo.mask(core, T.cores[(rank + 1) % n])),
+                 back=[way(topo, helper_of(T, topo, (rank + t) % n), core)[3] for t in range(STEPS)])
+    ops = build(g, T, peers, COST)
     link(ops)
-    order, _ = plan(ops, COST)
-    emit(g, T, ops, order, engines)
+    emit(g, T, ops, merge(ops, lines(ops, ORDER)))

@@ -4,8 +4,9 @@ from concourse.mybir import AluOpType, ActivationFunctionType
 V, STEPS, NCH = 4096, 6, 4
 NM = (STEPS - 1) * NCH
 NF = STEPS - 1
-SIDE = 2
-PAIR = 1
+SIDE = (0, 2, 2, 2, 2)
+NL = 2
+LAST = "pair"
 BIG = 12582912.0
 BF, F32, I32, U16, F16 = "bfloat16", "float32", "int32", "uint16", "float16"
 
@@ -14,203 +15,72 @@ SCRATCH = {
     "RLI": ("sbuf", [128, 256], I32), "RLB": ("sbuf", [128, 256], BF), "RLL": ("sbuf", [128, 256], BF),
     "CBI": ("sbuf", [128, 256], I32), "COI": ("sbuf", [128, 256], I32), "L0": ("sbuf", [128, 256], U16),
     "CY": ("sbuf", [128, 16, 32], F16), "CZ": ("sbuf", [128, 16, 32], F16), "CS": ("sbuf", [128, 16, 16], F16),
-    "OY": ("sbuf", [128, 16, 32], F16), "OZ": ("sbuf", [128, 16, 32], F16), "OS": ("sbuf", [128, 16, 16], F16),
+    "OY": ("sbuf", [128, 16, 32], F16), "OZ": ("sbuf", [128, 16, 32], F16),
     "COX": ("sbuf", [128, 520], BF),
     "DMI": ("sbuf", [128, 2, 16, 16], I32), "DMR": ("sbuf", [128, 16, 32], F16),
     "DMU": ("sbuf", [128, 16, 32], F16), "DMZ": ("sbuf", [128, 512], U16),
     "OMI": ("sbuf", [128, 512], I32), "OMB": ("sbuf", [128, 512], BF),
-    "PI": ("sbuf", [128, 128], F32), "PC": ("sbuf", [128, 4], I32), "PD": ("sbuf", [128, 4], I32), "PG": ("sbuf", [128, 4], I32),
-    "PF": ("sbuf", [128, 4], F32), "MK": ("sbuf", [128, 4], F32), "LO": ("sbuf", [128, 256], BF), "HI": ("sbuf", [128, 256], BF),
-    "ID": ("sbuf", [128, 128], BF), "IB": ("sbuf", [128, 16, 8], BF), "IF": ("sbuf", [128, 128], F32), "IS": ("sbuf", [128, 128], BF),
-    "IH": ("sbuf", [128, 128], F16), "IN": ("sbuf", [128, 128], F16), "IP": ("sbuf", [128, 128], F16),
+    "PC": ("sbuf", [128, 4], I32), "PG": ("sbuf", [128, 4], I32), "PD": ("sbuf", [128, 4], I32), "MK": ("sbuf", [128, 4], F32),
+    "LO": ("sbuf", [128, 256], BF), "HI": ("sbuf", [128, 256], BF),
+    "IB": ("sbuf", [128, 16, 8], BF), "IF": ("sbuf", [128, 128], F32), "IH": ("sbuf", [128, 128], F16),
     "ZR": ("sbuf", [128, 1024], BF), "SEL": ("sbuf", [128, 144], BF), "FS": ("sbuf", [128, 64], BF),
-    "TI": ("sbuf", [128, 256], F32), "MV": ("sbuf", [128, 256], F16), "MN": ("sbuf", [128, 256], F16), "MP": ("sbuf", [128, 256], F16),
+    "MV": ("sbuf", [128, 256], F16), "MW": ("sbuf", [128, 256], F16),
     "PA": ("sbuf", [128, 4, 32], BF), "PB": ("sbuf", [128, 4, 32], BF), "PO": ("sbuf", [128, 4, 32], BF),
     "X0": ("sbuf", [128, 113, 8], F16), "X1": ("sbuf", [128, 113, 8], F16),
     "IND": ("sbuf", [128, 2048], BF), "GT": ("sbuf", [128, 2048], BF), "TR": ("sbuf", [128, 2048], BF),
     "B": ("sbuf", [128, 256], F32), "IDX": ("sbuf", [128, 256], U16),
     "MSG": ("sbuf", [128, NM * 64], U16), "OUT": ("sbuf", [128, NM * 64], U16),
     "OIN": ("sbuf", [128, STEPS * NCH * 64], BF), "OOUT": ("sbuf", [128, NM * 64], BF),
-    "PK": ("sbuf", [128, 256], BF), "EIN": ("sbuf", [128, 2560], BF), "HE": ("sbuf", [128, 2432], BF), "YE": ("sbuf", [128, 1024], BF),
-    "ZB": ("sbuf", [128, 4, 32], F32), "ZO": ("sbuf", [128, 4, 32], F32), "YN": ("sbuf", [128, 128], I32),
-    "YO": ("sbuf", [128, 512], F32), "YI": ("sbuf", [128, 512], F32),
+    "OP": ("sbuf", [128, NM // 2, 3, 2, 64], BF),
+    "PK": ("sbuf", [128, 256], BF), "EIN": ("sbuf", [128, 2560], BF), "HE": ("sbuf", [128, 2560], BF), "YE": ("sbuf", [128, 1024], BF),
+    "YS": ("sbuf", [128, 512], F32), "YR": ("sbuf", [128, 512], F32),
+    "ZB": ("sbuf", [128, 4, 4, 32], F32), "YO": ("sbuf", [128, 256], I32), "YI": ("sbuf", [128, 256], I32),
+    "YN": ("sbuf", [128, 512], I32), "YF": ("sbuf", [128, 512], F32),
     "JB0": ("psum", [128, 512], F32), "JB1": ("psum", [128, 512], F32), "BB0": ("psum", [128, 512], F32), "BB1": ("psum", [128, 512], F32),
     "F0": ("psum", [128, 512], F32), "F1": ("psum", [128, 512], F32), "OB0": ("psum", [128, 512], F32), "OB1": ("psum", [128, 512], F32),
 }
 SCRATCH.update({"W%d" % t: ("sbuf", [128, V], BF) for t in range(STEPS)})
-SEMAPHORES = (["cA", "cV", "cP", "cG", "sent", "outs", "a_rl"] + ["d%d" % i for i in range(36)]
+SEMAPHORES = (["cA", "cV", "cP", "cG", "sent", "outs", "a_rl", "go"] + ["d%d" % i for i in range(36)]
               + ["m%d" % n for n in range(NM)] + ["o%d" % n for n in range(NM)] + ["y%d" % c for c in range(NCH)]
               + ["e%d" % t for t in range(STEPS + 1)] + ["f%d" % t for t in range(STEPS)]
               + ["g%d" % t for t in range(1, NF)] + ["b%d" % t for t in range(1, NF)])
 
-COST = dict(r=1.4, f=1.0, ov=5.0, ova=30.0, pe=0.63, hop=70.0, lat=3300.0, first=2000.0, call=700.0, dma0=2000.0, dmab=0.0045,
-            fold=11000.0, loads="wdo|c", wa=10, ga=64, ooa=0, sv=0, zc=1, ne=2, jl=0, hr=0, cv=0, og=1, vs=4, rsa=(), cx={},
-            vx={0: 16, 1: 16, 2: 16, 3: 16, 23: 16}, wx={0: 8, 1: 16, 2: 16, 3: 16, 20: 12, 21: 12, 22: 14, 23: 8},
-            gx={0: 32, 1: 40, 23: 32}, ta="AVAVAVAV")
-COST.update(wa=9, vs=3, vx={0: 16, 1: 16, 2: 16, 3: 16, 20: 16, 21: 16, 22: 16, 23: 16}, wx={0: 8, 1: 16, 2: 16, 3: 16, 20: 12, 21: 13, 22: 13, 23: 11},
-            gx={0: 32, 1: 40, 23: 40}, rsa=(20, 21))
+COST = dict(wa=13, ga=46, wx={0: 8, 1: 16, 2: 16, 3: 16, 4: 10, 20: 13, 21: 13, 22: 14, 23: 11},
+            gx={0: 32, 1: 40, 2: 64, 3: 64, 20: 64, 21: 64, 22: 64, 23: 40}, ta="AVAVAVAV", gate=0, ra=3, pk=3, fa=1, dh=1, ne=3)
 ORDER = dict(turns=(5, 20), queues=dict(
-    A=('setup mat fs late w0 w1 w2 tab.2 tw tab w3 co gt0 gt1 gt2 w4 gt3',
-       'w0 gt-1',
-       'w20 gt19 w21 gt20 w22 gt21 rs20 w23 gt22 rs21 gt23 y23'),
-    V=('setup mat rl cb fs x b1 late w0 dm.4 b0 dm.1 om.1 dm.5 c0.1 dm.2 cw0 om.1 dm.3 om.1 dm.2 om dm c0 cw1 tab co.2 idx0 b2 co.1 cw2 co c1 c2.1 gt0 c2 th0 h0 rs0 idx1 cw3 out0 b3 gt1 idx2 c3.1 th1 pp0 h1 c3 out1 pp1 idx3 oo0 rs1 th2 h2 rs2 pp2 out2 w4 wb4 b4 c4.1 oo1 cw4 c4',
-       'oo-3 wb0 th-2 h-2 b0 idx-1 pp-2 rs-2 out-2 w0 cw0 c0',
-       'oo17 w20 th18 h18 b20 idx19 rs18 out18 pp18 cw20 c20 oo18 w21 th19 h19 b21 idx20 pp19 out19 rs19 c21.1 cw21 oo19 c21 w22 b22 h20 th20 pp20 idx21 c22.1 cw22 c22 tree22.1 b23 y20.1 tree22.1 y20.1 w23 h21 th21 idx22 pp21 y20.1 c23.1 cw23 c23 y20.1 y21.1 tree23.1 y21.1 y20 idx23 th22 h22 gt23 pp22 y21.1 rs22 tree22.1 y21.1 y22.1 y21 th23 y22.1 tree23.1 h23 y22 rs23 tree22 pp23 tree23.1 y23.1 tree23 y23 em23 ef23'),
-    P=('jb0 jb1 vote0 jb2 co vote1 vote2.1 oa0 f0 oa1 bb0 vote2 os0 f1 jb3 vote3.1 bb1 oa2 ob0 vote3 f2 os1 bb2 os2 oa3 ob2 ob1 jb4 vote4.1 f3 vote4',
-       'bb-2 oa-1 os-2 ob-2 jb0 vote0.1 f-1 vote0',
-       'bb18 os18 ob18 jb20 oa19 vote20.1 f19 vote20 bb19 jb21 os19 oa20 ym20 ob19 vote21.1 f20 vote21 bb20.1 oa21 jb22 vote22.1 bb20 vote22 ob20.1 f21 ym21.1 ob20 ym21 oa22 bb21.1 ym22.1 bb21 jb23 vote23 ym23.1 f22 ob21 bb22.1 ym22 bb22 oa23 f23 ob22 ym23 bb23 ob23'),
-    G=('setup late rl fold3 out0 out1 oo0 out2 oo1',
-       'oo-3 out-2 fold0 side-1',
-       'oo17 out18 side19 out19 oo18 oo19 fold21 y20 y21 y22 e23 y23')))
-COST.update(og=2)
-ORDER = dict(turns=(5, 20), queues=dict(
-    A=('setup mat fs late w0 w2 w1 tab.3 tw tab w3 co gt0 gt1 gt2 w4 gt3',
-       'w0 gt-1',
-       'w20 gt19 w21 gt20 w22 rs20 gt21 w23 gt22 rs21 gt23 y23'),
-    V=('setup mat rl cb fs x late b0 w0 dm.4 b1 dm.1 om.1 dm.4 om.1 dm.6 c0.1 dm.2 om.1 dm.2 cw0 om dm.1 c0 dm c1.1 tab co.2 cw1 co.1 cw2 co b2 idx0 c2.1 c1 gt0 b3 c2 th0 h0 cw3 idx1 out0 rs0 gt1 pp0 idx2 h1 th1 c3.1 out1 c3 pp1 rs1 h2 th2 pp2 oo0 idx3 oo1 w4 out2 wb4 b4 rs2 cw4 c4 oo2',
-       'wb0 th-2 h-2 b0 idx-1 pp-2 rs-2 out-2 w0 cw0 c0.1 oo-2 c0',
-       'h18 th18 w20 b20 idx19 out18 cw20 pp18 c20.1 rs18 c20 oo18 w21 b21 th19 rs19 h19 idx20 pp19 cw21 out19 c21 oo19 th20 h20 w22 b22 pp20 idx21 c22.1 cw22 c22 y20.1 tree22.1 y20.1 b23 idx22 w23 th21 h21 y20.1 tree22.1 y20.1 cw23 c23 y21.1 y20 pp21 y21.1 idx23 tree23.1 th22 h22 gt23 y21.1 rs22 y21 pp22 y22.1 tree23.1 y22 th23 rs23 tree23.1 h23 tree22.1 tree23 pp23 tree22 y23 em23 ef23'),
-    P=('jb0 jb1 vote0 vote1.1 jb2 co vote2.1 vote1 oa0 f0 oa1 bb0 vote2 os0 jb3 f1 ob0 oa2 bb1 os1 f2 vote3 ob1 bb2 os2 ob2 jb4 oa3 vote4.1 f3 vote4',
-       'bb-2 os-2 jb0 ob-2 oa-1 vote0.1 f-1 vote0',
-       'bb18 oa19 os18 jb20 vote20.1 ob18 f19 vote20 os19 bb19 ob19 oa20 ym20.1 jb21 f20 ym20 vote21 jb22 bb20 oa21 vote22 ob20.1 f21 ob20 jb23 ym21.1 bb21.1 oa22 bb21 vote23.1 ym22 vote23 ym21 f22 ob21.1 oa23 ob21 bb22 ob22 f23 ym23 bb23.1 ob23.1 bb23 ob23'),
-    G=('setup late rl fold3 out0 out1 oo1 out2',
-       'out-2 fold-1 oo-2',
-       'out18 fold19 out19 oo19 fold21 y20 y21 y22 e23 y23')))
-COST["wx"].update({20: 13, 21: 14, 22: 14, 23: 12})
-COST["rsa"] = (20, 21, 22)
-ORDER = dict(turns=(5, 20), queues=dict(
-    A=('setup mat fs late w0 w1 w2 tab.3 tw tab w3 co gt0 gt1 gt2 w4 gt3',
-       'w0 gt-1',
-       'w20 gt19 w21 gt20 w22 rs20 gt21 w23 gt22 rs21 gt23 rs22 y23'),
-    V=('setup mat rl cb fs x late w0 dm.4 b2 b0 dm.1 om.1 dm.2 b1 dm.3 c0.1 dm.7 om.1 dm.3 cw0 om cw1 dm c0 tab co.3 idx0 co c1.1 c2.1 c1 gt0 c2 th0 h0 idx1 cw2 pp0 out0 b3 gt1 rs0 idx2 c3.1 cw3 th1 h1 c3 pp1 out1 rs1 oo1 oo0 h2 rs2 pp2 th2 w4 b4 idx3 out2 wb4 cw4 c4.1 oo2 c4',
-       'wb0 th-2 h-2 b0 idx-1 pp-2 rs-2 out-2 w0 cw0 c0.1 oo-2 c0',
-       'b20 h18 th18 pp18 w20 idx19 out18 c20.1 rs18 cw20 c20 tree20.1 b21 th19 tree20.1 h19 idx20 w21 pp19 out19 rs19 cw21 tree20.1 c21 tree21.1 oo18 oo19 tree21.1 tree20 w22 h20 th20 idx21 b22 tree21.1 pp20 c22.1 cw22 c22 y20.1 tree21 tree22.1 idx22 b23 tree22.1 th21 w23 y20.1 h21 c23.1 cw23 pp21 y20.1 c23 tree23.1 y20.1 idx23 y20.1 gt23 h22 th22 y21.1 pp22 y20 y21.2 tree23.1 y22.1 y21 y22.1 tree23.1 y22.2 th23 rs23 y22 h23 tree22.1 pp23 tree22 y23.1 tree23 y23 em23 ef23'),
-    P=('jb1 jb0 vote0 co jb2 vote1.1 oa0 vote1 f0 oa1 bb0 vote2 os0 f1 oa2 bb1 jb3 os1 ob1 ob0 f2 vote3 bb2 os2 ob2 jb4 oa3 vote4.1 f3 vote4',
-       'bb-2 os-2 jb0 ob-2 oa-1 vote0.1 f-1 vote0',
-       'bb18 jb20 oa19 os18 vote20.1 f19 vote20 bb19 ob18 ym20.1 os19 jb21 ob19 vote21.1 oa20 vote21 f20 ym20 bb20 jb22 oa21 vote22.1 ob20.1 vote22 f21 ym21.1 ob20 ym21 bb21 jb23 ym22.1 vote23.1 oa22 ym22 vote23 f22 ob21.1 oa23 ob21 bb22 ob22 f23 ym23 bb23.1 ob23.1 bb23 ob23'),
-    G=('setup late rl fold3 out0 out1 oo1 out2',
-       'out-2 fold0 oo-2',
-       'out18 out19 oo19 y20 y21 y22 e23 y23')))
-COST["wx"].update({20: 12, 21: 13, 22: 13, 23: 11})
-COST["rsa"] = (20, 21)
-ORDER = dict(turns=(5, 20), queues=dict(
-    A=('setup mat fs late w0 w2 w1 tab.3 tw tab w3 co gt0 gt1 gt2 w4 gt3',
-       'w0 gt-1',
-       'w20 gt19 w21 gt20 w22 rs20 gt21 w23 gt22 rs21 gt23 y23'),
-    V=('setup mat rl cb fs x late b0 w0 dm.4 b1 dm.1 om.1 dm.4 om.1 dm.6 c0.1 dm.2 om.1 dm.2 cw0 om dm.1 c0 dm c1.1 tab co.2 cw1 co.1 cw2 co b2 idx0 c2.1 c1 gt0 b3 c2 th0 h0 cw3 idx1 out0 rs0 gt1 pp0 idx2 h1 th1 c3.1 out1 c3 pp1 rs1 h2 th2 pp2 oo0 idx3 oo1 w4 out2 wb4 b4 rs2 cw4 c4 oo2',
-       'wb0 th-2 h-2 b0 idx-1 pp-2 rs-2 out-2 w0 cw0 c0.1 oo-2 c0',
-       'h18 th18 w20 b20 idx19 out18 cw20 pp18 c20.1 rs18 c20 oo18 w21 b21 th19 rs19 h19 idx20 pp19 cw21 out19 c21 oo19 th20 h20 w22 b22 pp20 idx21 c22.1 cw22 c22 y20.1 tree22.1 y20.1 b23 idx22 w23 th21 h21 y20.1 tree22.1 y20.1 cw23 c23 y21.1 y20 pp21 y21.1 idx23 tree23.1 th22 h22 gt23 y21.1 rs22 y21 pp22 y22.1 tree23.1 y22 th23 rs23 tree23.1 h23 tree22.1 tree23 pp23 tree22 y23 em23 ef23'),
-    P=('jb0 jb1 vote0 vote1.1 jb2 co vote2.1 vote1 oa0 f0 oa1 bb0 vote2 os0 jb3 f1 ob0 oa2 bb1 os1 f2 vote3 ob1 bb2 os2 ob2 jb4 oa3 vote4.1 f3 vote4',
-       'bb-2 os-2 jb0 ob-2 oa-1 vote0.1 f-1 vote0',
-       'bb18 oa19 os18 jb20 vote20.1 ob18 f19 vote20 os19 bb19 ob19 oa20 ym20.1 jb21 f20 ym20 vote21 jb22 bb20 oa21 vote22 ob20.1 f21 ob20 jb23 ym21.1 bb21.1 oa22 bb21 vote23.1 ym22 vote23 ym21 f22 ob21.1 oa23 ob21 bb22 ob22 f23 ym23 bb23.1 ob23.1 bb23 ob23'),
-    G=('setup late rl out0 fold3 out1 oo1 out2',
-       'out-2 fold0 side-1 oo-2',
-       'out18 side19 out19 oo19 fold21 y20 y21 y22 e23 y23')))
-COST["rsa"] = ()
-ORDER = dict(turns=(5, 20), queues=dict(
-    A=('setup w0 w1 w2 tab.1 tw tab w3 gt0 gt1 gt2 w4 gt3',
+    A=('rp w0 w1 w2 tw tab w3 gt0 gt1 gt2 gt3 w4',
        'w0 gt-1',
        'w20 gt19 w21 gt20 w22 gt21 w23 gt22 gt23 y23'),
-    V=('mat.1 setup.2 mat.1 x.1 mat.2 setup.2 fs.3 setup.2 fs.1 rl late.1 fs.1 cb.2 mat.1 fs.1 mat.1 cb.1 late.1 setup cb.1 late.2 cb.2 late.1 cb.1 late.1 cb late x mat.1 b1 mat b0 fs b2 w0 dm.1 c0.1 dm.3 cw0 om.1 dm.1 c0 dm.2 om.1 dm.1 om.1 dm.7 om dm c1.1 tab co.2 cw1 cw2 idx0 co.1 c2.1 co.4 c1 b3 co gt0 c2 th0 h0 cw3 idx1 out0 pp0 gt1 rs0 idx2 th1 h1 c3.1 out1 c3 pp1 rs1 oo0 th2 h2 rs2 oo1 out2 w4 idx3 b4 wb4 pp2 cw4 c4.1 oo2 c4',
-       'wb0 th-2 h-2 b0 idx-1 pp-2 rs-2 out-2 w0 cw0 c0.1 oo-2 c0',
-       'th18 h18 w20 idx19 out18 pp18 b20 rs18 cw20 c20 th19 h19 rs19 pp19 idx20 out19 b21 oo18 w21 oo19 cw21 c21 b22 w22 rs20 h20 th20 idx21 pp20 c22 cw22 tree22.1 y20.1 b23 w23 h21 y20.1 th21 rs21 idx22 y20.1 cw23 c23 tree23.1 y21.1 y20.2 pp21 idx23 y20 y21.1 th22 rs22 h22 gt23 pp22 y21.1 tree22.1 y21 y22.1 tree23.1 y22.2 th23 y22.1 rs23 y22 h23 tree23.1 tree22.1 pp23 tree22 tree23 y23 em23 ef23'),
-    P=('jb0 jb1 vote0 vote1.1 jb2 co vote2.1 vote1 oa0 f0 bb0 os0 vote2 oa1 f1 oa2 bb1.1 jb3 bb1 os1 ob0 vote3.1 f2 ob1 bb2 vote3 os2 oa3 jb4 ob2 vote4.1 f3 vote4',
-       'bb-2 os-2 jb0 ob-2 oa-1 vote0.1 f-1 vote0',
-       'bb18 os18 oa19 jb20 ob18 vote20.1 f19 vote20 ym20.1 bb19 os19 ob19 ym21.1 oa20 ym20 jb21 ym21 vote21.1 f20 vote21 ob20.1 jb22 ob20 oa21 bb20 vote22.1 f21 vote22 jb23 ym22.1 bb21.1 oa22 ym22 bb21 vote23.1 ob21.1 vote23 f22 ob21 ob22.1 oa23 bb22 ob22 f23 ym23 bb23.1 ob23.1 bb23 ob23'),
-    G=('setup late rl out0 fold3 out1 oo1 out2',
-       'out-2 fold0 side-1 oo-2',
-       'out18 side19 out19 oo19 fold21 y20 y21 y22 e23 y23')))
-COST.update(wa=8, vs=4, wx={0: 8, 1: 16, 2: 14, 3: 10, 20: 9, 21: 10, 22: 12, 23: 10}, gx={0: 32, 1: 36, 2: 48, 23: 32})
-ORDER = dict(turns=(5, 20), queues=dict(
-    A=('setup w0 w1 w2 tw tab w3 gt0 gt1 gt2 w4 gt3',
-       'w0 gt-1',
-       'w20 gt19 w21 gt20 w22 gt21 w23 gt22 gt23 y23'),
-    V=('setup.1 mat.1 setup.1 mat.1 setup.1 x.1 mat.3 fs.1 mat.1 setup.2 late.1 setup.1 rl cb.2 mat.1 cb.2 late.1 fs.1 cb.1 fs.1 cb.2 fs.3 cb late.1 fs b1 setup b2 late.2 x mat b0 w0 dm.4 c0.1 dm.1 om.1 dm.6 w2 dm.1 b3 om.1 dm.1 late.1 dm.2 late dm.2 cw0 c0 dm c1.1 om.1 tab.3 om tab co.2 idx0 cw2 co.1 cw1 co.4 c2.1 c1 co gt0 idx1 c2 th0 h0 w3 out0 gt1 c3.1 idx2 rs0 pp0 rs1 th1 h1 cw3 c3 out1 pp1 gt2 th2 h2 oo1 rs2 oo0 out2 w4 b4 idx3 wb4 cw4 pp2 c4.1 oo2 c4',
-       'wb0 th-2 h-2 b0 idx-1 pp-2 rs-2 out-2 w0 cw0 c0.1 oo-2 c0',
-       'w20 th18 h18 b20 idx19 rs18 out18 cw20 c20 pp18 idx20 rs19 th19 h19 pp19 out19 oo18 w21 oo19 cw21 b21 c21 w22 b22 h20 rs20 th20 pp20 idx21 tree22.1 c22 cw22 y20.1 w23 rs21 th21 h21 y20.1 b23 y20.1 idx22 y20.1 c23.1 cw23 c23 pp21 y20.1 tree23.1 y21.1 tree22.1 y20 y21.1 h22 rs22 th22 pp22 idx23 y21.1 gt23 y21.1 y22.1 y21 y22.3 th23 y22 rs23 h23 tree23.1 tree22.1 tree23.1 pp23 tree23 tree22 y23 em23 ef23'),
-    P=('jb0 jb1 vote0 vote1.1 co.2 jb2 co vote1 vote2.1 oa0 f0 bb0 oa1 vote2 os0 f1 oa2 bb1 os1 ob1 jb3 f2 ob0 bb2 vote3 oa3 jb4 os2 ob2 vote4.1 f3 vote4',
-       'bb-2 os-2 jb0 ob-2 oa-1 vote0.1 f-1 vote0',
-       'bb18 jb20 os18 oa19 vote20 f19 ob18 ym20.1 bb19 os19 ob19 ym20 oa21 jb21 oa20 vote21.1 ym21.1 f20 vote21 ym21 ob20.1 bb20.1 ob20 jb22 bb20 f21 vote22 oa22 bb21 jb23 ym22.1 vote23.1 ob21 ym22 f22 vote23 oa23 bb22 ob22 f23 ym23 bb23.1 ob23.1 bb23 ob23'),
-    G=('setup late rl out0 fold3 out1 oo1 out2',
-       'out-2 fold0 side-1 oo-2',
-       'out18 side19 out19 oo19 fold21 y20 y21 y22 e23 y23')))
-COST.update(wa=10, vs=3, og=2, ta="AVAVAVAA", wx={0: 9, 1: 16, 2: 16, 3: 16, 20: 13, 21: 14, 22: 15, 23: 12}, gx={0: 32, 1: 44, 23: 44})
-ORDER = dict(turns=(5, 20), queues=dict(
-    A=('setup w0 w1 w2 tab.2 tw tab w3 gt0 gt1 gt2 gt3 w4',
-       'w0 gt-1',
-       'w20 gt19 w21 gt20 w22 gt21 w23 gt22 gt23 y23'),
-    V=('setup.1 mat.1 setup.1 mat.3 x.1 setup.1 late.1 setup.1 rl setup.2 fs.2 cb.2 mat.1 cb.1 mat.1 cb.1 mat.1 late.2 setup fs.1 cb.2 fs.1 late.1 cb x b0 late.2 mat b2 fs.1 late b1 dm.1 w0 dm.3 fs.1 c0.1 fs dm.1 cw0 dm.4 b3 dm om.1 cw1 om.1 c1.1 tab.1 co.1 c0 om.1 co.1 tab.1 c1 om idx0 tab co.1 cw2 co.2 idx1 co.2 c2 co gt0 c3.1 th0 h0 idx2 cw3 pp0 out0 gt1 rs0 c3 h1 th1 rs1 out1 oo0 idx3 pp1 th2 h2 pp2 oo1 rs2 out2 w4 wb4 b4 oo2 c4.1 cw4 c4',
-       'wb0 th-2 h-2 b0 idx-1 pp-2 out-2 w0 rs-2 cw0 c0 oo-2',
-       'w20 th18 h18 b20 idx19 out18 rs18 cw20 c20.1 pp18 c20 b21 th19 h19 w21 oo18 idx20 out19 rs19 cw21 pp19 c21.1 oo19 c21 b22 h20 w22 rs20 pp20 th20 idx21 tree22.1 c22.1 tree22.1 c22 y20.1 cw22 w23 y20.2 b23 h21 th21 idx22 y20.1 tree22.1 cw23 rs21 tree23.1 c23.1 y20.1 c23 y21.1 y20 pp21 rs22 y21.1 h22 th22 idx23 pp22 gt23 tree23.1 y21.2 y22.1 y21 y22.3 th23 h23 y22 rs23 pp23 tree23.1 y23.1 tree22 tree23 y23 em23 ef23'),
-    P=('jb0 vote0.1 jb1 vote0 jb2 vote1 co.2 jb3 co vote2 oa0 oa1 f0 bb0 vote3.1 os0 f1 ob0 oa2 bb1 vote3 os1 f2 os2 bb2.1 ob1 bb2 oa3 ob2 jb4 f3 vote4',
-       'bb-2 os-2 jb0 ob-2 oa-1 vote0.1 f-1 vote0',
-       'bb18 jb20 ym20.1 oa19 os18 ob18 f19 vote20 bb19 jb21 os19 ym20 ob19 oa20 oa21 f20 vote21 ym21.1 ob20.1 bb20.1 ym21 ob20 bb20 jb22 f21 ym22.1 vote22 oa22 bb21 jb23 ob21.1 vote23.1 f22 ym22 vote23 oa23 ob21 bb22 ob22 f23 ym23 bb23 ob23'),
-    G=('setup rl late out0 fold3 out1 oo1 out2',
-       'oo-3 out-2 fold0 side-1',
-       'oo17 out18 side19 out19 oo19 fold21 y20 y21 y22 e23 y23')))
-COST.update(wa=9, vs=4, ta="AVAVAVAV", wx={0: 8, 1: 16, 2: 16, 3: 16, 20: 12, 21: 13, 22: 14, 23: 11}, gx={0: 32, 1: 40, 23: 40})
-ORDER = dict(turns=(5, 20), queues=dict(
-    A=('setup w0 w1 w2 tab.1 tw tab w3 gt0 gt1 gt2 gt3 w4',
-       'w0 gt-1',
-       'w20 gt19 w21 gt20 w22 gt21 w23 gt22 gt23 y23'),
-    V=('late.1 mat.1 setup.1 mat.1 setup.2 mat.2 setup.2 mat.1 x.1 rl fs.1 x cb.2 fs.1 mat.1 fs.1 cb.1 mat.1 setup.1 mat cb.1 setup late.2 fs.1 late.1 cb fs.2 b0 b3 b1 late.1 b2 late.1 w0 dm.3 c0.1 dm.1 c0 cw0 om.1 dm.1 om.2 dm.3 c1.1 dm.1 idx0 dm om c1 tab co.2 cw1 fs co.1 c2.1 co.4 cw2 c2 idx1 co gt0 c3.1 th0 h0 late pp0 cw3 rs0 out0 idx2 gt1 c3 th1 h1 oo0 rs1 out1 pp1 idx3 th2 h2 oo1 rs2 pp2 out2 oo2 wb4 w4 b4 cw4 c4',
-       'b0 th-2 h-2 wb0 idx-1 out-2 w0 pp-2 rs-2 cw0 c0.1 oo-2 c0',
-       'b20 h18 th18 w20 idx19 out18 c20.1 rs18 pp18 cw20 c20 b21 oo18 th19 h19 w21 idx20 rs19 pp19 out19 c21.1 oo19 cw21 c21 w22 th20 h20 idx21 b22 rs20 pp20 y20.1 tree22.1 y20.1 cw22 c22.1 y20.1 c22 w23 b23 th21 tree22.1 h21 rs21 y20.1 idx22 pp21 cw23 tree23.1 c23.1 y21.1 c23 y20.1 tree23.1 y20 y21.2 th22 rs22 h22 idx23 y21.1 pp22 gt23 y22.1 y21 y22.4 th23 h23 y22 pp23 rs23 tree22.1 tree23 tree22 y23 em23 ef23'),
-    P=('jb1 jb0 vote0 vote1.1 jb2 vote1 co vote2.1 jb3 oa1 oa0 f0 vote2 bb0 os0 ob0 vote3.1 f1 oa2 bb1 vote3 os1 f2 ob1 os2 bb2.1 ob2 bb2 oa3 f3 jb4 vote4',
-       'bb-2 jb0 os-2 oa-1 ob-2 vote0.1 f-1 vote0',
-       'bb18 jb20 ym20.1 oa19 os18 ob18 vote20.1 f19 vote20 bb19.1 jb21 bb19 os19 ym20 ym21.1 ob19 oa20 vote21.1 oa21 f20 vote21 bb20 ob20 ym21 jb22 ym22.1 vote22.1 f21 oa22 vote22 bb21 ob21.1 jb23 ob21 vote23.1 oa23 ym22 f22 vote23 bb22 ob22.1 ym23.1 ob22 f23 ym23 bb23 ob23'),
-    G=('late.1 setup rl late out0 fold3 out1 oo1 out2',
+    V=('zr setup.1 sel.1 setup.1 rp setup.1 rl setup.1 cb.3 setup.1 sel cb setup b3 b0 b2 b1 '
+       'w0 dm.2 c0.2 dm.2 c0 dm.1 cw0 om.1 dm.2 c1.1 dm.5 om.1 co.1 cw1 dm om co.1 c1.1 co.1 tab.3 co.1 tab co.3 c1 c2.1 idx0 c2.1 cw2 idx1 co gt0 c2 c3.1 th0 h0 idx2 cw3 rs0 out0 gt1 c3 late.1 th1 h1 pp0 late out1 idx3 h2.1 oo0 pp1 h2 rs1 th2 oo1 pp2 rs2 out2 w4 oo2 b4 cw4 c4',
+       'th-2 h-2 w0 idx-1 pp-2 out-2 b0 c0.1 cw0 gt-1 c0.1 rs-2 c0 oo-2',
+       'w20 th18 h18 b20 rs18 idx19 pp18 out18 c20.1 cw20 c20.1 gt19 c20 oo18 th19 h19 b21 idx20 rs19 pp19 out19 w21 oo19 cw21 c21.2 w22 c21 b22 rs20 h20.1 th20.1 h20 idx21 pp20 cw22 th20 c22 y20.1 w23 b23 th21.1 h21 idx22 th21 y20 pp21 rs21 cw23 c23 y21.1 tree22.1 idx23 y21 tree22.1 th22.1 h22 th22 rs22 pp22 gt23 tree23.1 y22.1 th23 y22 h23 rs23 tree23.1 pp23 tree23.1 tree22.1 y23.1 tree23 tree22 y23.1 yo23.1 y23.1 yo23 y23 em23.2 un22.2 em23.1 un22.1 em23.1 un22 em23 ef23'),
+    P=('jb1 jb0 vote1.1 vote0 co.2 vote1.1 co.1 vote1 co jb2 vote2.2 jb3 f0 vote2 bb0 os0 vote3.1 f1 vote3 bb1 os1 ob0 f2 os2 ob1 bb2 ob2 f3 jb4 vote4',
+       'bb-2 jb0 os-2 vote0.1 ob-2 f-1 vote0',
+       'bb18 jb20 os18 ob18 vote20.2 f19 vote20 bb19 os19 ob19 jb21 ym20 vote21.1 ym21 f20 vote21 jb22 bb20 ob20 vote22.2 f21 vote22 bb21 ob21.2 jb23 ob21 vote23 ym22 f22 bb22 ob22 ym23 f23 bb23.1 ob23.1 bb23 ob23'),
+    G=('setup if rl cox mat fs x late out0 fold3 out1 oo1 out2',
        'out-2 fold0 oo-2 side-1',
-       'out18 side19 out19 oo19 fold21 y20 y21 y22 e23 y23')))
-COST.update(wa=12, vs=16, ga=52, ne=3, sv=1, ta="AVAVAVAV", vx={}, wx={0: 8, 1: 16, 2: 16, 3: 16, 4: 10, 20: 13, 21: 13, 22: 14, 23: 11},
-            gx={0: 32, 1: 40, 2: 64, 3: 64, 20: 64, 21: 64, 22: 64, 23: 40})
-ORDER = dict(turns=(5, 20), queues=dict(
-    A=('setup w0 w1 w2 tw tab w3 gt0 gt1 gt2 gt3 w4',
-       'w0 gt-1',
-       'w20 gt19 w21 gt20 w22 gt21 w23 gt22 gt23 y23'),
-    V=('mat.1 setup.1 mat.1 late.1 mat.1 x.1 mat.1 setup.2 fs.1 setup.1 mat.2 rl mat.1 cb.1 setup.1 cb.1 setup.1 fs.1 x cb.1 late.1 fs.1 cb.1 late.1 fs.1 late.1 cb.2 late.1 setup cb.1 fs.1 cb mat late.1 b2 b0 b1 b3 fs.1 w0 dm.3 c0.1 dm.1 c0.1 dm.1 c0 cw0 dm.2 om.2 cw1 om.1 dm.1 om dm idx0 c1.2 tab co.2 cw2 co.1 c1 co.4 c2.1 fs c2.1 co idx1 gt0 c2 c3.1 th0 h0 cw3 idx2 pp0 rs0 out0 gt1 c3 oo0 th1 h1 rs1 out1 pp1 idx3 late h2 th2 oo1 rs2 pp2 b4 oo2 out2 w4 c4.1 cw4 c4',
-       'w0 th-2 h-2 b0 rs-2 idx-1 pp-2 out-2 c0.1 cw0 c0.1 gt-1 c0 oo-2',
-       'w20 h18 th18 rs18 pp18 idx19 out18 b20 cw20 c20.1 oo18 c20.1 gt19 c20 w21 b21 h19 th19 idx20 pp19 rs19 out19 c21.1 oo19 cw21 c21 w22 b22 th20 h20 rs20 idx21 pp20 cw22 c22 tree22.1 y20.1 w23 y20.1 idx22 rs21 tree22.1 th21 y20.1 h21 b23 cw23 pp21 tree23.1 c23.1 y20.2 c23.1 y20 y21.1 c23 y21.2 tree23.1 rs22 th22 h22 idx23 y21.1 pp22 gt23 y21.1 tree22.1 y22.1 tree22 y21 y22.3 th23 h23 y22 pp23 rs23 tree23.1 y23.1 tree23 y23 em23 ef23'),
-    P=('jb0 jb1 vote0 jb2 vote1 co vote2.2 oa0 jb3 oa1 f0 vote2 bb0 vote3.1 ob0 oa2 f1 vote3.1 bb1 vote3 f2 ob1 bb2.1 ob2 bb2 jb4 oa3 f3 vote4',
-       'bb-2 jb0 ob-2 oa-1 vote0.2 f-1 vote0',
-       'bb18 ob18 ym20.1 oa19 jb20 vote20.2 f19 vote20 jb21 bb19 ob19 ym20 ym21.1 oa20 oa21 vote21.1 f20 vote21 jb22 ym21 bb20.1 ob20.1 bb20 ob20 vote22.2 ym22.1 vote22 f21 oa22 ob21.1 bb21 oa23 ym22 jb23 ob21 vote23.1 f22 vote23 ob22.1 bb22 ob22 f23 ym23 bb23 ob23'),
-    G=('late.1 setup rl late out0 fold3 out1 oo1 out2',
-       'out-2 fold0 oo-2 side-1',
-       'out18 side19 out19 oo19 fold21 y20 y21 y22 e23 y23')))
-ORDER = dict(turns=(5, 20), queues=dict(
-    A=('setup w0 w1 w2 tab.2 tw tab w3 gt0 gt1 gt2 gt3 w4',
-       'w0 gt-1',
-       'w20 gt19 w21 gt20 w22 gt21 w23 gt22 gt23 y23'),
-    V=('setup.1 mat.2 x.1 mat.1 setup.1 mat.1 late.1 setup.1 mat.3 setup.1 rl setup.1 cb.1 cb.1 fs.1 setup.1 cb.1 fs.1 x fs.1 cb.1 late.1 late.1 late.2 cb.1 fs.1 mat cb.1 fs.1 late.1 cb.1 fs.1 cb setup fs b0 b2 b1 b3 w0 dm.1 c0.1 dm.2 om.1 c0.1 om.1 dm.1 c0 dm.1 om dm.2 c1.1 dm.1 cw0 dm.3 c1.1 cw1 dm c1 tab.2 idx0 tab co.2 idx1 co.1 cw2 co.4 c2 co gt0 gt1 h0 th0 cw3 idx2 out0 c3.1 rs0 pp0 h1 th1 c3 out1 rs1 oo0 idx3 late pp1 h2 th2 oo1 pp2 out2 rs2 oo2 b4 w4 c4.1 cw4 c4',
-       'w0 h-2 b0 th-2 rs-2 idx-1 pp-2 out-2 c0.1 cw0 c0.1 gt-1 c0 oo-2',
-       'b20 w20 h18 pp18 th18 idx19 cw20 out18 rs18 c20.1 gt19 c20 oo18 w21 b21 h19 rs19 idx20 th19 pp19 cw21 out19 c21.2 oo19 w22 c21 b22 h20 rs20 th20 idx21 pp20 c22.1 cw22 c22 tree22.1 y20.1 w23 y20.2 rs21 h21 idx22 tree22.1 th21 pp21 c23.1 b23 y20.1 tree23.1 cw23 y21.1 c23 y20.1 y21.1 tree23.1 y21.1 rs22 h22 idx23 y20 pp22 tree22.1 th22 y21.1 gt23 y21 y22.1 tree22 y22.2 h23 rs23 th23 y22 pp23 tree23.1 y23.2 tree23 y23 em23 ef23'),
-    P=('jb0 vote0.2 jb1 vote0 jb2 vote1 co vote2.2 oa0 jb3 f0 vote2 bb0 oa1 f1 vote3.1 bb1 ob0 vote3 oa2 f2 ob1 bb2 ob2 oa3 jb4 f3 vote4',
-       'bb-2 jb0 ob-2 oa-1 vote0.2 f-1 vote0',
-       'jb20 bb18 oa19 ob18 ym20.1 vote20.1 f19 vote20 jb21 bb19 ob19 oa20 ym20 oa21 vote21.1 f20 vote21 jb22 ym21.1 ob20.1 bb20.1 ym21 ob20 bb20 vote22 f21 ym22.1 oa22 ob21.1 bb21 oa23 ob21 jb23 vote23.1 f22 vote23 ym22 bb22.1 ob22.1 bb22 ob22 f23 ym23 bb23 ob23'),
-    G=('setup rl late out0 out1 fold3 oo1 out2',
-       'out-2 fold0 oo-2 side-1',
-       'out18 side19 out19 oo19 fold21 y20 y21 y22 e23 y23')))
-ORDER = dict(turns=(5, 20), queues=dict(
-    A=('setup w0 w1 w2 tw tab w3 gt0 gt1 gt2 gt3 w4',
-       'w0 gt-1',
-       'w20 gt19 w21 gt20 w22 gt21 w23 gt22 gt23 y23'),
-    V=('mat.1 setup.1 mat.1 late.1 mat.1 x.1 mat.1 setup.2 fs.1 setup.1 mat.2 rl mat.1 cb.1 setup.1 cb.1 setup.1 fs.1 x cb.1 late.1 fs.1 cb.1 late.1 fs.1 late.1 cb.2 late.1 setup cb.1 fs.1 cb mat late.1 b2 b0 b1 b3 fs.1 w0 dm.3 c0.1 dm.1 c0.1 dm.1 c0 cw0 dm.2 om.2 cw1 om.1 dm.1 om dm idx0 c1.2 tab co.2 cw2 co.1 c1 co.4 c2.1 fs c2.1 co idx1 gt0 c2 c3.1 th0 h0 cw3 idx2 pp0 rs0 out0 gt1 c3 oo0 th1 h1 rs1 out1 pp1 idx3 late h2 th2 oo1 rs2 pp2 b4 oo2 out2 w4 c4.1 cw4 c4',
-       'w0 th-2 h-2 b0 rs-2 idx-1 pp-2 out-2 c0.1 cw0 c0.1 gt-1 c0 oo-2',
-       'b20 w20 th18 h18 rs18 pp18 idx19 out18 cw20 c20.1 gt19 c20 w21 th19 b21 h19 rs19 idx20 oo18 pp19 out19 c21.1 cw21 oo19 c21 w22 b22 h20 rs20 th20 pp20 idx21 c22.1 cw22 tree22.1 y20.1 oo20 c22 y20.1 w23 b23 rs21 th21 y20.1 h21 idx22 c23.1 cw23 pp21 c23.1 y20.1 c23 y21.1 tree23.1 tree22.1 oo21 y21.1 y20.1 h22 idx23 y20 th22 pp22 rs22 gt23 y21.2 tree22.1 y21.1 y22.1 oo22 y21 tree23.1 th23 y22.1 h23 y22.2 rs23 y22 tree22 tree23.1 pp23 y23.1 tree23 y23 em23 ef23'),
-    P=('jb0 jb1 vote0 jb2 vote1 co vote2.2 oa0 jb3 oa1 f0 vote2 bb0 vote3.1 ob0 oa2 f1 vote3.1 bb1 vote3 f2 ob1 bb2.1 ob2 bb2 jb4 oa3 f3 vote4',
-       'bb-2 jb0 ob-2 oa-1 vote0.2 f-1 vote0',
-       'bb18 oa19 ob18 jb20 ym20 vote20.1 f19 vote20 bb19 jb21 ob19 oa20 vote21.1 oa21 f20 vote21 jb22 ym21 bb20.1 ob20.1 bb20 vote22.1 ob20 vote22.1 f21 vote22 ym22 jb23 oa22 bb21 vote23 ob21.1 f22 oa23 ob21 bb22 ob22.1 ym23.1 f23 ob22 bb23.1 ym23 bb23 ob23'),
-    G=('late.1 setup rl late out0 fold3 out1 oo1 out2',
-       'out-2 fold0 oo-2 side-1',
-       'out18 side19 out19 oo19 fold21 y20 y21 y22 e23 y23')))
-COST.update(og=2)
+       'out18 side19 out19 oo19 fold21 y20 y21 y22 e23 y23'),
+    S=('first wp maps rp.1 om.3 co rp om rlw tw tab', '', 'un22 y23 ef23')))
+COST.update(fa=0, dh=1, ga=48)
 ORDER["queues"].update(
-    V=ORDER["queues"]["V"][:2] + ('w20 h18 th18 rs18 pp18 idx19 out18 b20 cw20 c20.1 oo18 c20.1 gt19 c20 w21 b21 h19 th19 idx20 pp19 rs19 out19 c21.1 oo19 cw21 c21 w22 b22 th20 h20 rs20 idx21 pp20 cw22 c22 tree22.1 y20.1 w23 y20.1 idx22 rs21 tree22.1 th21 y20.1 h21 b23 cw23 pp21 tree23.1 c23.1 y20.2 c23.1 y20 y21.1 c23 y21.2 tree23.1 rs22 th22 h22 idx23 y21.1 pp22 gt23 y21.1 tree22.1 y22.1 tree22 y21 y22.3 th23 h23 y22 pp23 rs23 tree23.1 y23.1 tree23 y23 em23 ef23',),
-    P=ORDER["queues"]["P"][:2] + ('bb18 ob18 ym20.1 oa19 jb20 vote20.2 f19 vote20 jb21 bb19 ob19 ym20 ym21.1 oa20 oa21 vote21.1 f20 vote21 jb22 ym21 bb20.1 ob20.1 bb20 ob20 vote22.2 ym22.1 vote22 f21 oa22 ob21.1 bb21 oa23 ym22 jb23 ob21 vote23.1 f22 vote23 ob22.1 bb22 ob22 f23 ym23 bb23 ob23',),
-    G=('late.1 setup rl late out0 fold3 out1 oo1 out2',
-       'out-2 fold0 side-1 oo-2',
-       'out18 side19 out19 oo19 fold21 y20 y21 y22 e23 y23'))
-COST.update(wa=13, ga=48)
+    V=('zr setup.1 rp setup.1 sel.1 setup.2 rl cb.4 setup.1 cb.2 sel setup cb b2 b0 b3 w0 dm.1 c0.2 dm.1 c0 dm.2 b1 dm.1 om.1 cw0 om.1 dm.2 c1.1 dm.1 cw1 c1.1 dm.1 co.2 dm.1 idx0 dm om.1 co.1 tab.3 om tab c1 co.1 cw2 co.3 c2.2 idx1 co gt0 c2 c3.1 h0 th0 cw3 pp0 idx2 out0 gt1 c3 rs0 h1 th1 oo0 out1 pp1 idx3 h2 rs1 rs2 th2 pp2 late.1 oo1 late oo2 b4 out2 w4 cw4 c4',
+       'w0 h-2 rs-2 th-2 idx-1 b0 pp-2 out-2 cw0 c0.2 gt-1 oo-2 c0',
+       'w20 h18 th18 idx19 b20 rs18 pp18 out18 cw20 c20.2 gt19 oo18 c20 b21 h19 th19 idx20 pp19 rs19 out19 w21 cw21 oo19 c21.1 w22 c21 h20.1 b22 h20 idx21 rs20.1 th20 pp20 rs20 c22.1 cw22 c22.1 b23 c22 w23 y20.1 h21 rs21.1 th21 y20 idx22 rs21 pp21 cw23 c23 tree22.1 y21 tree22.1 idx23 h22 rs22.1 th22 pp22 rs22 gt23 tree23.1 y22 h23 rs23.1 th23 tree23.1 rs23 pp23 tree22.1 tree23.1 y23.1 tree23 tree22 y23.1 yo23.1 y23.1 yo23 y23 em23.2 un22.3 em23.1 un22 em23 ef23'),
+    P=('jb0 vote0.1 jb1 vote0 vote1 jb2 co jb3 vote2.2 f0 vote2 bb0 os0 ob0 vote3.1 f1 vote3 bb1 os1 f2 os2 ob1 ob2 bb2 jb4 f3 vote4',
+       'bb-2 jb0 os-2 ob-2 vote0.2 f-1 vote0',
+       'bb18 os18 ob18 jb20 vote20.2 f19 vote20 bb19 os19 ob19 ym20 jb21 vote21.1 f20 vote21 jb22 bb20 ob20.1 ym21 ob20 vote22.1 f21 vote22 jb23 bb21 ym22 ob21 vote23 f22 bb22 ob22 f23 ym23 bb23 ob23'))
+COST.update(fa=0, dh=0, ga=48)
+ORDER["queues"].update(
+    A=('rp w0 w1 w2 tab tw w3 gt0 gt1 gt2 gt3 w4', 'w0 gt-1', 'w20 gt19 w21 gt20 w22 gt21 w23 gt22 gt23 y23'),
+    V=('zr setup.2 rp setup.2 rl cb.2 sel.1 setup.1 cb.1 sel cb setup b1 b0 b3 b2 w0 dm.2 c0.2 cw0 dm.2 c0 dm.1 om.2 c1.1 idx0 dm.4 om.1 dm.1 co.1 dm.1 co.1 dm c1.1 cw2 cw1 tab.3 om tab co.1 c1 co.4 c2.2 co idx1 gt0 c2 c3.1 th0 h0 idx2 cw3 out0 gt1 c3 pp0 h1 rs1 th1 late.1 idx3 rs0 pp1 out1 b4 h2 oo0 th2 pp2 oo1 w4 out2 rs2 late cw4 c4',
+       'w0 b0 h-2 idx-1 th-2 rs-2 oo-3 pp-2 c0.1 out-2 cw0 c0.1 gt-1 c0',
+       'w20 h18.1 th18 h18 oo17 idx19 b20 pp18 out18 c20.1 cw20 c20.1 gt19 rs18 c20 oo18 b21 th19 h19 idx20 rs19 w21 out19 cw21 pp19 c21.1 b22 oo19 w22 c21 rs20.1 th20 h20 idx21 pp20 cw22 rs20 c22.2 y20.1 b23 c22 w23 th21 h21 idx22 rs21.1 y20 pp21 rs21 cw23 c23.2 y21.1 c23 tree22.1 idx23 y21 tree22.1 h22 rs22.1 th22 pp22 rs22 gt23 tree23.1 y22.1 tree22.1 h23.1 rs23.1 y22 h23 th23 tree23.1 pp23 rs23 tree22 y23.1 tree23.1 y23.1 tree23 yo23.1 y23.1 yo23 y23 em23.2 un22.1 em23.1 un22.2 em23.1 un22 em23 ef23'),
+    P=('jb1 jb0 vote0 vote1.1 jb2 vote1 co vote2.2 jb3 f0 vote2 bb0 os0 vote3.1 f1 vote3 os1 bb1 ob1 f2 ob0 os2 bb2 jb4 ob2 f3 vote4',
+       'bb-2 os-2 ob-2 jb0 vote0.2 f-1 vote0',
+       'bb18 jb20 os18 ym20 ob18 vote20.2 f19 vote20 os19 bb19 ob19 jb21 ym21 vote21.1 f20 vote21 jb22 bb20 ob20 vote22.2 f21 vote22 jb23 bb21 ob21 vote23 ym22 f22 bb22 ob22 f23 ym23 bb23 ob23'),
+    G=('setup if rl cox mat fs x late out0 fold3 out1 oo1 out2', 'out-2 oo-3 side-1 fold0', 'oo17 out18 side19 out19 oo19 fold21 y20 y21 y22 e23 y23'),
+    S=('first wp maps.7 rp.1 maps om co rlw.3 rp rlw tab tw', '', 'un22 y23 ef23'))
 
 
 def build(g, T, peers, cost):
@@ -220,44 +90,40 @@ def build(g, T, peers, cost):
     nd = [0]
     now = [0, "setup"]
 
-    def op(eng, fn, rd, wr, dur, banks=(), kind="c", sem=None, after=None, lat=0.0, inc=0):
-        ops.append(dict(eng=eng, fn=fn, rd=rd, wr=wr, dur=dur, banks=banks, kind=kind, sem=sem, after=after, inc=inc,
-                        lat=lat, i=len(ops), n=now[0], tag=now[1]))
+    def op(eng, fn, rd, wr, banks=(), kind="c", sem=None, after=None, inc=0):
+        ops.append(dict(eng=eng, fn=fn, rd=rd, wr=wr, banks=banks, kind=kind, sem=sem, after=after, inc=inc,
+                        i=len(ops), n=now[0], tag=now[1]))
         return len(ops) - 1
 
     def at(tag):
         now[1] = tag
 
-    def vec(fn, rd, wr, n, banks=(), two=0):
-        return op("V", lambda: [fn()], rd, wr, max(64.0, n) * cost["f"] + cost["ov"] + cost.get("ps", 0) * len(banks) + cost.get("tt", 0) * two, banks)
+    def vec(fn, rd, wr, banks=()):
+        return op("V", lambda: [fn()], rd, wr, banks)
 
-    def act(fn, rd, wr, n, banks=()):
-        return op("A", lambda: [fn()], rd, wr, max(64.0, n) * cost["f"] + cost["ova"], banks)
+    def tt(out, a, b, alu, rd, wr, banks=()):
+        return vec(lambda: v.tensor_tensor(out, a, b, alu), rd, wr, banks)
 
-    def tt(out, a, b, alu, rd, wr, n, banks=()):
-        return vec(lambda: v.tensor_tensor(out, a, b, alu), rd, wr, n, banks, 1)
+    def ts(out, a, s1, s2, ops2, rd, wr, banks=()):
+        return vec(lambda: v.tensor_scalar(out, a, s1, s2, *ops2), rd, wr, banks)
 
-    def ts(out, a, s1, s2, ops2, rd, wr, n, banks=()):
-        return vec(lambda: v.tensor_scalar(out, a, s1, s2, *ops2), rd, wr, n, banks)
-
-    def gather(eng, out, win, rd, wr, n):
+    def gather(eng, out, win, rd, wr):
         if eng == "A":
-            return op("A", lambda: [s.activation(out, win, M.Copy)], rd, wr, (78 + cost["r"] * n) * cost["f"])
-        return op("V", lambda: [v.tensor_copy(out, win)], rd, wr, (60 + cost["r"] * n) * cost["f"])
+            return op("A", lambda: [s.activation(out, win, M.Copy)], rd, wr)
+        return op("V", lambda: [v.tensor_copy(out, win)], rd, wr)
 
     def mm(lst, rd, banks, first=True, last=True):
-        n = sum(x[3] for x in lst)
         return op("P", lambda: [pe.matmul(x[0], x[1], x[2], first and k == 0, last and k == len(lst) - 1) for k, x in enumerate(lst)],
-                  rd, [], n * cost["pe"] * cost["f"] + 30, banks)
+                  rd, [], banks)
 
-    def dma(out, in_, rd, wr, nbytes, q="S", sem=None):
+    def dma(out, in_, rd, wr, q="S", sem=None):
         if sem is None:
             sem = "d%d" % nd[0]
             nd[0] += 1
         qu = g.sync if q == "S" else g.scalar
-        return op(q, lambda: [qu.dma_start(out, in_)], rd, wr, cost.get("sq", 100.0), kind="dma", sem=sem, lat=nbytes * cost["dmab"] + cost.get("dr", 0.0))
+        return op(q, lambda: [qu.dma_start(out, in_)], rd, wr, kind="dma", sem=sem)
 
-    def send(dst, srcs, peer, sem, rd, after=None):
+    def send(dst, srcs, peer, sem, rd, after=None, alu=2):
         rid, pid, mask, engines = peers[peer]
 
         def fn():
@@ -265,18 +131,28 @@ def build(g, T, peers, cost):
                 g.remote_dma(dst, srcs[0], T.sem[sem], T.sem.sent, pid, rid, mask)
             else:
                 g.remote_dma_fused([RemoteDMATransfer(dst_ids=[DstId(rid=rid, pnc=pid)], dma_engine_mask=mask,
-                                                      remote_sem=T.sem[sem], srcs=srcs, dsts=[dst], alu_op=2)],
+                                                      remote_sem=T.sem[sem], srcs=srcs, dsts=[dst], alu_op=alu)],
                                    local_sem=T.sem.sent)
             return []
-        return op("G", fn, rd, [], cost["call"], kind="send", after=after, inc=engines)
+        return op("G", fn, rd, [], kind="send", after=after, inc=engines)
 
-    def arrive(i, sem, wr, engines, lat, kind="arr"):
-        op(None, None, [], wr, 0.0, kind=kind, sem=sem, after=i, lat=lat, inc=engines)
+    def arrive(i, sem, wr, engines):
+        op(None, None, [], wr, kind="arr", sem=sem, after=i, inc=engines)
 
-    def post(dst, srcs, peer, sem, rd, wr, more=0.0, after=None):
+    def post(dst, srcs, peer, sem, rd, wr, after=None):
         i = send(dst, srcs, peer, sem, rd, after)
-        arrive(i, sem, wr, peers[peer][3], cost["lat"] + more)
+        arrive(i, sem, wr, peers[peer][3])
         return i
+
+    def post2(jobs, rd):
+        def fn():
+            g.remote_dma_fused([RemoteDMATransfer(dst_ids=[DstId(rid=rid, pnc=pid)], dma_engine_mask=mask, remote_sem=T.sem[sem],
+                                                  srcs=[src], dsts=[dst], alu_op=0)
+                                for (dst, src, sem, wr), (rid, pid, mask, engines) in zip(jobs, peers["half"])], local_sem=T.sem.sent)
+            return []
+        i = op("G", fn, rd, [], kind="send", inc=peers["prev"][3])
+        for (dst, src, sem, wr), way_ in zip(jobs, peers["half"]):
+            arrive(i, sem, wr, way_[3])
 
     def xv(buf, f, n=1):
         return buf[:, f * 16 + 1:(f + n) * 16:2, :]
@@ -284,142 +160,140 @@ def build(g, T, peers, cost):
     def xt(buf, f, bit):
         return buf[:, f * 16 + 1 - bit:f * 16 + 17 - bit, :]
 
-    dma(T.RLI[:], T.rl[:], [], ["RLI"], 131072)
-    dma(T.CBI[:], T.cb[:], [], ["CBI"], 131072)
-    dma(T.WP[:, V:V + 16], T.wp[:, 0:16], [], ["WPw"], 16384)
-
-    def load(what):
-        if what == "w":
-            dma(T.WP[:, 0:V], T.wp[:], [], ["WP"], 1048576)
-        elif what == "d":
-            for g0 in range(2):
-                for k in range(4):
-                    dma(T.DMI[:, g0, k * 4:k * 4 + 4, :], T.dm[g0::2, k * 2048:(k + 1) * 2048], [], [("DMI", g0, k)], 32768)
-        elif what == "o":
-            for k in range(4):
-                a = k % 2 * V + k // 2 * 2048
-                dma(T.OMI[:, k * 128:(k + 1) * 128], T.om[:, a:a + 2048], [], [("OMI", k)], 65536)
-        else:
-            dma(T.COI[:], T.co[:], [], ["COI"], 131072)
-    early, late = cost["loads"].split("|")
-    for what in early:
-        load(what)
+    at("first")
+    dma(T.RLI[:], T.rl[:], [], ["RLI"])
+    dma(T.CBI[:], T.cb[:], [], ["CBI"])
+    at("wp")
+    dma(T.WP[:, V:V + 16], T.wp[:, 0:16], [], ["WPw"])
+    dma(T.WP[:, 0:V], T.wp[:], [], ["WP"])
 
     at("rl")
-    vec(lambda: v.tensor_copy(T.RLB[:], T.RLI[:]), ["RLI"], ["RLB"], 256)
-    post(T.RLL[:], [T.RLB[:]], "prev", "a_rl", ["RLB"], ["RLL"], more=cost["first"])
-    at("setup")
-
-    op("G", lambda: [g.iota(T.PC[:, 0:1], [[0, 1]], 0, 1)], [], ["PC"], 160.0)
-    op("G", lambda: [g.iota(T.PI[:], [[-1, 128]], 0, 1, allow_small_or_imprecise_dtypes=True)], [], ["PI"], 420.0)
-    op("G", lambda: [g.iota(T.LO[:], [[1, 256]], 0, 0, allow_small_or_imprecise_dtypes=True)], [], ["LO"], 670.0)
-    vec(lambda: v.memset(T.ZR[:], 0.0), [], ["ZR"], 512)
+    vec(lambda: v.tensor_copy(T.RLB[:], T.RLI[:]), ["RLI"], ["RLB"])
+    i = post(T.RLL[:], [T.RLB[:]], "prev", "a_rl", ["RLB"], ["RLL"])
+    GO = []
+    if cost["gate"]:
+        op("G", lambda: g.sem_inc(T.sem.go, 1), [], ["GO"], kind="sig", sem="go", after=i)
+        GO = ["GO"]
+    at("maps")
+    for g0 in range(2):
+        for k in range(4):
+            dma(T.DMI[:, g0, k * 4:k * 4 + 4, :], T.dm[g0::2, k * 2048:(k + 1) * 2048], GO, [("DMI", g0, k)])
+    at("om")
     for k in range(4):
-        act(lambda k=k: s.activation(T.RLW[:, 16 + k * 1024:16 + (k + 1) * 1024], T.ZR[:], M.Copy), ["ZR"], [("RLW0", k)], 1024)
-    ts(T.PG[:, 0:1], T.PC[:, 0:1], 4, 1, (A.logical_shift_right, A.bitwise_and), ["PC"], ["PG"], 1)
-    ts(T.PD[:, 0:1], T.PC[:, 0:1], 15, None, (A.bitwise_and,), ["PC"], ["PD"], 1)
+        a = k % 2 * V + k // 2 * 2048
+        dma(T.OMI[:, k * 128:(k + 1) * 128], T.om[:, a:a + 2048], GO, [("OMI", k)])
+    at("co")
+    dma(T.COI[:], T.co[:], GO, ["COI"])
+
+    def iota(out, pattern, base, mult, wr):
+        op("G", lambda: [g.iota(out, pattern, base, mult, allow_small_or_imprecise_dtypes=True)], [], wr)
+
+    def mark(out, in_, pattern, base, mult, x, rd, wr, keep=A.not_equal):
+        op("G", lambda: [g.affine_select(out, in_, pattern, keep, x, base, mult)], rd, wr)
+    at("zr")
+    vec(lambda: v.memset(T.ZR[:], 0.0), [], ["ZR"])
+    at("setup")
+    op("G", lambda: [g.iota(T.PC[:, 0:1], [[0, 1]], 0, 1)], [], ["PC"])
+    iota(T.LO[:], [[1, 256]], 0, 0, ["LO"])
+    ts(T.PG[:, 0:1], T.PC[:, 0:1], 4, 1, (A.logical_shift_right, A.bitwise_and), ["PC"], ["PG"])
+    ts(T.PD[:, 0:1], T.PC[:, 0:1], 15, None, (A.bitwise_and,), ["PC"], ["PD"])
     for x in range(2):
-        ts(T.MK[:, x:x + 1], T.PG[:, 0:1], float(x), None, (A.is_equal,), ["PG"], [("MK", x)], 1)
-    ts(T.PF[:, 0:1], T.PD[:, 0:1], -8.0, 256.0, (A.add, A.mult), ["PD"], ["PF"], 1)
-    ts(T.HI[:], T.LO[:], 0.0, T.PF[:, 0:1], (A.mult, A.add), ["PF", "LO"], ["HI"], 128)
+        ts(T.MK[:, x:x + 1], T.PG[:, 0:1], float(x), None, (A.is_equal,), ["PG"], [("MK", x)])
+    ts(T.MK[:, 2:3], T.PD[:, 0:1], -8.0, 256.0, (A.add, A.mult), ["PD"], ["PF"])
+    ts(T.HI[:], T.ZR[:, 0:256], T.MK[:, 2:3], None, (A.add,), ["PF", "ZR"], ["HI"])
+
+    at("rp")
+    for k in range(4):
+        if k < cost["ra"]:
+            op("A", lambda k=k: [s.activation(T.RLW[:, 16 + k * 1024:16 + (k + 1) * 1024], T.ZR[:], M.Copy)], ["ZR"], [("RLW0", k)])
+        else:
+            vec(lambda k=k: v.memset(T.RLW[:, 16 + k * 1024:16 + (k + 1) * 1024], 0.0), [], [("RLW0", k)])
+    R0K = [("RLW0", k) for k in range(4)]
+    dma(T.RLW[3::16, 16:16 + V], T.HI[:], R0K + ["HI"], [("RLW", 3)])
+    dma(T.RLW[4::16, 16:16 + V], T.LO[:], R0K + ["LO"], [("RLW", 4)])
+    at("rlw")
+    for f in range(3):
+        dma(T.RLW[f::16, 16 - f:16 - f + V], T.RLL[:], R0K + ["RLL"], [("RLW", f)])
+    for f in (1, 2):
+        dma(T.RLW[f::16, 16 - f + V:18 - f + V], T.RLL[0::16, 0:2], R0K + ["RLL"], [("RLW", 10 + f)])
+    RLK = R0K + [("RLW", f) for f in (0, 1, 2, 3, 4, 11, 12)]
 
     def turn(src, key, add, Y, Z):
         for x in range(2):
-            ts(Y[:, :, x * 16:x * 16 + 16], src[:], add, T.MK[:, x:x + 1], (A.add, A.mult), [key, ("MK", x)], [(key, "Y", x)], 256)
-        vec(lambda: v.transpose(Z[:], Y[:]), [(key, "Y", 0), (key, "Y", 1)], [(key, "Z")], 256)
+            ts(Y[:, :, x * 16:x * 16 + 16], src[:], add, T.MK[:, x:x + 1], (A.add, A.mult), [key, ("MK", x)], [(key, "Y", x)])
+        vec(lambda: v.transpose(Z[:], Y[:]), [(key, "Y", 0), (key, "Y", 1)], [(key, "Z")])
 
     at("cb")
     turn(T.CBI, "CBI", -2048.0, T.CY, T.CZ)
-    tt(T.CS[:], T.CZ[:, :, 0:16], T.CZ[:, :, 16:32], A.add, [("CBI", "Z")], [("CBI", "S")], 256)
+    tt(T.CS[:], T.CZ[:, :, 0:16], T.CZ[:, :, 16:32], A.add, [("CBI", "Z")], [("CBI", "S")])
     for h in range(4):
-        ts(T.L0[:, h::4], T.CS[:, h::4, :], 2048.0, None, (A.add,), [("CBI", "S")], [("L0", h)], 32)
+        ts(T.L0[:, h::4], T.CS[:, h::4, :], 2048.0, None, (A.add,), [("CBI", "S")], [("L0", h)])
     L0K = [("L0", h) for h in range(4)]
-
-    at("rlw")
-    R0K = [("RLW0", k) for k in range(4)]
-    dma(T.RLW[3::16, 16:16 + V], T.HI[:], R0K + ["HI"], [("RLW", 3)], 65536)
-    dma(T.RLW[4::16, 16:16 + V], T.LO[:], R0K + ["LO"], [("RLW", 4)], 65536)
-    for f in range(3):
-        dma(T.RLW[f::16, 16 - f:16 - f + V], T.RLL[:], R0K + ["RLL"], [("RLW", f)], 65536)
-    for f in (1, 2):
-        dma(T.RLW[f::16, 16 - f + V:18 - f + V], T.RLL[0::16, 0:2], R0K + ["RLL"], [("RLW", 10 + f)], 100)
-    for what in late:
-        load(what)
-    RLK = R0K + [("RLW", f) for f in (0, 1, 2, 3, 4, 11, 12)]
 
     at("dm")
     for g0 in range(2):
         for m in range(2):
             ts(T.DMR[:, :, g0 * 16 + m:g0 * 16 + 16:2], T.DMI[:, g0, m * 8:m * 8 + 8, :], -2048.0, None, (A.add,),
-               [("DMI", g0, 2 * m), ("DMI", g0, 2 * m + 1)], [("DMR", g0, m)], 128)
-    vec(lambda: v.transpose(T.DMU[:], T.DMR[:]), [("DMR", g0, m) for g0 in range(2) for m in range(2)], ["DMU"], 256)
+               [("DMI", g0, 2 * m), ("DMI", g0, 2 * m + 1)], [("DMR", g0, m)])
+    vec(lambda: v.transpose(T.DMU[:], T.DMR[:]), [("DMR", g0, m) for g0 in range(2) for m in range(2)], ["DMU"])
     for q in range(8):
-        ts(T.DMZ[:, q::8], T.DMU[:, q::8, :], 2048.0, None, (A.add,), ["DMU"], [("DMZ", q)], 32)
+        ts(T.DMZ[:, q::8], T.DMU[:, q::8, :], 2048.0, None, (A.add,), ["DMU"], [("DMZ", q)])
     ZK = [("DMZ", q) for q in range(8)]
 
-    at("mat")
-    vec(lambda: v.memset(T.SEL[:], 0.0), [], ["SEL"], 72)
-    vec(lambda: v.memset(T.COX[:], 0.0), [], ["COX0"], 260)
-    vec(lambda: v.memset(T.SEL[:, 15::16], 1.0 / 128), [], ["SEL"], 9)
-    for buf, x in (("ID", 1.0), ("IF", 1.0), ("IB", 1.0), ("IH", 1.0), ("IN", -1.0)):
-        ts(T[buf][:], T.PI[:], 0.0, x, (A.is_equal, A.mult), ["PI"], [buf], 128)
+    at("sel")
+    vec(lambda: v.memset(T.SEL[:], 0.0), [], ["SEL"])
+    vec(lambda: v.memset(T.SEL[:, 15::16], 1.0 / 128), [], ["SEL"])
+    for tag, buf in (("if", "IF"), ("mat", "IB"), ("mat", "IH")):
+        at(tag)
+        mark(T[buf][:], T.ZR[:, 0:128], [[-1, 128]], 0, 1, 1.0, ["ZR"], [buf])
+    at("cox")
+    iota(T.COX[:], [[0, 520]], 0, 0, ["COX0"])
     at("x")
     for p in range(2):
-        vec(lambda p=p: v.tensor_copy(T["X%d" % p][:], T.ZR[:, 0:904]), ["ZR"], [("X0", p)], 452)
-
-    def row(f):
-        return T.ID[:, f::16]
-
-    def fs(f):
-        return T.FS[:, f * 8:(f + 1) * 8]
+        mark(T["X%d" % p][:, 0:113:2, :], T.ZR[:, 0:456], [[0, 456]], 0, 0, 0.0, ["ZR"], [("X0", p)])
     at("fs")
-    tt(fs(0), row(5), row(0), A.subtract, ["ID"], [("FS", 0)], 8)
-    tt(fs(4), row(3), row(4), A.add, ["ID"], [("FS", 4)], 8)
-    ts(fs(3), row(5), 1.0, None, (A.mult,), ["ID"], [("FS", 3)], 8)
-    tt(fs(1), fs(0), row(1), A.subtract, ["ID", ("FS", 0)], [("FS", 1)], 8)
-    ts(fs(5), row(0), -1.0, None, (A.mult,), ["ID"], [("FS", 5)], 8)
-    ts(fs(6), row(1), -1.0, None, (A.mult,), ["ID"], [("FS", 6)], 8)
-    tt(fs(2), fs(1), row(2), A.subtract, ["ID", ("FS", 1)], [("FS", 2)], 8)
-    FSK = [("FS", f) for f in range(7)]
+    for a, b, r, step, x, new in ((0, 3, 5, 0, -1.0, 1), (3, 4, 3, 0, 1.0, 1), (4, 6, 0, 1, -1.0, 1), (6, 7, 5, 0, 1.0, 1),
+                                  (0, 3, 0, 0, 1.0, 0), (3, 4, 4, 0, 1.0, 0), (1, 3, 1, 0, 1.0, 0), (2, 3, 2, 0, 1.0, 0),
+                                  (7, 8, 0, 0, 1.0, 1), (7, 8, 1, 0, 1.0, 0), (7, 8, 2, 0, 1.0, 0)):
+        fk = [("FS", f) for f in range(a, b)]
+        mark(T.FS[:, a * 8:b * 8], (T.ZR if new else T.FS)[:, a * 8:b * 8], [[-step, b - a], [-16, 8]], -r, 1, x, ["ZR"] + fk * (1 - new), fk)
+    FSK = [("FS", f) for f in range(8)]
 
     at("om")
     for k in range(4):
         vec(lambda k=k: v.tensor_copy(T.OMB[:, k // 2 * 256 + k % 2:k // 2 * 256 + 256:2], T.OMI[:, k * 128:(k + 1) * 128]),
-            [("OMI", k)], [("OMB", k)], 128)
+            [("OMI", k)], [("OMB", k)])
     at("co")
     turn(T.COI, "COI", 1.0, T.OY, T.OZ)
     for h in range(4):
-        tt(T.COX[:, 2 * h + 1:513:8], T.OZ[:, h::4, 0:16], T.OZ[:, h::4, 16:32], A.add, [("COI", "Z"), "COX0"], [("COX", h)], 64)
+        tt(T.COX[:, 2 * h + 1:513:8], T.OZ[:, h::4, 0:16], T.OZ[:, h::4, 16:32], A.add, [("COI", "Z"), "COX0"], [("COX", h)])
     for c in range(NCH):
-        mm([(T.OB1[:, c * 64:c * 64 + 64], T.COX[:, 128 * c + 1 - bit:128 * c + 129 - bit], T.IB[:, bit::2, :], 64)
+        mm([(T.OB1[:, c * 64:c * 64 + 64], T.COX[:, 128 * c + 1 - bit:128 * c + 129 - bit], T.IB[:, bit::2, :])
             for bit in range(2)], ["IB", "COX0"] + [("COX", h) for h in range(4)], ["OB1"])
-    vec(lambda: v.tensor_copy(T.OIN[:, 0:256], T.OB1[:, 0:256]), [], [("OIN", c) for c in range(NCH)], 256, ["OB1"])
+    vec(lambda: v.tensor_copy(T.OIN[:, 0:256], T.OB1[:, 0:256]), [], [("OIN", c) for c in range(NCH)], ["OB1"])
 
     at("tw")
     TK = [("TAB", 8)]
-    gather("A", T.TAB[:, 2 * V:2 * V + 32], T.RLW[:, 16:16 + V].indirect(T.DMZ[:, 0:2]), RLK + ZK, TK, 32)
-    dma(T.TAB[5::16, 2 * V:2 * V + 4], T.OMB[0::16, 0:4], [("OMB", 0), ("OMB", 1)], TK, 100)
+    gather("A", T.TAB[:, 2 * V:2 * V + 32], T.RLW[:, 16:16 + V].indirect(T.DMZ[:, 0:2]), RLK + ZK, TK)
+    dma(T.TAB[5::16, 2 * V:2 * V + 4], T.OMB[0::16, 0:4], [("OMB", 0), ("OMB", 1)], TK)
     at("tab")
     for half in range(2):
         pk = [("TAB", k) for k in range(4 * half, 4 * half + 4)]
         for _, k in pk:
             gather(cost["ta"][k], T.TAB[:, k * 1024:(k + 1) * 1024], T.RLW[:, 16:16 + V].indirect(T.DMZ[:, k * 64:(k + 1) * 64]),
-                   RLK + ZK, [("TAB", k)], 1024)
-        dma(T.TAB[5::16, half * V:(half + 1) * V], T.OMB[:, half * 256:(half + 1) * 256], [("OMB", 2 * half), ("OMB", 2 * half + 1)], pk, 65536)
+                   RLK + ZK, [("TAB", k)])
+        dma(T.TAB[5::16, half * V:(half + 1) * V], T.OMB[:, half * 256:(half + 1) * 256], [("OMB", 2 * half), ("OMB", 2 * half + 1)], pk)
         TK = TK + pk
 
     at("late")
     for bit in range(2):
-        op("G", lambda bit=bit: [g.iota(T.TI[:, bit * 128:bit * 128 + 128], [[2, 4], [0, 2], [8, 16]], bit, -1,
-                                        allow_small_or_imprecise_dtypes=True)], [], [("TI", bit)], 420.0)
-    vec(lambda: v.memset(T.PA[:], 0.0), [], [("PA", 0), ("PA", 1)], 64)
-    ts(T.MV[:], T.TI[:], 0.0, None, (A.is_equal,), [("TI", 0), ("TI", 1)], ["MV"], 256)
+        for buf, x in (("MV", 1.0), ("MW", 256.0)):
+            mark(T[buf][:, bit * 128:bit * 128 + 128], T.ZR[:, 0:128], [[2, 4], [0, 2], [8, 16]], bit, -1, x, ["ZR"], [(buf, bit)])
     for x in range(2):
-        vec(lambda x=x: v.memset(T.PA[x * 64:x * 64 + 64, :, x * 16:x * 16 + 16], 1.0), [], [("PA", x)], 64)
-    ts(T.MN[:], T.MV[:], -1.0, None, (A.mult,), ["MV"], ["MN"], 128)
-    for buf, same in (("PB", 32.0), ("PO", -1.0 / 64)):
-        ts(T[buf][:], T.PA[:], 128.0 + same, -128.0, (A.mult, A.add), [("PA", 0), ("PA", 1)], [buf], 64)
-    MVK = ["MV", "MN", ("PA", 0), ("PA", 1), "PB", "PO"]
+        mark(T.PA[:, :, x * 16:x * 16 + 16], T.ZR[:, 0:64], [[0, 64]], (-64, 63)[x], (1, -1)[x], 1.0, ["ZR"], [("PA", x)], A.is_ge)
+    ts(T.PB[:], T.PA[:], 24576.0, -16384.0, (A.mult, A.add), [("PA", 0), ("PA", 1)], ["PB"])
+    ts(T.PO[:], T.PA[:], 128.0 - 1.0 / 64, -128.0, (A.mult, A.add), [("PA", 0), ("PA", 1)], ["PO"])
+    MVK = [("MV", 0), ("MV", 1), ("MW", 0), ("MW", 1), ("PA", 0), ("PA", 1), "PB", "PO"]
 
     omsg = [None]
     for t in range(STEPS):
@@ -433,184 +307,179 @@ def build(g, T, peers, cost):
             jb, bb, fb, ob, x0, s0 = "JB%d" % p, "BB%d" % p, "F%d" % p, "OB%d" % p, ("X0", p), p * 1024
             lst, c0, lk = (T.L0, l0, L0K) if t == 0 else (T.MSG, (n - NCH) * 64, [("MSG", n - NCH)])
             wa = cost["wx"].get(n, cost["wa"])
-            side = 2 if last else NCH
+            side, w0 = (NCH, c) if not last else (NL, c) if c < NL else (1, c * 1024)
 
             def wv(a, b, e=0, ne=1):
-                w0 = c // side * side * 1024 + c % side
-                return W[:, w0 + (a * 64 + e) * side:w0 + b * 64 * side - c % side:side * ne]
-            wb = min(16, wa + cost["vx"].get(n, cost["vs"]))
-            for tag, eng, a, b in (("w", "A", 0, wa), ("w", "V", wa, wb), ("wb", "V", wb, 16)):
-                at(tag)
+                return W[:, w0 + (a * 64 + e) * side:w0 + (b * 64 - 1) * side + 1:side * ne]
+            at("w")
+            for eng, a, b in (("A", 0, wa), ("V", wa, 16)):
                 if b > a:
                     gather(eng, wv(a, b), T.WP[:, 0:V + 16].indirect(lst[:, c0 + a * 4:c0 + b * 4]),
-                           ["WP", "WPw"] + lk, [("W", n, k) for k in range(a, b)], (b - a) * 64)
+                           ["WP", "WPw"] + lk, [("W", n, k) for k in range(a, b)])
             wk = [("W", n, k) for k in range(16)]
             at("b")
-            ts(T.B[:, l0:l0 + 64], lst[:, c0:c0 + 64], 2.0, -1.0 / 256, (A.mult, A.add), lk, [("B", c)], 64)
+            ts(T.B[:, l0:l0 + 64], lst[:, c0:c0 + 64], 2.0, -1.0 / 256, (A.mult, A.add), lk, [("B", c)])
             at("jb")
-            if not cost["jl"]:
-                mm([(JB[:, 0:64], T.IF[:], T.B[:, l0:l0 + 64], 256)], ["IF", ("B", c)], [jb], last=False)
-            cv = cost["cx"].get(n, wa if cost["cv"] and wa < 15 else 15)
-            ne = cost["ne"]
-            for tag, a, b, a2 in (("cv", cv, 15, cv + 1), ("cw", 15, 16, 0)):
-                if b > a:
-                    at(tag)
-                    tt(T.IND[:, s0 + a * 64:s0 + b * 64], wv(a, b), wv(a2, a2 + b - a), A.is_gt, wk[a:b] + wk[a2:a2 + b - a],
-                       [("IND", p, k, e) for k in range(a, b) for e in range(4)], (b - a) * 64)
-            parts = {1: ((0, 1),), 2: ((0, 2), (1, 2)), 3: ((0, 2), (1, 4), (3, 4))}[ne]
+            mm([(JB[:, 0:64], T.IF[:], T.B[:, l0:l0 + 64])], ["IF", ("B", c)], [jb], last=False)
+            at("cw")
+            tt(T.IND[:, s0 + 960:s0 + 1024], wv(15, 16), wv(0, 1), A.is_gt, [wk[15], wk[0]], [("IND", p, 15, e) for e in range(4)])
+            parts = {1: ((0, 1),), 2: ((0, 2), (1, 2)), 3: ((0, 2), (1, 4), (3, 4))}[cost["ne"]]
             for j, (e, st) in enumerate(parts):
                 at("c")
-                tt(T.IND[:, s0 + e:s0 + cv * 64:st], wv(0, cv, e, st), wv(1, cv + 1, e, st), A.is_gt, wk[:cv + 1],
-                   [("IND", p, k, x) for k in range(cv) for x in range(e, 4, st)], cv * 64 // st)
+                tt(T.IND[:, s0 + e:s0 + 960:st], wv(0, 15, e, st), wv(1, 16, e, st), A.is_gt, wk,
+                   [("IND", p, k, x) for k in range(15) for x in range(e, 4, st)])
                 at("vote")
-                mm([(JB[:, 0:64], T.SEL[:, 15 - r:143 - r], T.IND[:, s0 + r:s0 + 1024:16], 64) for r in range(e, 16, st)],
-                   ["SEL"] + [("IND", p, k, x) for k in range(16) for x in range(e, 4, st)], [jb], first=j == 0 and cost["jl"] == 1, last=j == ne - 1)
-                if j == 0 and cost["jl"]:
-                    at("jb")
-                    mm([(JB[:, 0:64], T.IF[:], T.B[:, l0:l0 + 64], 256)], ["IF", ("B", c)], [jb], first=False, last=False)
+                mm([(JB[:, 0:64], T.SEL[:, 15 - r:143 - r], T.IND[:, s0 + r:s0 + 1024:16]) for r in range(e, 16, st)],
+                   ["SEL"] + [("IND", p, k, x) for k in range(16) for x in range(e, 4, st)], [jb], first=False, last=j == len(parts) - 1)
             at("idx")
-            ts(T.IDX[:, l0:l0 + 64], JB[:, 0:64], BIG, BIG, (A.add, A.subtract), [], [("IDX", c)], 64, [jb])
+            ts(T.IDX[:, l0:l0 + 64], JB[:, 0:64], BIG, BIG, (A.add, A.subtract), [], [("IDX", c)], [jb])
             ga = cost["gx"].get(n, cost["ga"])
             gk = []
             at("gt")
             for eng, a, b in (("A", 0, ga), ("V", ga, 64)):
                 if b > a:
                     gather(eng, T.GT[:, s0 + a * 16:s0 + b * 16], T.TAB[:].indirect(T.IDX[:, l0 + a:l0 + b]),
-                           TK + [("IDX", c)], [("GT", p, eng)], (b - a) * 16)
+                           TK + [("IDX", c)], [("GT", p, eng)])
                     gk.append(("GT", p, eng))
             o1 = T.OIN[:, n * 64:n * 64 + 64]
-            nf = 2 if last or cost["sv"] else 1
-            oa = [(F[:, f * 64:f * 64 + 64], T.ID[:], o1, 64) for f in range(2 + nf)]
-            fm = [(F[:, i:448:8], T.GT[:, s0 + i:s0 + 1024:8], T.FS[:, 0:56], 64) for i in range(8)]
-            if cost["zc"]:
-                at("oa")
-                a = 128 + 64 * nf
-                mm(oa + [(F[:, a:448], T.ID[:], T.ZR[:, a:448], 448 - a)], ["ID", "IS", "ZR", ("OIN", n)], [fb], last=False)
-                at("f")
-                mm(fm, FSK + gk, [fb], first=False)
-            else:
-                at("f")
-                mm(fm + oa, FSK + gk + ["ID", "IS", ("OIN", n)], [fb])
+            nf = 8 if last or cost["fa"] else 6
+            at("f")
+            mm([(F[:, i:nf * 64:8], T.GT[:, s0 + i:s0 + 1024:8], T.FS[:, 0:nf * 8]) for i in range(8)], FSK + gk, [fb])
             at("h")
-            nh = 2 + nf if cost["hr"] else 2
-            ts(xv(X, 0, nh), F[:, 0:64 * nh], 0.0, 1.0, (A.max, A.min), [x0], [("h", p)] + [("rs", p)] * cost["hr"], 64 * nh, [fb])
+            for f in range(2):
+                tt(xv(X, f), F[:, f * 64:f * 64 + 64], o1, A.is_lt, [x0, ("OIN", n)], [("h", p, f)], [fb])
+            hk = [("h", p, 0), ("h", p, 1)]
             at("th")
-            vec(lambda F=F, X=X: v.tensor_copy(xv(X, 4), F[:, 256:320]), [x0], [("th", p)], 64, [fb])
+            dh = cost["dh"]
+            if dh:
+                tt(xv(X, 4), F[:, 192:256], xv(X, 0), A.add, [x0, hk[0]], [("th", p)], [fb])
+            else:
+                vec(lambda F=F, X=X: v.tensor_copy(xv(X, 4), F[:, 192:256]), [x0], [("th", p)], [fb])
+            fa = cost["fa"] and not last
             at("rs")
-            if not cost["hr"] and n not in cost["rsa"]:
-                ts(xv(X, 2, nf), F[:, 128:128 + 64 * nf], 0.0, None, (A.max,), [x0], [("rs", p)], 64 * nf, [fb])
+            if fa:
+                part = T.OP[:, n // 2, 0, p, :]
+                tt(part, F[:, 384:448], o1, A.add, [("OIN", n)], [("OP", n, 0)], [fb])
+                tt(part, F[:, 448:512], part, A.min, [("OP", n, 0)], [("OP", n, 0)], [fb])
+            elif last:
+                tt(xv(X, 2), F[:, 384:448], o1, A.add, [x0, ("OIN", n)], [("rs", p)], [fb])
+                tt(xv(X, 2), F[:, 448:512], xv(X, 2), A.min, [x0, ("rs", p)], [("rs", p)], [fb])
+            else:
+                tt(xv(X, 2), F[:, 128:192], o1, A.min, [x0, ("OIN", n)], [("rs", p)], [fb])
             at("pp")
-            tt(xv(X, 5, 2), xv(X, 0, 2), F[:, 320:448], A.mult, [x0, ("h", p)], [("pp", p)], 128, [fb])
-            if not cost["hr"] and n in cost["rsa"]:
-                at("rs")
-                act(lambda F=F, X=X, nf=nf: s.activation(xv(X, 2, nf), F[:, 128:128 + 64 * nf], M.Relu), [x0], [("rs", p)], 64 * nf, [fb])
+            if fa:
+                tt(T.OP[:, n // 2, 1:3, p, :], xv(X, 0, 2), F[:, 256:384], A.mult, [x0] + hk, [("OP", n, 1)], [fb])
+            else:
+                tt(xv(X, 5, 2), xv(X, 0, 2), F[:, 256:384], A.mult, [x0] + hk, [("pp", p)], [fb])
             if not last:
                 at("bb")
-                mm([(BB[:, 0:64], xt(X, 4, bit), T.IH[:, bit::2], 64) for bit in range(2)], ["IH", x0, ("th", p)], [bb], last=False)
-                mm([(BB[:, 0:64], xt(X, f, bit), T.IH[:, bit::2], 64) for f in (0, 1) for bit in range(2)], ["IH", x0, ("h", p)], [bb], first=False)
+                if dh:
+                    mm([(BB[:, 0:64], xt(X, 1, bit), T.IH[:, bit::2]) for bit in range(2)], ["IH", x0, hk[1]], [bb], last=False)
+                    mm([(BB[:, 0:64], xt(X, 4, bit), T.IH[:, bit::2]) for bit in range(2)], ["IH", x0, ("th", p)], [bb], first=False)
+                else:
+                    mm([(BB[:, 0:64], xt(X, 4, bit), T.IH[:, bit::2]) for bit in range(2)], ["IH", x0, ("th", p)], [bb], last=False)
+                    mm([(BB[:, 0:64], xt(X, f, bit), T.IH[:, bit::2]) for f in (0, 1) for bit in range(2)], ["IH", x0] + hk, [bb], first=False)
                 at("out")
-                ts(T.OUT[:, n * 64:n * 64 + 64], BB[:, 0:64], 2048.0, None, (A.add,), [], [("OUT", n)], 64, [bb])
+                ts(T.OUT[:, n * 64:n * 64 + 64], BB[:, 0:64], 2048.0, None, (A.add,), [], [("OUT", n)], [bb])
                 i = post(T.MSG[:, n * 64:n * 64 + 64], [T.OUT[:, n * 64:n * 64 + 64]], "next", "m%d" % n, [("OUT", n)], [("MSG", n)])
-                if not cost["sv"]:
-                    at("os")
-                    mm([(OB[:, 0:64], T.ID[:], o1, 64)] + [(OB[:, i:64:8], T.GT[:, s0 + i:s0 + 1024:8], row(5), 64) for i in range(8)],
-                       ["ID", ("OIN", n)] + gk, [ob], last=False)
-                at("ob")
-                mm([(OB[:, 0:64], m[:], xv(X, f), 64) for f, m in ((2, T.IN), (3, T.IH), (5, T.IH), (6, T.IH)) if f != 3 or cost["sv"]],
-                   ["IN", "IH", "IP", x0, ("rs", p), ("pp", p)], [ob], first=bool(cost["sv"]))
-                at("oo")
-                if cost["ooa"]:
-                    act(lambda n=n, OB=OB: s.activation(T.OOUT[:, n * 64:n * 64 + 64], OB[:, 0:64], M.Copy), [], [("OOUT", n)], 64, [ob])
-                else:
-                    vec(lambda n=n, OB=OB: v.tensor_copy(T.OOUT[:, n * 64:n * 64 + 64], OB[:, 0:64]), [], [("OOUT", n)], 64, [ob])
-                og = cost["og"]
-                if c % og == og - 1:
-                    a, b = (n + 1 - og) * 64, (n + 1) * 64
-                    omsg[0] = post(T.OIN[:, a + 256:b + 256], [T.OOUT[:, a:b]], "next", "o%d" % n, [("OOUT", k) for k in range(n + 1 - og, n + 1)],
-                                   [("OIN", k + NCH) for k in range(n + 1 - og, n + 1)], after=i)
-            else:
-                y0 = 2 * l0
-
-                def back(out, fields):
-                    return [(out[:, 0:128], xt(X, f, bit), (T.MN if f == 2 else T.MV)[:, bit * 128:bit * 128 + 128], 128)
-                            for f in fields for bit in range(2)]
-                at("ym")
-                short = True
-                for out, const, bank in ((BB, T.PB, bb), (OB, T.PO, ob))[:1 + short]:
-                    mm([(out[:, 0:128], T.PA[:], const[:], 128)], MVK, [bank], last=False)
-                at("bb")
-                mm(back(BB, (4,)), MVK + [x0, ("th", p)], [bb], first=False, last=False)
-                mm(back(BB, (0, 1)), MVK + [x0, ("h", p)], [bb], first=False)
-                at("ob")
-                if short:
-                    mm(back(OB, (2, 3)), MVK + [x0, ("rs", p)], [ob], first=False, last=False)
-                    mm(back(OB, (5, 6)), MVK + [x0, ("pp", p)], [ob], first=False)
-                else:
-                    mm([(OB[:, 256:320], m[:], xv(X, f), 64) for f, m in ((2, T.IN), (3, T.IH), (5, T.IH), (6, T.IH))],
-                       ["IN", "IH", x0, ("rs", p), ("pp", p)], [ob])
+            if fa:
+                if c % 2:
                     at("oo")
-                    vec(lambda OB=OB, X=X: v.tensor_copy(xv(X, 3), OB[:, 256:320]), [x0], [("rs", p)], 64, [ob])
-                    at("ob")
-                    mm([(OB[:, 0:128], T.PA[:], T.PO[:], 128)] + back(OB, (3,)), MVK + [x0, ("rs", p)], [ob])
+                    omsg[0] = send(T.OIN[:, n * 64 + 192:n * 64 + 320], [T.OP[:, n // 2, f] for f in range(3)], "next", "o%d" % n,
+                                   [("OP", k, f) for k in (n - 1, n) for f in range(2)], after=i, alu=1)
+                    arrive(omsg[0], "o%d" % n, [("OIN", k + NCH) for k in (n - 1, n)], peers["next"][3])
+            elif not last:
+                at("os")
+                mm([(OB[:, i:64:8], T.GT[:, s0 + i:s0 + 1024:8], T.FS[:, 48:56]) for i in range(8)], FSK + gk, [ob], last=False)
+                at("ob")
+                mm([(OB[:, 0:64], T.IH[:], xv(X, f)) for f in (5, 6)], ["IH", x0, ("pp", p)], [ob], first=False)
+                at("oo")
+                tt(T.OOUT[:, n * 64:n * 64 + 64], OB[:, 0:64], xv(X, 2), A.add, [x0, ("rs", p)], [("OOUT", n)], [ob])
+                if c % 2:
+                    a, b = (n - 1) * 64, (n + 1) * 64
+                    omsg[0] = post(T.OIN[:, a + 256:b + 256], [T.OOUT[:, a:b]], "next", "o%d" % n, [("OOUT", k) for k in (n - 1, n)],
+                                   [("OIN", k + NCH) for k in (n - 1, n)], after=i)
+            else:
+                packed = c < cost["pk"]
+                O2, o2 = (BB, bb) if packed else (OB, ob)
+
+                def back(out, fields, m):
+                    return [(out[:, 0:128], xt(X, f, bit), m[:, bit * 128:bit * 128 + 128]) for f in fields for bit in range(2)]
+                at("ym")
+                mm([(BB[:, 0:128], T.PA[:], T.PB[:])], MVK, [bb], last=False)
+                if not packed:
+                    mm([(OB[:, 0:128], T.PA[:], T.PO[:])], MVK, [ob], last=False)
+                at("bb")
+                mm(back(BB, (1,) if dh else (0, 1), T.MW), MVK + [x0] + hk, [bb], first=False, last=False)
+                mm(back(BB, (4,), T.MW), MVK + [x0, ("th", p)], [bb], first=False, last=not packed)
+                at("ob")
+                mm(back(O2, (2,), T.MV), MVK + [x0, ("rs", p)], [o2], first=False, last=False)
+                mm(back(O2, (5, 6), T.MV), MVK + [x0, ("pp", p)], [o2], first=False)
                 at("y")
-                vec(lambda BB=BB: v.transpose(T.ZB[:], BB[:, 0:128]), [], ["ZB"], 128, [bb])
-                tt(T.YN[:, 0:64], T.ZB[:, :, 0:16], T.ZB[:, :, 16:32], A.max, ["ZB"], [("YN", 0)], 128)
-                vec(lambda OB=OB: v.transpose(T.ZO[:], OB[:, 0:128]), [], ["ZO"], 128, [ob])
-                ts(T.YN[:, 64:128], T.YN[:, 0:64], V - 1, None, (A.bitwise_and,), [("YN", 0)], [("YN", 1)], 64)
-                tt(T.YO[:, y0 + 64:y0 + 128], T.ZO[:, :, 0:16], T.ZO[:, :, 16:32], A.max, ["ZO"], [("YO", c, 1)], 128)
-                vec(lambda y0=y0: v.tensor_copy(T.YO[:, y0:y0 + 64], T.YN[:, 64:128]), [("YN", 1)], [("YO", c, 0)], 64)
-                post(T.YI[:, y0:y0 + 128], [T.YO[:, y0:y0 + 128]], "prev", "y%d" % c, [("YO", c, 0), ("YO", c, 1)], [("YI", c)], more=300.0)
-                dma(T.yb[:, l0:l0 + 64], T.YI[:, y0:y0 + 64], [("YI", c)], [], 32768, sem="outs")
-                dma(T.yo[:, l0:l0 + 64], T.YI[:, y0 + 64:y0 + 128], [("YI", c)], [], 32768, q="A" if c == NCH - 1 else "S", sem="outs")
-                if c < 2 and PAIR:
-                    if c == 1:
-                        at("fold")
-                        i = send(T.HE[:, 2304:2432], [W[:, k * 128:(k + 1) * 128] for k in range(16)], "pair", "f%d" % NF,
-                                 [("W", j, k) for j in (n - 1, n) for k in range(16)], after=omsg[0])
-                        arrive(i, "e6", [("EIN", 9)], peers["back"][t], 1.8 * cost["lat"])
-                        ops[-1]["hold"] = 0.65 * cost["fold"]
-                    continue
-                at("tree")
-                tt(T.TR[:, s0:s0 + 512], wv(0, 8), wv(8, 16), A.max, wk, [("TR", p, 8)], 512)
-                a = s0
-                for k in (4, 2, 1):
-                    b = a + 128 * k
-                    tt(T.TR[:, b:b + k * 64] if k > 1 else T.PK[:, l0:l0 + 64], T.TR[:, a:a + k * 64], T.TR[:, a + k * 64:a + k * 128], A.max,
-                       [("TR", p, 2 * k)], [("TR", p, k) if k > 1 else ("PK", c)], k * 64)
-                    a = b
+                vec(lambda BB=BB, p=p: v.transpose(T.ZB[:, p], BB[:, 0:128]), [], [("ZB", p)], [bb])
+                tt(T.YO[:, l0:l0 + 64], T.ZB[:, p, :, 0:16], T.ZB[:, p, :, 16:32], A.max, [("ZB", p)], [("YO", c)])
+                if not packed:
+                    y0 = 2 * l0
+                    ts(T.YN[:, l0:l0 + 64], T.YO[:, l0:l0 + 64], 8, V - 1, (A.logical_shift_right, A.bitwise_and), [("YO", c)], [("YN", c, 0)])
+                    vec(lambda l0=l0, y0=y0: v.tensor_copy(T.YS[:, y0:y0 + 64], T.YN[:, l0:l0 + 64]), [("YN", c, 0)], [("YS", c, 0)])
+                    at("yo")
+                    vec(lambda OB=OB, p=p: v.transpose(T.ZB[:, 2 + p], OB[:, 0:128]), [], [("ZO", p)], [ob])
+                    tt(T.YS[:, y0 + 64:y0 + 128], T.ZB[:, 2 + p, :, 0:16], T.ZB[:, 2 + p, :, 16:32], A.max, [("ZO", p)], [("YS", c, 1)])
+                    at("y")
+                    post(T.YR[:, y0:y0 + 128], [T.YS[:, y0:y0 + 128]], "prev", "y%d" % c, [("YS", c, 0), ("YS", c, 1)], [("YR", c)])
+                    dma(T.yb[:, l0:l0 + 64], T.YR[:, y0:y0 + 64], [("YR", c)], [], sem="outs")
+                    dma(T.yo[:, l0:l0 + 64], T.YR[:, y0 + 64:y0 + 128], [("YR", c)], [], q="A" if c == NCH - 1 else "S", sem="outs")
+                else:
+                    post(T.YI[:, l0:l0 + 64], [T.YO[:, l0:l0 + 64]], "prev", "y%d" % c, [("YO", c)], [("YI", c)])
+                if c >= NL:
+                    at("tree")
+                    tt(T.TR[:, s0:s0 + 512], wv(0, 8), wv(8, 16), A.max, wk, [("TR", p, 8)])
+                    a = s0
+                    for k in (4, 2, 1):
+                        b = a + 128 * k
+                        tt(T.TR[:, b:b + k * 64] if k > 1 else T.PK[:, l0:l0 + 64], T.TR[:, a:a + k * 64], T.TR[:, a + k * 64:a + k * 128], A.max,
+                           [("TR", p, 2 * k)], [("TR", p, k) if k > 1 else ("PK", c)])
+                        a = b
+                if c == cost["pk"] - 1:
+                    at("un")
+                    a, b = 0, l0 + 64
+                    yk = [("YI", j) for j in range(a // 64, b // 64)]
+                    ts(T.YN[:, a:b], T.YI[:, a:b], 8, V - 1, (A.logical_shift_right, A.bitwise_and), yk, [("YN", c, 0)])
+                    ts(T.YN[:, 256 + a:256 + b], T.YI[:, a:b], 255, None, (A.bitwise_and,), yk, [("YN", c, 1)])
+                    vec(lambda a=a, b=b: v.tensor_copy(T.YF[:, a:b], T.YN[:, a:b]), [("YN", c, 0)], [("YF", c, 0)])
+                    ts(T.YF[:, 256 + a:256 + b], T.YN[:, 256 + a:256 + b], -1.0, None, (A.add,), [("YN", c, 1)], [("YF", c, 1)])
+                    dma(T.yb[:, a:b], T.YF[:, a:b], [("YF", c, 0)], [], sem="outs")
+                    dma(T.yo[:, a:b], T.YF[:, 256 + a:256 + b], [("YF", c, 1)], [], sem="outs")
+                if c == NL - 1:
+                    at("fold")
+                    i = send(T.HE[:, 2304:2304 + 64 * NL], [W[:, k * 64 * NL:(k + 1) * 64 * NL] for k in range(16)], LAST, "f%d" % NF,
+                             [("W", j, k) for j in range(n - c, n + 1) for k in range(16)], after=omsg[0])
+                    arrive(i, "e6", [("EIN", 9)], peers["back"][t])
 
         if not last:
             at("fold")
-            side = SIDE if t else 0
+            side = SIDE[t]
             wall = [("W", t * NCH + c, k) for c in range(NCH) for k in range(16)]
             i = send(T.HE[:, t * 256:(t + 1) * 256], [W[:, k * 256:(k + 1) * 256] for k in range(side, 16)], "help", "f%d" % t, wall)
-            arrive(i, "e%d" % t, [("EIN", t)], peers["back"][t], 1.6 * cost["lat"], kind="fold")
-            ops[-1]["fold"] = (16 - side) / 16
+            arrive(i, "e%d" % t, [("EIN", t)], peers["back"][t])
             if side:
                 at("side")
                 i = send(T.HE[:, (4 + t) * 256:(5 + t) * 256], [W[:, k * 256:(k + 1) * 256] for k in range(side)], "pair", "g%d" % t, wall)
-                arrive(i, "b%d" % t, [("EIN", 4 + t)], peers["back"][t], 1.8 * cost["lat"])
-                ops[-1]["hold"] = side / 16 * cost["fold"]
+                arrive(i, "b%d" % t, [("EIN", 4 + t)], peers["back"][t])
         else:
             at("e")
-            a = 128 if PAIR else 0
-            post(T.EIN[:, 2304 + a:2560], [T.PK[:, a:256]], "prev", "e5", [("PK", c) for c in range(a // 64, NCH)], [("EIN", 10)] + [("EIN", 9)] * (a == 0))
+            post(T.EIN[:, 2304 + 64 * NL:2560], [T.PK[:, 64 * NL:256]], "prev", "e5", [("PK", c) for c in range(NL, NCH)], [("EIN", 10)])
             at("em")
-            if SIDE:
-                tt(T.YE[:, 0:512], T.EIN[:, 0:512], T.EIN[:, 1280:1792], A.max, [("EIN", j) for j in (0, 1, 5, 6)], [("YE", 0)], 512)
-                tt(T.YE[:, 512:1024], T.EIN[:, 512:1024], T.EIN[:, 1792:2304], A.max, [("EIN", j) for j in (2, 3, 7, 8)], [("YE", 1)], 512)
-                tt(T.YE[:, 0:512], T.YE[:, 0:512], T.YE[:, 512:1024], A.max, [("YE", 0), ("YE", 1)], [("YE", 0)], 512)
-            else:
-                tt(T.YE[:, 0:512], T.EIN[:, 0:512], T.EIN[:, 512:1024], A.max, [("EIN", j) for j in range(4)], [("YE", 0)], 512)
-            tt(T.YE[:, 512:768], T.YE[:, 0:256], T.YE[:, 256:512], A.max, [("YE", 0)], [("YE", 1)], 256)
+            tt(T.YE[:, 0:512], T.EIN[:, 0:512], T.EIN[:, 1280:1792], A.max, [("EIN", j) for j in (0, 1, 5, 6)], [("YE", 0)])
+            tt(T.YE[:, 512:1024], T.EIN[:, 512:1024], T.EIN[:, 1792:2304], A.max, [("EIN", j) for j in (2, 3, 7, 8)], [("YE", 1)])
+            tt(T.YE[:, 0:512], T.YE[:, 0:512], T.YE[:, 512:1024], A.max, [("YE", 0), ("YE", 1)], [("YE", 0)])
+            tt(T.YE[:, 512:768], T.YE[:, 0:256], T.YE[:, 256:512], A.max, [("YE", 0)], [("YE", 1)])
+            tt(T.YE[:, 768:1024], T.YE[:, 512:768], T.EIN[:, 1024:1280], A.max, [("YE", 1), ("YE", 0), ("EIN", 4)], [("YE", 2)])
             at("ef")
             for c in range(NCH):
-                src = T.EIN[:, 2304 + c:2432:2] if c < 2 and PAIR else T.EIN[:, 2304 + c * 64:2368 + c * 64]
-                tt(T.YE[:, c * 64:c * 64 + 64], T.YE[:, 512 + c:768:NCH], src, A.max, [("YE", 1), ("EIN", 9 + c // 2)], [("YE", 2, c)], 64)
-            for c in range(NCH):
-                tt(T.YE[:, 256 + c * 64:320 + c * 64], T.YE[:, c * 64:c * 64 + 64], T.EIN[:, 1024 + c:1280:NCH], A.max,
-                   [("YE", 2, c), ("EIN", 4)], [("YE", 3, c)], 64)
-            dma(T.ye[:], T.YE[:, 256:512], [("YE", 3, c) for c in range(NCH)], [], 65536, sem="outs")
+                src = T.EIN[:, 2304 + c:2304 + 64 * NL:NL] if c < NL else T.EIN[:, 2304 + c * 64:2368 + c * 64]
+                tt(T.YE[:, 256 + c * 64:320 + c * 64], T.YE[:, 768 + c:1024:NCH], src, A.max, [("YE", 2), ("EIN", 9 + (c >= NL))], [("YE", 3, c)])
+            dma(T.ye[:], T.YE[:, 256:512], [("YE", 3, c) for c in range(NCH)], [], sem="outs")
     return ops
 
 
@@ -644,10 +513,6 @@ def link(ops):
             rd[k] = []
         d.pop(o["i"], None)
         o["deps"] = [(j, w and not (o["eng"] == "P" and ops[j]["eng"] == "P")) for j, w in d.items()]
-    seq = sorted((o["slot"], o["i"]) for o in ops if o.get("slot") is not None)
-    for (_, i), (_, j) in zip(seq, seq[1:]):
-        if i not in [x for x, w in ops[j]["deps"]]:
-            ops[j]["deps"].append((i, False))
 
 
 def lines(ops, order):
@@ -666,25 +531,26 @@ def lines(ops, order):
             k = int(k or len(calls))
             out[e] += calls[:k]
             del calls[:k]
-    out["S"] = [o["i"] for o in ops if o["eng"] == "S"]
-    assert sum(len(x) for x in out.values()) == len([o for o in ops if o["eng"]]), [k for k, x in left.items() if x and k[0] not in ("S", None)]
+    assert sum(len(x) for x in out.values()) == len([o for o in ops if o["eng"]]), [k for k, x in left.items() if x and k[0]]
     return out
 
 
 def merge(ops, line):
     done, out, at = [False] * len(ops), [], {e: 0 for e in line}
-    landing = {o["after"]: o["i"] for o in ops if not o["eng"]}
+    landing = {}
+    for o in ops:
+        if not o["eng"]:
+            landing.setdefault(o["after"], []).append(o["i"])
     while len(out) < len(ops):
         n = len(out)
         for e in line:
             while at[e] < len(line[e]) and all(done[j] for j, w in ops[line[e][at[e]]]["deps"]):
                 i = line[e][at[e]]
                 at[e] += 1
-                for k in (i, landing.get(i)):
-                    if k is not None:
-                        done[k] = True
-                        ops[k]["st"] = len(out)
-                        out.append(k)
+                for k in [i] + landing.get(i, []):
+                    done[k] = True
+                    ops[k]["st"] = len(out)
+                    out.append(k)
         if len(out) == n:
             raise ValueError([(e, ops[line[e][at[e]]]["tag"], ops[line[e][at[e]]]["n"]) for e in line if at[e] < len(line[e])])
     return out
@@ -716,6 +582,9 @@ def emit(g, T, ops, order):
         if o["kind"] == "send":
             count["sent"] = count.get("sent", 0) + o["inc"]
             continue
+        if o["kind"] == "sig":
+            o["mark"], o["know"] = (o["sem"], 1), {o["sem"]: 1}
+            continue
         sem, inc = (o["sem"], 16) if o["kind"] == "dma" else ("c" + e, 1)
         for x in ins:
             x.then_inc(T.sem[sem], inc)
@@ -745,6 +614,18 @@ def fold_mask(T, topo, rank):
     return topo.mask(core, helper_of(T, topo, rank)) & ~topo.mask(core, T.cores[(rank + 1) % len(T.cores)])
 
 
+def peers_of(T, topo, rank):
+    n, core = len(T.cores), T.cores[rank]
+    before = T.cores[(rank - 1) % n]
+    lanes = topo.engines(core, before)
+    return dict(next=way(topo, core, T.cores[(rank + 1) % n]), prev=way(topo, core, T.cores[(rank - 1) % n]),
+                help=way(topo, core, helper_of(T, topo, rank), fold_mask(T, topo, rank)),
+                pair=way(topo, core, helper_of(T, topo, rank), topo.mask(core, T.cores[(rank + 1) % n])),
+                wide=way(topo, core, helper_of(T, topo, rank)),
+                half=[way(topo, core, before, sum(1 << e for e in part)) for part in (lanes[:len(lanes) // 2], lanes[len(lanes) // 2:])],
+                back=[way(topo, helper_of(T, topo, (rank + t) % n), core)[3] for t in range(STEPS)])
+
+
 def rank_program(g, core, T, topo):
     n = len(T.cores)
     rank = T.rank_of(core)
@@ -755,18 +636,14 @@ def rank_program(g, core, T, topo):
                 side, sent = way(topo, T.cores[q], T.cores[(q + 1) % n])[3], 0
                 jobs = [(0, "f0", main, "e0", 0, 256)]
                 for t in range(1, NF):
-                    jobs += [(t, "g%d" % t, side, "b%d" % t, (4 + t) * 256, 256)] * (SIDE > 0) + [(t, "f%d" % t, main, "e%d" % t, t * 256, 256)]
-                for t, landed, count, sem, a, width in jobs + [(NF, "f%d" % NF, side, "e6", 2304, 128)] * PAIR:
+                    jobs += [(t, "g%d" % t, side, "b%d" % t, (4 + t) * 256, 256), (t, "f%d" % t, main, "e%d" % t, t * 256, 256)]
+                for t, landed, count, sem, a, width in jobs + [(NF, "f%d" % NF, peers_of(T, topo, q)[LAST][3], "e6", 2304, 64 * NL)]:
                     rid, pid, mask, engines = way(topo, core, T.cores[(q - t) % n])
                     g.wait_ge(T.sem[landed], count)
                     g.remote_dma(T.EIN[:, a:a + width], T.HE[:, a:a + width], T.sem[sem], T.sem.sent, pid, rid, mask)
                     sent += engines
                 g.wait_ge(T.sem.sent, sent)
         return
-    peers = dict(next=way(topo, core, T.cores[(rank + 1) % n]), prev=way(topo, core, T.cores[(rank - 1) % n]),
-                 help=way(topo, core, helper_of(T, topo, rank), fold_mask(T, topo, rank)),
-                 pair=way(topo, core, helper_of(T, topo, rank), topo.mask(core, T.cores[(rank + 1) % n])),
-                 back=[way(topo, helper_of(T, topo, (rank + t) % n), core)[3] for t in range(STEPS)])
-    ops = build(g, T, peers, COST)
+    ops = build(g, T, peers_of(T, topo, rank), COST)
     link(ops)
     emit(g, T, ops, merge(ops, lines(ops, ORDER)))

from concourse.bass import DstId, RemoteDMATransfer
from concourse.mybir import AluOpType, ActivationFunctionType

V, STEPS, NCH = 4096, 6, 4
NM = (STEPS - 1) * NCH
NF = STEPS - 1
SIDE = (0, 2, 2, 2, 2)
NL = 2
LAST = "pair"
BIG = 12582912.0
BF, F32, I32, U16, F16 = "bfloat16", "float32", "int32", "uint16", "float16"

SCRATCH = {
    "WP": ("sbuf", [128, V + 16], BF), "RLW": ("sbuf", [128, V + 32], BF), "TAB": ("sbuf", [128, 2 * V + 32], BF),
    "RLI": ("sbuf", [128, 256], I32), "RLB": ("sbuf", [128, 256], BF), "RLL": ("sbuf", [128, 256], BF),
    "CBI": ("sbuf", [128, 256], I32), "COI": ("sbuf", [128, 256], I32), "L0": ("sbuf", [128, 256], U16),
    "CY": ("sbuf", [128, 16, 32], F16), "CZ": ("sbuf", [128, 16, 32], F16), "CS": ("sbuf", [128, 16, 16], F16),
    "OY": ("sbuf", [128, 16, 32], F16), "OZ": ("sbuf", [128, 16, 32], F16),
    "COX": ("sbuf", [128, 520], BF),
    "DMI": ("sbuf", [128, 2, 16, 16], I32), "DMR": ("sbuf", [128, 16, 32], F16),
    "DMU": ("sbuf", [128, 16, 32], F16), "DMZ": ("sbuf", [128, 512], U16),
    "OMI": ("sbuf", [128, 512], I32), "OMB": ("sbuf", [128, 512], BF),
    "PC": ("sbuf", [128, 4], I32), "PG": ("sbuf", [128, 4], I32), "PD": ("sbuf", [128, 4], I32), "MK": ("sbuf", [128, 4], F32),
    "LO": ("sbuf", [128, 256], BF), "HI": ("sbuf", [128, 256], BF),
    "IB": ("sbuf", [128, 16, 8], BF), "IF": ("sbuf", [128, 128], F32), "IH": ("sbuf", [128, 128], F16),
    "ZR": ("sbuf", [128, 1024], BF), "SEL": ("sbuf", [128, 144], BF), "FS": ("sbuf", [128, 64], BF),
    "MV": ("sbuf", [128, 256], F16), "MW": ("sbuf", [128, 256], F16),
    "PA": ("sbuf", [128, 4, 32], BF), "PB": ("sbuf", [128, 4, 32], BF), "PO": ("sbuf", [128, 4, 32], BF),
    "X0": ("sbuf", [128, 113, 8], F16), "X1": ("sbuf", [128, 113, 8], F16),
    "IND": ("sbuf", [128, 2048], BF), "GT": ("sbuf", [128, 2048], BF), "TR": ("sbuf", [128, 2048], BF),
    "B": ("sbuf", [128, 256], F32), "IDX": ("sbuf", [128, 256], U16),
    "MSG": ("sbuf", [128, NM * 64], U16), "OUT": ("sbuf", [128, NM * 64], U16),
    "OIN": ("sbuf", [128, STEPS * NCH * 64], BF), "OOUT": ("sbuf", [128, NM * 64], BF),
    "OP": ("sbuf", [128, NM // 2, 3, 2, 64], BF),
    "PK": ("sbuf", [128, 256], BF), "EIN": ("sbuf", [128, 2560], BF), "HE": ("sbuf", [128, 2560], BF), "YE": ("sbuf", [128, 1024], BF),
    "YS": ("sbuf", [128, 512], F32), "YR": ("sbuf", [128, 512], F32),
    "ZB": ("sbuf", [128, 4, 4, 32], F32), "YO": ("sbuf", [128, 256], I32), "YI": ("sbuf", [128, 256], I32),
    "YN": ("sbuf", [128, 512], I32), "YF": ("sbuf", [128, 512], F32),
    "JB0": ("psum", [128, 512], F32), "JB1": ("psum", [128, 512], F32), "BB0": ("psum", [128, 512], F32), "BB1": ("psum", [128, 512], F32),
    "F0": ("psum", [128, 512], F32), "F1": ("psum", [128, 512], F32), "OB0": ("psum", [128, 512], F32), "OB1": ("psum", [128, 512], F32),
}
SCRATCH.update({"W%d" % t: ("sbuf", [128, V], BF) for t in range(STEPS)})
SEMAPHORES = (["cA", "cV", "cP", "cG", "sent", "outs", "a_rl", "go"] + ["d%d" % i for i in range(36)]
              + ["m%d" % n for n in range(NM)] + ["o%d" % n for n in range(NM)] + ["y%d" % c for c in range(NCH)]
              + ["e%d" % t for t in range(STEPS + 1)] + ["f%d" % t for t in range(STEPS)]
              + ["g%d" % t for t in range(1, NF)] + ["b%d" % t for t in range(1, NF)])

COST = dict(wa=13, ga=46, wx={0: 8, 1: 16, 2: 16, 3: 16, 4: 10, 20: 13, 21: 13, 22: 14, 23: 11},
            gx={0: 32, 1: 40, 2: 64, 3: 64, 20: 64, 21: 64, 22: 64, 23: 40}, ta="AVAVAVAV", gate=0, ra=3, pk=3, fa=1, dh=1, ne=3)
ORDER = dict(turns=(5, 20), queues=dict(
    A=('rp w0 w1 w2 tw tab w3 gt0 gt1 gt2 gt3 w4',
       'w0 gt-1',
       'w20 gt19 w21 gt20 w22 gt21 w23 gt22 gt23 y23'),
    V=('zr setup.1 sel.1 setup.1 rp setup.1 rl setup.1 cb.3 setup.1 sel cb setup b3 b0 b2 b1 '
       'w0 dm.2 c0.2 dm.2 c0 dm.1 cw0 om.1 dm.2 c1.1 dm.5 om.1 co.1 cw1 dm om co.1 c1.1 co.1 tab.3 co.1 tab co.3 c1 c2.1 idx0 c2.1 cw2 idx1 co gt0 c2 c3.1 th0 h0 idx2 cw3 rs0 out0 gt1 c3 late.1 th1 h1 pp0 late out1 idx3 h2.1 oo0 pp1 h2 rs1 th2 oo1 pp2 rs2 out2 w4 oo2 b4 cw4 c4',
       'th-2 h-2 w0 idx-1 pp-2 out-2 b0 c0.1 cw0 gt-1 c0.1 rs-2 c0 oo-2',
       'w20 th18 h18 b20 rs18 idx19 pp18 out18 c20.1 cw20 c20.1 gt19 c20 oo18 th19 h19 b21 idx20 rs19 pp19 out19 w21 oo19 cw21 c21.2 w22 c21 b22 rs20 h20.1 th20.1 h20 idx21 pp20 cw22 th20 c22 y20.1 w23 b23 th21.1 h21 idx22 th21 y20 pp21 rs21 cw23 c23 y21.1 tree22.1 idx23 y21 tree22.1 th22.1 h22 th22 rs22 pp22 gt23 tree23.1 y22.1 th23 y22 h23 rs23 tree23.1 pp23 tree23.1 tree22.1 y23.1 tree23 tree22 y23.1 yo23.1 y23.1 yo23 y23 em23.2 un22.2 em23.1 un22.1 em23.1 un22 em23 ef23'),
    P=('jb1 jb0 vote1.1 vote0 co.2 vote1.1 co.1 vote1 co jb2 vote2.2 jb3 f0 vote2 bb0 os0 vote3.1 f1 vote3 bb1 os1 ob0 f2 os2 ob1 bb2 ob2 f3 jb4 vote4',
       'bb-2 jb0 os-2 vote0.1 ob-2 f-1 vote0',
       'bb18 jb20 os18 ob18 vote20.2 f19 vote20 bb19 os19 ob19 jb21 ym20 vote21.1 ym21 f20 vote21 jb22 bb20 ob20 vote22.2 f21 vote22 bb21 ob21.2 jb23 ob21 vote23 ym22 f22 bb22 ob22 ym23 f23 bb23.1 ob23.1 bb23 ob23'),
    G=('setup if rl cox mat fs x late out0 fold3 out1 oo1 out2',
       'out-2 fold0 oo-2 side-1',
       'out18 side19 out19 oo19 fold21 y20 y21 y22 e23 y23'),
    S=('first wp maps rp.1 om.3 co rp om rlw tw tab', '', 'un22 y23 ef23')))
COST.update(fa=0, dh=1, ga=48)
ORDER["queues"].update(
    V=('zr setup.1 rp setup.1 sel.1 setup.2 rl cb.4 setup.1 cb.2 sel setup cb b2 b0 b3 w0 dm.1 c0.2 dm.1 c0 dm.2 b1 dm.1 om.1 cw0 om.1 dm.2 c1.1 dm.1 cw1 c1.1 dm.1 co.2 dm.1 idx0 dm om.1 co.1 tab.3 om tab c1 co.1 cw2 co.3 c2.2 idx1 co gt0 c2 c3.1 h0 th0 cw3 pp0 idx2 out0 gt1 c3 rs0 h1 th1 oo0 out1 pp1 idx3 h2 rs1 rs2 th2 pp2 late.1 oo1 late oo2 b4 out2 w4 cw4 c4',
       'w0 h-2 rs-2 th-2 idx-1 b0 pp-2 out-2 cw0 c0.2 gt-1 oo-2 c0',
       'w20 h18 th18 idx19 b20 rs18 pp18 out18 cw20 c20.2 gt19 oo18 c20 b21 h19 th19 idx20 pp19 rs19 out19 w21 cw21 oo19 c21.1 w22 c21 h20.1 b22 h20 idx21 rs20.1 th20 pp20 rs20 c22.1 cw22 c22.1 b23 c22 w23 y20.1 h21 rs21.1 th21 y20 idx22 rs21 pp21 cw23 c23 tree22.1 y21 tree22.1 idx23 h22 rs22.1 th22 pp22 rs22 gt23 tree23.1 y22 h23 rs23.1 th23 tree23.1 rs23 pp23 tree22.1 tree23.1 y23.1 tree23 tree22 y23.1 yo23.1 y23.1 yo23 y23 em23.2 un22.3 em23.1 un22 em23 ef23'),
    P=('jb0 vote0.1 jb1 vote0 vote1 jb2 co jb3 vote2.2 f0 vote2 bb0 os0 ob0 vote3.1 f1 vote3 bb1 os1 f2 os2 ob1 ob2 bb2 jb4 f3 vote4',
       'bb-2 jb0 os-2 ob-2 vote0.2 f-1 vote0',
       'bb18 os18 ob18 jb20 vote20.2 f19 vote20 bb19 os19 ob19 ym20 jb21 vote21.1 f20 vote21 jb22 bb20 ob20.1 ym21 ob20 vote22.1 f21 vote22 jb23 bb21 ym22 ob21 vote23 f22 bb22 ob22 f23 ym23 bb23 ob23'))
COST.update(fa=0, dh=0, ga=48)
ORDER["queues"].update(
    A=('rp w0 w1 w2 tab tw w3 gt0 gt1 gt2 gt3 w4', 'w0 gt-1', 'w20 gt19 w21 gt20 w22 gt21 w23 gt22 gt23 y23'),
    V=('zr setup.2 rp setup.2 rl cb.2 sel.1 setup.1 cb.1 sel cb setup b1 b0 b3 b2 w0 dm.2 c0.2 cw0 dm.2 c0 dm.1 om.2 c1.1 idx0 dm.4 om.1 dm.1 co.1 dm.1 co.1 dm c1.1 cw2 cw1 tab.3 om tab co.1 c1 co.4 c2.2 co idx1 gt0 c2 c3.1 th0 h0 idx2 cw3 out0 gt1 c3 pp0 h1 rs1 th1 late.1 idx3 rs0 pp1 out1 b4 h2 oo0 th2 pp2 oo1 w4 out2 rs2 late cw4 c4',
       'w0 b0 h-2 idx-1 th-2 rs-2 oo-3 pp-2 c0.1 out-2 cw0 c0.1 gt-1 c0',
       'w20 h18.1 th18 h18 oo17 idx19 b20 pp18 out18 c20.1 cw20 c20.1 gt19 rs18 c20 oo18 b21 th19 h19 idx20 rs19 w21 out19 cw21 pp19 c21.1 b22 oo19 w22 c21 rs20.1 th20 h20 idx21 pp20 cw22 rs20 c22.2 y20.1 b23 c22 w23 th21 h21 idx22 rs21.1 y20 pp21 rs21 cw23 c23.2 y21.1 c23 tree22.1 idx23 y21 tree22.1 h22 rs22.1 th22 pp22 rs22 gt23 tree23.1 y22.1 tree22.1 h23.1 rs23.1 y22 h23 th23 tree23.1 pp23 rs23 tree22 y23.1 tree23.1 y23.1 tree23 yo23.1 y23.1 yo23 y23 em23.2 un22.1 em23.1 un22.2 em23.1 un22 em23 ef23'),
    P=('jb1 jb0 vote0 vote1.1 jb2 vote1 co vote2.2 jb3 f0 vote2 bb0 os0 vote3.1 f1 vote3 os1 bb1 ob1 f2 ob0 os2 bb2 jb4 ob2 f3 vote4',
       'bb-2 os-2 ob-2 jb0 vote0.2 f-1 vote0',
       'bb18 jb20 os18 ym20 ob18 vote20.2 f19 vote20 os19 bb19 ob19 jb21 ym21 vote21.1 f20 vote21 jb22 bb20 ob20 vote22.2 f21 vote22 jb23 bb21 ob21 vote23 ym22 f22 bb22 ob22 f23 ym23 bb23 ob23'),
    G=('setup if rl cox mat fs x late out0 fold3 out1 oo1 out2', 'out-2 oo-3 side-1 fold0', 'oo17 out18 side19 out19 oo19 fold21 y20 y21 y22 e23 y23'),
    S=('first wp maps.7 rp.1 maps om co rlw.3 rp rlw tab tw', '', 'un22 y23 ef23'))


def build(g, T, peers, cost):
    ops = []
    A, M = AluOpType, ActivationFunctionType
    v, s, pe = g.vector, g.scalar, g.tensor
    nd = [0]
    now = [0, "setup"]

    def op(eng, fn, rd, wr, banks=(), kind="c", sem=None, after=None, inc=0):
        ops.append(dict(eng=eng, fn=fn, rd=rd, wr=wr, banks=banks, kind=kind, sem=sem, after=after, inc=inc,
                        i=len(ops), n=now[0], tag=now[1]))
        return len(ops) - 1

    def at(tag):
        now[1] = tag

    def vec(fn, rd, wr, banks=()):
        return op("V", lambda: [fn()], rd, wr, banks)

    def tt(out, a, b, alu, rd, wr, banks=()):
        return vec(lambda: v.tensor_tensor(out, a, b, alu), rd, wr, banks)

    def ts(out, a, s1, s2, ops2, rd, wr, banks=()):
        return vec(lambda: v.tensor_scalar(out, a, s1, s2, *ops2), rd, wr, banks)

    def gather(eng, out, win, rd, wr):
        if eng == "A":
            return op("A", lambda: [s.activation(out, win, M.Copy)], rd, wr)
        return op("V", lambda: [v.tensor_copy(out, win)], rd, wr)

    def mm(lst, rd, banks, first=True, last=True):
        return op("P", lambda: [pe.matmul(x[0], x[1], x[2], first and k == 0, last and k == len(lst) - 1) for k, x in enumerate(lst)],
                  rd, [], banks)

    def dma(out, in_, rd, wr, q="S", sem=None):
        if sem is None:
            sem = "d%d" % nd[0]
            nd[0] += 1
        qu = g.sync if q == "S" else g.scalar
        return op(q, lambda: [qu.dma_start(out, in_)], rd, wr, kind="dma", sem=sem)

    def send(dst, srcs, peer, sem, rd, after=None, alu=2):
        rid, pid, mask, engines = peers[peer]

        def fn():
            if len(srcs) == 1:
                g.remote_dma(dst, srcs[0], T.sem[sem], T.sem.sent, pid, rid, mask)
            else:
                g.remote_dma_fused([RemoteDMATransfer(dst_ids=[DstId(rid=rid, pnc=pid)], dma_engine_mask=mask,
                                                      remote_sem=T.sem[sem], srcs=srcs, dsts=[dst], alu_op=alu)],
                                   local_sem=T.sem.sent)
            return []
        return op("G", fn, rd, [], kind="send", after=after, inc=engines)

    def arrive(i, sem, wr, engines):
        op(None, None, [], wr, kind="arr", sem=sem, after=i, inc=engines)

    def post(dst, srcs, peer, sem, rd, wr, after=None):
        i = send(dst, srcs, peer, sem, rd, after)
        arrive(i, sem, wr, peers[peer][3])
        return i

    def post2(jobs, rd):
        def fn():
            g.remote_dma_fused([RemoteDMATransfer(dst_ids=[DstId(rid=rid, pnc=pid)], dma_engine_mask=mask, remote_sem=T.sem[sem],
                                                  srcs=[src], dsts=[dst], alu_op=0)
                                for (dst, src, sem, wr), (rid, pid, mask, engines) in zip(jobs, peers["half"])], local_sem=T.sem.sent)
            return []
        i = op("G", fn, rd, [], kind="send", inc=peers["prev"][3])
        for (dst, src, sem, wr), way_ in zip(jobs, peers["half"]):
            arrive(i, sem, wr, way_[3])

    def xv(buf, f, n=1):
        return buf[:, f * 16 + 1:(f + n) * 16:2, :]

    def xt(buf, f, bit):
        return buf[:, f * 16 + 1 - bit:f * 16 + 17 - bit, :]

    at("first")
    dma(T.RLI[:], T.rl[:], [], ["RLI"])
    dma(T.CBI[:], T.cb[:], [], ["CBI"])
    at("wp")
    dma(T.WP[:, V:V + 16], T.wp[:, 0:16], [], ["WPw"])
    dma(T.WP[:, 0:V], T.wp[:], [], ["WP"])

    at("rl")
    vec(lambda: v.tensor_copy(T.RLB[:], T.RLI[:]), ["RLI"], ["RLB"])
    i = post(T.RLL[:], [T.RLB[:]], "prev", "a_rl", ["RLB"], ["RLL"])
    GO = []
    if cost["gate"]:
        op("G", lambda: g.sem_inc(T.sem.go, 1), [], ["GO"], kind="sig", sem="go", after=i)
        GO = ["GO"]
    at("maps")
    for g0 in range(2):
        for k in range(4):
            dma(T.DMI[:, g0, k * 4:k * 4 + 4, :], T.dm[g0::2, k * 2048:(k + 1) * 2048], GO, [("DMI", g0, k)])
    at("om")
    for k in range(4):
        a = k % 2 * V + k // 2 * 2048
        dma(T.OMI[:, k * 128:(k + 1) * 128], T.om[:, a:a + 2048], GO, [("OMI", k)])
    at("co")
    dma(T.COI[:], T.co[:], GO, ["COI"])

    def iota(out, pattern, base, mult, wr):
        op("G", lambda: [g.iota(out, pattern, base, mult, allow_small_or_imprecise_dtypes=True)], [], wr)

    def mark(out, in_, pattern, base, mult, x, rd, wr, keep=A.not_equal):
        op("G", lambda: [g.affine_select(out, in_, pattern, keep, x, base, mult)], rd, wr)
    at("zr")
    vec(lambda: v.memset(T.ZR[:], 0.0), [], ["ZR"])
    at("setup")
    op("G", lambda: [g.iota(T.PC[:, 0:1], [[0, 1]], 0, 1)], [], ["PC"])
    iota(T.LO[:], [[1, 256]], 0, 0, ["LO"])
    ts(T.PG[:, 0:1], T.PC[:, 0:1], 4, 1, (A.logical_shift_right, A.bitwise_and), ["PC"], ["PG"])
    ts(T.PD[:, 0:1], T.PC[:, 0:1], 15, None, (A.bitwise_and,), ["PC"], ["PD"])
    for x in range(2):
        ts(T.MK[:, x:x + 1], T.PG[:, 0:1], float(x), None, (A.is_equal,), ["PG"], [("MK", x)])
    ts(T.MK[:, 2:3], T.PD[:, 0:1], -8.0, 256.0, (A.add, A.mult), ["PD"], ["PF"])
    ts(T.HI[:], T.ZR[:, 0:256], T.MK[:, 2:3], None, (A.add,), ["PF", "ZR"], ["HI"])

    at("rp")
    for k in range(4):
        if k < cost["ra"]:
            op("A", lambda k=k: [s.activation(T.RLW[:, 16 + k * 1024:16 + (k + 1) * 1024], T.ZR[:], M.Copy)], ["ZR"], [("RLW0", k)])
        else:
            vec(lambda k=k: v.memset(T.RLW[:, 16 + k * 1024:16 + (k + 1) * 1024], 0.0), [], [("RLW0", k)])
    R0K = [("RLW0", k) for k in range(4)]
    dma(T.RLW[3::16, 16:16 + V], T.HI[:], R0K + ["HI"], [("RLW", 3)])
    dma(T.RLW[4::16, 16:16 + V], T.LO[:], R0K + ["LO"], [("RLW", 4)])
    at("rlw")
    for f in range(3):
        dma(T.RLW[f::16, 16 - f:16 - f + V], T.RLL[:], R0K + ["RLL"], [("RLW", f)])
    for f in (1, 2):
        dma(T.RLW[f::16, 16 - f + V:18 - f + V], T.RLL[0::16, 0:2], R0K + ["RLL"], [("RLW", 10 + f)])
    RLK = R0K + [("RLW", f) for f in (0, 1, 2, 3, 4, 11, 12)]

    def turn(src, key, add, Y, Z):
        for x in range(2):
            ts(Y[:, :, x * 16:x * 16 + 16], src[:], add, T.MK[:, x:x + 1], (A.add, A.mult), [key, ("MK", x)], [(key, "Y", x)])
        vec(lambda: v.transpose(Z[:], Y[:]), [(key, "Y", 0), (key, "Y", 1)], [(key, "Z")])

    at("cb")
    turn(T.CBI, "CBI", -2048.0, T.CY, T.CZ)
    tt(T.CS[:], T.CZ[:, :, 0:16], T.CZ[:, :, 16:32], A.add, [("CBI", "Z")], [("CBI", "S")])
    for h in range(4):
        ts(T.L0[:, h::4], T.CS[:, h::4, :], 2048.0, None, (A.add,), [("CBI", "S")], [("L0", h)])
    L0K = [("L0", h) for h in range(4)]

    at("dm")
    for g0 in range(2):
        for m in range(2):
            ts(T.DMR[:, :, g0 * 16 + m:g0 * 16 + 16:2], T.DMI[:, g0, m * 8:m * 8 + 8, :], -2048.0, None, (A.add,),
               [("DMI", g0, 2 * m), ("DMI", g0, 2 * m + 1)], [("DMR", g0, m)])
    vec(lambda: v.transpose(T.DMU[:], T.DMR[:]), [("DMR", g0, m) for g0 in range(2) for m in range(2)], ["DMU"])
    for q in range(8):
        ts(T.DMZ[:, q::8], T.DMU[:, q::8, :], 2048.0, None, (A.add,), ["DMU"], [("DMZ", q)])
    ZK = [("DMZ", q) for q in range(8)]

    at("sel")
    vec(lambda: v.memset(T.SEL[:], 0.0), [], ["SEL"])
    vec(lambda: v.memset(T.SEL[:, 15::16], 1.0 / 128), [], ["SEL"])
    for tag, buf in (("if", "IF"), ("mat", "IB"), ("mat", "IH")):
        at(tag)
        mark(T[buf][:], T.ZR[:, 0:128], [[-1, 128]], 0, 1, 1.0, ["ZR"], [buf])
    at("cox")
    iota(T.COX[:], [[0, 520]], 0, 0, ["COX0"])
    at("x")
    for p in range(2):
        mark(T["X%d" % p][:, 0:113:2, :], T.ZR[:, 0:456], [[0, 456]], 0, 0, 0.0, ["ZR"], [("X0", p)])
    at("fs")
    for a, b, r, step, x, new in ((0, 3, 5, 0, -1.0, 1), (3, 4, 3, 0, 1.0, 1), (4, 6, 0, 1, -1.0, 1), (6, 7, 5, 0, 1.0, 1),
                                  (0, 3, 0, 0, 1.0, 0), (3, 4, 4, 0, 1.0, 0), (1, 3, 1, 0, 1.0, 0), (2, 3, 2, 0, 1.0, 0),
                                  (7, 8, 0, 0, 1.0, 1), (7, 8, 1, 0, 1.0, 0), (7, 8, 2, 0, 1.0, 0)):
        fk = [("FS", f) for f in range(a, b)]
        mark(T.FS[:, a * 8:b * 8], (T.ZR if new else T.FS)[:, a * 8:b * 8], [[-step, b - a], [-16, 8]], -r, 1, x, ["ZR"] + fk * (1 - new), fk)
    FSK = [("FS", f) for f in range(8)]

    at("om")
    for k in range(4):
        vec(lambda k=k: v.tensor_copy(T.OMB[:, k // 2 * 256 + k % 2:k // 2 * 256 + 256:2], T.OMI[:, k * 128:(k + 1) * 128]),
            [("OMI", k)], [("OMB", k)])
    at("co")
    turn(T.COI, "COI", 1.0, T.OY, T.OZ)
    for h in range(4):
        tt(T.COX[:, 2 * h + 1:513:8], T.OZ[:, h::4, 0:16], T.OZ[:, h::4, 16:32], A.add, [("COI", "Z"), "COX0"], [("COX", h)])
    for c in range(NCH):
        mm([(T.OB1[:, c * 64:c * 64 + 64], T.COX[:, 128 * c + 1 - bit:128 * c + 129 - bit], T.IB[:, bit::2, :])
            for bit in range(2)], ["IB", "COX0"] + [("COX", h) for h in range(4)], ["OB1"])
    vec(lambda: v.tensor_copy(T.OIN[:, 0:256], T.OB1[:, 0:256]), [], [("OIN", c) for c in range(NCH)], ["OB1"])

    at("tw")
    TK = [("TAB", 8)]
    gather("A", T.TAB[:, 2 * V:2 * V + 32], T.RLW[:, 16:16 + V].indirect(T.DMZ[:, 0:2]), RLK + ZK, TK)
    dma(T.TAB[5::16, 2 * V:2 * V + 4], T.OMB[0::16, 0:4], [("OMB", 0), ("OMB", 1)], TK)
    at("tab")
    for half in range(2):
        pk = [("TAB", k) for k in range(4 * half, 4 * half + 4)]
        for _, k in pk:
            gather(cost["ta"][k], T.TAB[:, k * 1024:(k + 1) * 1024], T.RLW[:, 16:16 + V].indirect(T.DMZ[:, k * 64:(k + 1) * 64]),
                   RLK + ZK, [("TAB", k)])
        dma(T.TAB[5::16, half * V:(half + 1) * V], T.OMB[:, half * 256:(half + 1) * 256], [("OMB", 2 * half), ("OMB", 2 * half + 1)], pk)
        TK = TK + pk

    at("late")
    for bit in range(2):
        for buf, x in (("MV", 1.0), ("MW", 256.0)):
            mark(T[buf][:, bit * 128:bit * 128 + 128], T.ZR[:, 0:128], [[2, 4], [0, 2], [8, 16]], bit, -1, x, ["ZR"], [(buf, bit)])
    for x in range(2):
        mark(T.PA[:, :, x * 16:x * 16 + 16], T.ZR[:, 0:64], [[0, 64]], (-64, 63)[x], (1, -1)[x], 1.0, ["ZR"], [("PA", x)], A.is_ge)
    ts(T.PB[:], T.PA[:], 24576.0, -16384.0, (A.mult, A.add), [("PA", 0), ("PA", 1)], ["PB"])
    ts(T.PO[:], T.PA[:], 128.0 - 1.0 / 64, -128.0, (A.mult, A.add), [("PA", 0), ("PA", 1)], ["PO"])
    MVK = [("MV", 0), ("MV", 1), ("MW", 0), ("MW", 1), ("PA", 0), ("PA", 1), "PB", "PO"]

    omsg = [None]
    for t in range(STEPS):
        last = t == STEPS - 1
        W = T["W%d" % t]
        for c in range(NCH):
            l0, n = c * 64, t * NCH + c
            p = n % 2
            now[0] = n
            X, JB, BB, F, OB = T["X%d" % p], T["JB%d" % p], T["BB%d" % p], T["F%d" % p], T["OB%d" % p]
            jb, bb, fb, ob, x0, s0 = "JB%d" % p, "BB%d" % p, "F%d" % p, "OB%d" % p, ("X0", p), p * 1024
            lst, c0, lk = (T.L0, l0, L0K) if t == 0 else (T.MSG, (n - NCH) * 64, [("MSG", n - NCH)])
            wa = cost["wx"].get(n, cost["wa"])
            side, w0 = (NCH, c) if not last else (NL, c) if c < NL else (1, c * 1024)

            def wv(a, b, e=0, ne=1):
                return W[:, w0 + (a * 64 + e) * side:w0 + (b * 64 - 1) * side + 1:side * ne]
            at("w")
            for eng, a, b in (("A", 0, wa), ("V", wa, 16)):
                if b > a:
                    gather(eng, wv(a, b), T.WP[:, 0:V + 16].indirect(lst[:, c0 + a * 4:c0 + b * 4]),
                           ["WP", "WPw"] + lk, [("W", n, k) for k in range(a, b)])
            wk = [("W", n, k) for k in range(16)]
            at("b")
            ts(T.B[:, l0:l0 + 64], lst[:, c0:c0 + 64], 2.0, -1.0 / 256, (A.mult, A.add), lk, [("B", c)])
            at("jb")
            mm([(JB[:, 0:64], T.IF[:], T.B[:, l0:l0 + 64])], ["IF", ("B", c)], [jb], last=False)
            at("cw")
            tt(T.IND[:, s0 + 960:s0 + 1024], wv(15, 16), wv(0, 1), A.is_gt, [wk[15], wk[0]], [("IND", p, 15, e) for e in range(4)])
            parts = {1: ((0, 1),), 2: ((0, 2), (1, 2)), 3: ((0, 2), (1, 4), (3, 4))}[cost["ne"]]
            for j, (e, st) in enumerate(parts):
                at("c")
                tt(T.IND[:, s0 + e:s0 + 960:st], wv(0, 15, e, st), wv(1, 16, e, st), A.is_gt, wk,
                   [("IND", p, k, x) for k in range(15) for x in range(e, 4, st)])
                at("vote")
                mm([(JB[:, 0:64], T.SEL[:, 15 - r:143 - r], T.IND[:, s0 + r:s0 + 1024:16]) for r in range(e, 16, st)],
                   ["SEL"] + [("IND", p, k, x) for k in range(16) for x in range(e, 4, st)], [jb], first=False, last=j == len(parts) - 1)
            at("idx")
            ts(T.IDX[:, l0:l0 + 64], JB[:, 0:64], BIG, BIG, (A.add, A.subtract), [], [("IDX", c)], [jb])
            ga = cost["gx"].get(n, cost["ga"])
            gk = []
            at("gt")
            for eng, a, b in (("A", 0, ga), ("V", ga, 64)):
                if b > a:
                    gather(eng, T.GT[:, s0 + a * 16:s0 + b * 16], T.TAB[:].indirect(T.IDX[:, l0 + a:l0 + b]),
                           TK + [("IDX", c)], [("GT", p, eng)])
                    gk.append(("GT", p, eng))
            o1 = T.OIN[:, n * 64:n * 64 + 64]
            nf = 8 if last or cost["fa"] else 6
            at("f")
            mm([(F[:, i:nf * 64:8], T.GT[:, s0 + i:s0 + 1024:8], T.FS[:, 0:nf * 8]) for i in range(8)], FSK + gk, [fb])
            at("h")
            for f in range(2):
                tt(xv(X, f), F[:, f * 64:f * 64 + 64], o1, A.is_lt, [x0, ("OIN", n)], [("h", p, f)], [fb])
            hk = [("h", p, 0), ("h", p, 1)]
            at("th")
            dh = cost["dh"]
            if dh:
                tt(xv(X, 4), F[:, 192:256], xv(X, 0), A.add, [x0, hk[0]], [("th", p)], [fb])
            else:
                vec(lambda F=F, X=X: v.tensor_copy(xv(X, 4), F[:, 192:256]), [x0], [("th", p)], [fb])
            fa = cost["fa"] and not last
            at("rs")
            if fa:
                part = T.OP[:, n // 2, 0, p, :]
                tt(part, F[:, 384:448], o1, A.add, [("OIN", n)], [("OP", n, 0)], [fb])
                tt(part, F[:, 448:512], part, A.min, [("OP", n, 0)], [("OP", n, 0)], [fb])
            elif last:
                tt(xv(X, 2), F[:, 384:448], o1, A.add, [x0, ("OIN", n)], [("rs", p)], [fb])
                tt(xv(X, 2), F[:, 448:512], xv(X, 2), A.min, [x0, ("rs", p)], [("rs", p)], [fb])
            else:
                tt(xv(X, 2), F[:, 128:192], o1, A.min, [x0, ("OIN", n)], [("rs", p)], [fb])
            at("pp")
            if fa:
                tt(T.OP[:, n // 2, 1:3, p, :], xv(X, 0, 2), F[:, 256:384], A.mult, [x0] + hk, [("OP", n, 1)], [fb])
            else:
                tt(xv(X, 5, 2), xv(X, 0, 2), F[:, 256:384], A.mult, [x0] + hk, [("pp", p)], [fb])
            if not last:
                at("bb")
                if dh:
                    mm([(BB[:, 0:64], xt(X, 1, bit), T.IH[:, bit::2]) for bit in range(2)], ["IH", x0, hk[1]], [bb], last=False)
                    mm([(BB[:, 0:64], xt(X, 4, bit), T.IH[:, bit::2]) for bit in range(2)], ["IH", x0, ("th", p)], [bb], first=False)
                else:
                    mm([(BB[:, 0:64], xt(X, 4, bit), T.IH[:, bit::2]) for bit in range(2)], ["IH", x0, ("th", p)], [bb], last=False)
                    mm([(BB[:, 0:64], xt(X, f, bit), T.IH[:, bit::2]) for f in (0, 1) for bit in range(2)], ["IH", x0] + hk, [bb], first=False)
                at("out")
                ts(T.OUT[:, n * 64:n * 64 + 64], BB[:, 0:64], 2048.0, None, (A.add,), [], [("OUT", n)], [bb])
                i = post(T.MSG[:, n * 64:n * 64 + 64], [T.OUT[:, n * 64:n * 64 + 64]], "next", "m%d" % n, [("OUT", n)], [("MSG", n)])
            if fa:
                if c % 2:
                    at("oo")
                    omsg[0] = send(T.OIN[:, n * 64 + 192:n * 64 + 320], [T.OP[:, n // 2, f] for f in range(3)], "next", "o%d" % n,
                                   [("OP", k, f) for k in (n - 1, n) for f in range(2)], after=i, alu=1)
                    arrive(omsg[0], "o%d" % n, [("OIN", k + NCH) for k in (n - 1, n)], peers["next"][3])
            elif not last:
                at("os")
                mm([(OB[:, i:64:8], T.GT[:, s0 + i:s0 + 1024:8], T.FS[:, 48:56]) for i in range(8)], FSK + gk, [ob], last=False)
                at("ob")
                mm([(OB[:, 0:64], T.IH[:], xv(X, f)) for f in (5, 6)], ["IH", x0, ("pp", p)], [ob], first=False)
                at("oo")
                tt(T.OOUT[:, n * 64:n * 64 + 64], OB[:, 0:64], xv(X, 2), A.add, [x0, ("rs", p)], [("OOUT", n)], [ob])
                if c % 2:
                    a, b = (n - 1) * 64, (n + 1) * 64
                    omsg[0] = post(T.OIN[:, a + 256:b + 256], [T.OOUT[:, a:b]], "next", "o%d" % n, [("OOUT", k) for k in (n - 1, n)],
                                   [("OIN", k + NCH) for k in (n - 1, n)], after=i)
            else:
                packed = c < cost["pk"]
                O2, o2 = (BB, bb) if packed else (OB, ob)

                def back(out, fields, m):
                    return [(out[:, 0:128], xt(X, f, bit), m[:, bit * 128:bit * 128 + 128]) for f in fields for bit in range(2)]
                at("ym")
                mm([(BB[:, 0:128], T.PA[:], T.PB[:])], MVK, [bb], last=False)
                if not packed:
                    mm([(OB[:, 0:128], T.PA[:], T.PO[:])], MVK, [ob], last=False)
                at("bb")
                mm(back(BB, (1,) if dh else (0, 1), T.MW), MVK + [x0] + hk, [bb], first=False, last=False)
                mm(back(BB, (4,), T.MW), MVK + [x0, ("th", p)], [bb], first=False, last=not packed)
                at("ob")
                mm(back(O2, (2,), T.MV), MVK + [x0, ("rs", p)], [o2], first=False, last=False)
                mm(back(O2, (5, 6), T.MV), MVK + [x0, ("pp", p)], [o2], first=False)
                at("y")
                vec(lambda BB=BB, p=p: v.transpose(T.ZB[:, p], BB[:, 0:128]), [], [("ZB", p)], [bb])
                tt(T.YO[:, l0:l0 + 64], T.ZB[:, p, :, 0:16], T.ZB[:, p, :, 16:32], A.max, [("ZB", p)], [("YO", c)])
                if not packed:
                    y0 = 2 * l0
                    ts(T.YN[:, l0:l0 + 64], T.YO[:, l0:l0 + 64], 8, V - 1, (A.logical_shift_right, A.bitwise_and), [("YO", c)], [("YN", c, 0)])
                    vec(lambda l0=l0, y0=y0: v.tensor_copy(T.YS[:, y0:y0 + 64], T.YN[:, l0:l0 + 64]), [("YN", c, 0)], [("YS", c, 0)])
                    at("yo")
                    vec(lambda OB=OB, p=p: v.transpose(T.ZB[:, 2 + p], OB[:, 0:128]), [], [("ZO", p)], [ob])
                    tt(T.YS[:, y0 + 64:y0 + 128], T.ZB[:, 2 + p, :, 0:16], T.ZB[:, 2 + p, :, 16:32], A.max, [("ZO", p)], [("YS", c, 1)])
                    at("y")
                    post(T.YR[:, y0:y0 + 128], [T.YS[:, y0:y0 + 128]], "prev", "y%d" % c, [("YS", c, 0), ("YS", c, 1)], [("YR", c)])
                    dma(T.yb[:, l0:l0 + 64], T.YR[:, y0:y0 + 64], [("YR", c)], [], sem="outs")
                    dma(T.yo[:, l0:l0 + 64], T.YR[:, y0 + 64:y0 + 128], [("YR", c)], [], q="A" if c == NCH - 1 else "S", sem="outs")
                else:
                    post(T.YI[:, l0:l0 + 64], [T.YO[:, l0:l0 + 64]], "prev", "y%d" % c, [("YO", c)], [("YI", c)])
                if c >= NL:
                    at("tree")
                    tt(T.TR[:, s0:s0 + 512], wv(0, 8), wv(8, 16), A.max, wk, [("TR", p, 8)])
                    a = s0
                    for k in (4, 2, 1):
                        b = a + 128 * k
                        tt(T.TR[:, b:b + k * 64] if k > 1 else T.PK[:, l0:l0 + 64], T.TR[:, a:a + k * 64], T.TR[:, a + k * 64:a + k * 128], A.max,
                           [("TR", p, 2 * k)], [("TR", p, k) if k > 1 else ("PK", c)])
                        a = b
                if c == cost["pk"] - 1:
                    at("un")
                    a, b = 0, l0 + 64
                    yk = [("YI", j) for j in range(a // 64, b // 64)]
                    ts(T.YN[:, a:b], T.YI[:, a:b], 8, V - 1, (A.logical_shift_right, A.bitwise_and), yk, [("YN", c, 0)])
                    ts(T.YN[:, 256 + a:256 + b], T.YI[:, a:b], 255, None, (A.bitwise_and,), yk, [("YN", c, 1)])
                    vec(lambda a=a, b=b: v.tensor_copy(T.YF[:, a:b], T.YN[:, a:b]), [("YN", c, 0)], [("YF", c, 0)])
                    ts(T.YF[:, 256 + a:256 + b], T.YN[:, 256 + a:256 + b], -1.0, None, (A.add,), [("YN", c, 1)], [("YF", c, 1)])
                    dma(T.yb[:, a:b], T.YF[:, a:b], [("YF", c, 0)], [], sem="outs")
                    dma(T.yo[:, a:b], T.YF[:, 256 + a:256 + b], [("YF", c, 1)], [], sem="outs")
                if c == NL - 1:
                    at("fold")
                    i = send(T.HE[:, 2304:2304 + 64 * NL], [W[:, k * 64 * NL:(k + 1) * 64 * NL] for k in range(16)], LAST, "f%d" % NF,
                             [("W", j, k) for j in range(n - c, n + 1) for k in range(16)], after=omsg[0])
                    arrive(i, "e6", [("EIN", 9)], peers["back"][t])

        if not last:
            at("fold")
            side = SIDE[t]
            wall = [("W", t * NCH + c, k) for c in range(NCH) for k in range(16)]
            i = send(T.HE[:, t * 256:(t + 1) * 256], [W[:, k * 256:(k + 1) * 256] for k in range(side, 16)], "help", "f%d" % t, wall)
            arrive(i, "e%d" % t, [("EIN", t)], peers["back"][t])
            if side:
                at("side")
                i = send(T.HE[:, (4 + t) * 256:(5 + t) * 256], [W[:, k * 256:(k + 1) * 256] for k in range(side)], "pair", "g%d" % t, wall)
                arrive(i, "b%d" % t, [("EIN", 4 + t)], peers["back"][t])
        else:
            at("e")
            post(T.EIN[:, 2304 + 64 * NL:2560], [T.PK[:, 64 * NL:256]], "prev", "e5", [("PK", c) for c in range(NL, NCH)], [("EIN", 10)])
            at("em")
            tt(T.YE[:, 0:512], T.EIN[:, 0:512], T.EIN[:, 1280:1792], A.max, [("EIN", j) for j in (0, 1, 5, 6)], [("YE", 0)])
            tt(T.YE[:, 512:1024], T.EIN[:, 512:1024], T.EIN[:, 1792:2304], A.max, [("EIN", j) for j in (2, 3, 7, 8)], [("YE", 1)])
            tt(T.YE[:, 0:512], T.YE[:, 0:512], T.YE[:, 512:1024], A.max, [("YE", 0), ("YE", 1)], [("YE", 0)])
            tt(T.YE[:, 512:768], T.YE[:, 0:256], T.YE[:, 256:512], A.max, [("YE", 0)], [("YE", 1)])
            tt(T.YE[:, 768:1024], T.YE[:, 512:768], T.EIN[:, 1024:1280], A.max, [("YE", 1), ("YE", 0), ("EIN", 4)], [("YE", 2)])
            at("ef")
            for c in range(NCH):
                src = T.EIN[:, 2304 + c:2304 + 64 * NL:NL] if c < NL else T.EIN[:, 2304 + c * 64:2368 + c * 64]
                tt(T.YE[:, 256 + c * 64:320 + c * 64], T.YE[:, 768 + c:1024:NCH], src, A.max, [("YE", 2), ("EIN", 9 + (c >= NL))], [("YE", 3, c)])
            dma(T.ye[:], T.YE[:, 256:512], [("YE", 3, c) for c in range(NCH)], [], sem="outs")
    return ops


def link(ops):
    wr, rd, bank = {}, {}, {}
    for o in ops:
        d = {}
        for k in o["rd"]:
            if k in wr:
                d[wr[k]] = True
        for k in o["wr"]:
            if k in wr:
                d[wr[k]] = True
            for j in rd.get(k, []):
                d[j] = True
        for b in o["banks"]:
            eng, cur, prev = bank.get(b, (None, [], []))
            if eng != o["eng"]:
                eng, cur, prev = o["eng"], [], cur
            for j in prev:
                d[j] = True
            if eng == "P" and cur:
                d.setdefault(cur[-1], False)
            bank[b] = (eng, cur + [o["i"]], prev)
        if o["after"] is not None:
            d[o["after"]] = False
        for k in o["rd"]:
            rd.setdefault(k, []).append(o["i"])
        for k in o["wr"]:
            wr[k] = o["i"]
            rd[k] = []
        d.pop(o["i"], None)
        o["deps"] = [(j, w and not (o["eng"] == "P" and ops[j]["eng"] == "P")) for j, w in d.items()]


def lines(ops, order):
    left = {}
    for o in ops:
        left.setdefault((o["eng"], o["tag"], o["n"]), []).append(o["i"])
    out = {}
    for e, (first, turn, final) in order["queues"].items():
        words = [(w, 0) for w in first.split()]
        words += [(w, n) for n in range(*order["turns"]) for w in turn.split()] + [(w, 0) for w in final.split()]
        out[e] = []
        for w, n in words:
            w, _, k = w.partition(".")
            tag = w.rstrip("-0123456789")
            calls = left.get((e, tag, n + int(w[len(tag):] or 0)), [])
            k = int(k or len(calls))
            out[e] += calls[:k]
            del calls[:k]
    assert sum(len(x) for x in out.values()) == len([o for o in ops if o["eng"]]), [k for k, x in left.items() if x and k[0]]
    return out


def merge(ops, line):
    done, out, at = [False] * len(ops), [], {e: 0 for e in line}
    landing = {}
    for o in ops:
        if not o["eng"]:
            landing.setdefault(o["after"], []).append(o["i"])
    while len(out) < len(ops):
        n = len(out)
        for e in line:
            while at[e] < len(line[e]) and all(done[j] for j, w in ops[line[e][at[e]]]["deps"]):
                i = line[e][at[e]]
                at[e] += 1
                for k in [i] + landing.get(i, []):
                    done[k] = True
                    ops[k]["st"] = len(out)
                    out.append(k)
        if len(out) == n:
            raise ValueError([(e, ops[line[e][at[e]]]["tag"], ops[line[e][at[e]]]["n"]) for e in line if at[e] < len(line[e])])
    return out


def emit(g, T, ops, order):
    queue = {"A": g.scalar, "V": g.vector, "P": g.tensor, "G": g, "S": g.sync}
    know = {e: {} for e in queue}
    count = {}
    for i in order:
        o = ops[i]
        if not o["eng"]:
            o["mark"], o["know"] = (o["sem"], o["inc"]), {o["sem"]: o["inc"]}
            continue
        e = o["eng"]
        need = {}
        for j, w in o["deps"]:
            if w:
                sem, n = ops[j]["mark"]
                if need.get(sem, (0, 0))[0] < n:
                    need[sem] = (n, j)
        for sem, (n, j) in sorted(need.items(), key=lambda x: -ops[x[1][1]]["st"]):
            if know[e].get(sem, 0) < n:
                queue[e].wait_ge(T.sem[sem], n)
                for k, x in ops[j]["know"].items():
                    if know[e].get(k, 0) < x:
                        know[e][k] = x
        ins = o["fn"]()
        if o["kind"] == "send":
            count["sent"] = count.get("sent", 0) + o["inc"]
            continue
        if o["kind"] == "sig":
            o["mark"], o["know"] = (o["sem"], 1), {o["sem"]: 1}
            continue
        sem, inc = (o["sem"], 16) if o["kind"] == "dma" else ("c" + e, 1)
        for x in ins:
            x.then_inc(T.sem[sem], inc)
            count[sem] = count.get(sem, 0) + inc
        o["mark"] = (sem, count[sem])
        o["know"] = dict(know[e])
        o["know"][sem] = count[sem]
    for sem in ("cG", "cP", "cA", "cV", "sent", "outs"):
        g.wait_ge(T.sem[sem], count[sem])


def way(topo, src, dst, mask=None):
    assert topo.may_write(src, dst)
    rid, pid, _ = topo.addr(dst)
    mask = topo.mask(src, dst) if mask is None else mask
    return rid, pid, mask, len([e for e in topo.engines(src, dst) if mask >> e & 1])


def helper_of(T, topo, rank):
    core = T.cores[rank]
    return [c for c in topo.cores_of(core) if T.rank_of(c) is None and topo.die(c) == topo.die(core)
            and all(topo.may_write(c, other) for other in T.cores)][0]


def fold_mask(T, topo, rank):
    core = T.cores[rank]
    return topo.mask(core, helper_of(T, topo, rank)) & ~topo.mask(core, T.cores[(rank + 1) % len(T.cores)])


def peers_of(T, topo, rank):
    n, core = len(T.cores), T.cores[rank]
    before = T.cores[(rank - 1) % n]
    lanes = topo.engines(core, before)
    return dict(next=way(topo, core, T.cores[(rank + 1) % n]), prev=way(topo, core, T.cores[(rank - 1) % n]),
                help=way(topo, core, helper_of(T, topo, rank), fold_mask(T, topo, rank)),
                pair=way(topo, core, helper_of(T, topo, rank), topo.mask(core, T.cores[(rank + 1) % n])),
                wide=way(topo, core, helper_of(T, topo, rank)),
                half=[way(topo, core, before, sum(1 << e for e in part)) for part in (lanes[:len(lanes) // 2], lanes[len(lanes) // 2:])],
                back=[way(topo, helper_of(T, topo, (rank + t) % n), core)[3] for t in range(STEPS)])


def rank_program(g, core, T, topo):
    n = len(T.cores)
    rank = T.rank_of(core)
    if rank is None:
        for q in range(n):
            if helper_of(T, topo, q) == core:
                main = way(topo, T.cores[q], core, fold_mask(T, topo, q))[3]
                side, sent = way(topo, T.cores[q], T.cores[(q + 1) % n])[3], 0
                jobs = [(0, "f0", main, "e0", 0, 256)]
                for t in range(1, NF):
                    jobs += [(t, "g%d" % t, side, "b%d" % t, (4 + t) * 256, 256), (t, "f%d" % t, main, "e%d" % t, t * 256, 256)]
                for t, landed, count, sem, a, width in jobs + [(NF, "f%d" % NF, peers_of(T, topo, q)[LAST][3], "e6", 2304, 64 * NL)]:
                    rid, pid, mask, engines = way(topo, core, T.cores[(q - t) % n])
                    g.wait_ge(T.sem[landed], count)
                    g.remote_dma(T.EIN[:, a:a + width], T.HE[:, a:a + width], T.sem[sem], T.sem.sent, pid, rid, mask)
                    sent += engines
                g.wait_ge(T.sem.sent, sent)
        return
    ops = build(g, T, peers_of(T, topo, rank), COST)
    link(ops)
    emit(g, T, ops, merge(ops, lines(ops, ORDER)))
